import numpy as np, ml_dtypes
CORES = [16,18,20,22]
N = 4
BF = ml_dtypes.bfloat16
def gentries(a):
    return np.ascontiguousarray(a.reshape(8, 16, -1).transpose(0, 2, 1)).reshape(8, -1)
def gtable(e):
    e = np.asarray(e); return np.ascontiguousarray(e.reshape(8, -1, 16).transpose(0, 2, 1)).reshape(128, -1).astype(np.int32)
V, M, J, T, S, H = 4096, 80, 3, 3, 4, 12
L = J * M
def base(rng):
    c = np.arange(V)
    lv = rng.integers(0, 64, (N, 8, 1, V)); lv[:, 1::2] = (c * 127) // V
    x = lv + rng.integers(0, 128, (N, 8, 16, V))
    k = rng.integers(0, V, (N, 8, 16, V)); k[:, 1::2] = (c + rng.integers(-(V // 32), V // 8, (N, 4, 16, V))) & (V - 1)
    z = rng.integers(20, 200, (N, 8, 1, T, M)) + rng.integers(0, 56, (N, 8, 16, T, M))
    return x, k, z, rng.integers(0, V, (N, 8, T, J, M))
def pack(x, k, z, v):
    return {"x0": np.ascontiguousarray(x.reshape(N, 128, V)).astype(np.float32).astype(BF), "k0": np.ascontiguousarray(k.reshape(N, 128, V)).astype(np.int32),
            "z0": np.ascontiguousarray(z.reshape(N, 128, T * M)).astype(np.float32).astype(BF), "v0": np.stack([gtable(a.reshape(8, -1)) for a in v])}
def setup_inputs(rng):
    return pack(*base(rng))
def setup_inputs_spread(rng):
    x = (np.exp2(8 * rng.random((N, 8, 1, V))) * rng.random((N, 8, 16, V))).astype(np.int64)
    z = (np.exp2(8 * rng.random((N, 8, 1, T, M))) * rng.random((N, 8, 16, T, M))).astype(np.int64)
    return pack(x, (V * rng.random((N, 8, 16, V)) ** 2).astype(np.int64), z, (V * rng.random((N, 8, T, J, M)) ** 3).astype(np.int64))
def setup_inputs_ends(rng):
    def tips(hi, *shape):
        return hi * rng.integers(0, 2, shape)
    h = rng.random((N, 8, 1, V)); x = np.where(h < 0.25, 255, np.where(h < 0.5, 0, tips(255, N, 8, 16, V)))
    k = np.where(rng.random((N, 8, 16, V)) < 0.8, tips(V - 1, N, 8, 16, V), rng.integers(8, V - 1, (N, 8, 16, V)))
    h = rng.random((N, 8, 1, T, M)); z = np.where(h < 0.3, 0, np.where(h < 0.6, 255, 255 * (rng.random((N, 8, 16, T, M)) < 0.25)))
    v = np.where(rng.random((N, 8, T, J, M)) < 0.7, tips(V - 1, N, 8, T, J, M), rng.integers(8, V - 1, (N, 8, T, J, M)))
    even = ((np.arange(N)[:, None] + np.arange(8)[None, :] + N) & 1 == 0)[:, :, None]
    x[..., V - 1] = np.where(even, 255, x[..., V - 1]); x[..., 0] = np.where(even, x[..., 0], 255)
    i = np.arange(16); nl = H + 1 - (H & 1)
    z[:, :, :, 0, M - 1] = 0; z[:, :, :, 0, M - 2] = np.where(i < H, 254, 255); z[:, :, :, 0, M - 3] = np.where(i < nl, 254, 255)
    v[:, :, 0, :, M - 2:] = V - 1; k[:, :, 0, V - 1] = V - 1
    x[..., 565] = 255; k[:, :, 0, 2] = 565; k[:, :, 0, 3] = V - 1; v[:, :, 0, 0, M - 3] = 2; v[:, :, 0, 1, M - 3] = 3
    x[..., 7] = 255 - (np.argsort(rng.random((N, 8, 16)), axis=2) == 0).astype(np.int64)
    k[:, :, :15, 6] = 7; k[:, :, 15, 6] = np.where(even[:, :, 0], V - 1, 0); z[:, :, :, 0, M - 5] = 0; v[:, :, 0, :, M - 5] = 6
    z[:, :, :, 0, M - 4] = z[:, :, :, 0, M - 3]; x[..., 3673] = 255; x[..., 4093] = 255
    k[:, :, 0, 4] = 3673; k[:, :, 0, 5] = 4093; v[:, :, 0, 0, M - 4] = 4; v[:, :, 0, 1, M - 4] = 5
    return pack(x, k, z, v)
def setup_inputs_corners(rng):
    x, k, z, v = base(rng); o = rng.permutation(8); c = np.arange(V)
    x[:, o[0], 8:] = 0
    x[:, o[1]] = rng.integers(1, 101, (N, 16, V)); z[:, o[1]] = 0; h = int(rng.integers(0, N))
    x[np.array([h, (h - J) % N]), o[1]] = rng.integers(200, 256, (2, 16, V)); z[:, o[1], :, 1:] = rng.integers(100, 150, (N, 16, T - 1, M))
    k[:, o[2]] = c
    k[:, o[3]] = (c + 1) & (V - 1); x[:, o[3]] = np.where(c % (S + 1) == 0, rng.integers(200, 256, (N, 16, V)), 0); z[:, o[3]] = rng.integers(100, 151, (N, 16, T, M))
    d = rng.integers(1, S + 2, (N, T, J, M))
    d[:, 0, :, 0] = S + 1; d[:, 0, :, 1] = S; d[:, 0, 0, 2] = S; d[:, 0, 1:, 2] = S + 1; d[:, 0, :-1, 3] = S; d[:, 0, -1, 3] = 1
    v[:, o[3]] = (rng.integers(0, V // (S + 1) - 1, (N, T, J, M)) + 1) * (S + 1) - d; v[:, o[3], 0, 0, 4] = V - 1
    x[:, o[4]] = 255 * (np.argsort(rng.random((N, 16, V)), axis=1) < H - 1 + (c & 3)); k[:, o[4]] = (rng.integers(0, V, (N, 16, V)) & (V - 4)) | (c & 3); z[:, o[4]] = 100
    k[:, o[5]] = (V - 1) * rng.integers(0, 2, (N, 16, V)); v[:, o[5]] = (V - 1) * rng.integers(0, 2, (N, T, J, M))
    h = rng.integers(0, 5, (N, 16, V))
    k[:, o[6]] = np.where(h == 0, 0, np.where(h == 1, V - 1, np.where(h == 2, c, np.where(h == 3, (c + 1) & (V - 1), (c - 1) & (V - 1)))))
    v[:, o[6]] = rng.choice(np.array([0, 1, V - 2, V - 1]), (N, T, J, M))
    v[:, o[7]] = rng.integers(0, V, (T, 1, 1))
    return pack(x, k, z, v)
def setup_inputs_ties(rng):
    x, k, z, v = base(rng)
    x = rng.integers(100, 103, x.shape); z = rng.integers(100, 102, z.shape); z[..., ::8] = 102
    for q in range(N):
        for g in range(0, 8, 2):
            few = rng.permutation(V)[:64]; few[0] = V - 1; k[q, g] = few[rng.integers(0, 64, (16, V))]
    k[:, ::3, 8:] = k[:, ::3, :8]
    k[:, 7, 14:, 1::2] = V - 1; x[:, 7, :, V - 1] = 103
    return pack(x, k, z, v)
def setup_inputs_meets(rng):
    x, k, z, v = base(rng)
    for q in range(N):
        for g in range(8):
            n = 8 + 16 * g; few = rng.permutation(V)[:n]; few[0] = 0; few[1] = V - 1
            k[q, g][:, few] = few[rng.integers(0, n, (16, n))]
            for j in range(1, J + 1): v[(q - j) % N, g, :, j - 1] = few[rng.integers(0, n, (T, M))]
    return pack(x, k, z, v)
def check_inputs(d):
    bad = []
    for k, lo, hi in (("x0", 0, 255), ("k0", 0, V - 1), ("z0", 0, 255), ("v0", 0, V - 1)):
        a = np.asarray(d[k]).astype(np.float64)
        if not (np.min(a) >= lo and np.max(a) <= hi): bad.append("range of " + k)
        elif np.any(a != np.floor(a)): bad.append("whole numbers of " + k)
    return bad
def to_hosts(a):
    return np.stack([np.concatenate([a[(q - j) % N, :, j - 1] for j in range(1, J + 1)], axis=1) for q in range(N)])
def to_owners(a):
    return np.stack([np.stack([a[(r + j) % N, :, (j - 1) * M:j * M] for j in range(1, J + 1)], axis=1) for r in range(N)])
def lowest(n, on):
    a = np.flatnonzero(on)
    return a[np.unique(n[a], return_index=True)[1]]
def reference(x0, k0, z0, v0):
    X = x0.astype(np.float32).astype(np.int64).reshape(N, 8, 16, V); K = k0.astype(np.int64).reshape(N, 8, 16, V)
    Z = z0.astype(np.float32).astype(np.int64).reshape(N, 8, 16, T, M); start = np.stack([gentries(a) for a in v0]).astype(np.int64).reshape(N, 8, T, J, M)
    odd = np.zeros(N, np.int64)
    for t in range(T):
        v = to_hosts(start[:, :, t])
        z = np.stack([np.concatenate([Z[(q - j) % N, :, :, t] for j in range(1, J + 1)], axis=2) for q in range(N)])
        b = np.full((N, 8, L), S + 1, np.int64); zb = np.zeros((N, 8, 16, L), np.int64); wb = np.zeros((N, 8, L), np.int64)
        logv, logk = [], []
        for s in range(1, S + 1):
            kv = np.take_along_axis(K, v[:, :, None, :], 3)
            ix = kv.transpose(0, 1, 3, 2).reshape(N, 8, L * 16)
            xk = np.take_along_axis(X, ix[:, :, None, :], 3).reshape(N, 8, 16, L, 16)
            score = np.add.reduce(np.maximum(xk - z[..., None], 0), axis=2)
            k = np.argmax(score, axis=-1)
            w = np.take_along_axis(kv, k[:, :, None, :], 2)[:, :, 0]
            xw = np.take_along_axis(X, w[:, :, None, :], 3)
            bid = np.add.reduce((xw > z).astype(np.int64), axis=2) >= H + odd[:, None, None]
            z = (z + xw) >> 1
            now = bid & (b > S)
            b = np.where(now, s, b); wb = np.where(now, w, wb); zb = np.where(now[:, :, None, :], z, zb)
            logv.append(v); logk.append(k); v = w
        u = (wb * np.add.reduce(zb, axis=2)) & (V - 1)
        bo = to_owners(b); win = np.argmin(bo, axis=2); first = np.min(bo, axis=2)
        uo = np.take_along_axis(to_owners(u), win[:, :, None, :], 2)
        every = np.zeros((N, 8, J, M), np.int64)
        end = to_hosts(every + first[:, :, None, :]); uw = to_hosts(every + uo)
        won = to_hosts(win[:, :, None, :] == np.arange(J)[None, None, :, None]) & (end <= S); lost = ~won & (end <= S)
        for q in range(N):
            for g in range(8):
                a = lowest(wb[q, g], won[q, g]); n = wb[q, g, a]
                X[q, g][:, n] = (X[q, g][:, n] + zb[q, g][:, a]) >> 1
                for s in range(S, 0, -1):
                    a = lowest(logv[s - 1][q, g], lost[q, g] & (end[q, g] >= s))
                    n = logv[s - 1][q, g, a]; i = logk[s - 1][q, g, a]; c = K[q, g, i, n]
                    K[q, g, i, n] = (((uw[q, g, a] * c) >> 5) + c + s) & (V - 1)
        odd = np.add.reduce(won.reshape(N, -1).astype(np.int64), axis=1) & 1
    f8 = np.arange(1, 9)[None, None, :, None]
    return {"yx": np.add.reduce(X.reshape(N, 128, 8, V // 8) * f8, axis=2).astype(np.float32), "yk": np.add.reduce(K.reshape(N, 128, 8, V // 8) * f8, axis=2).astype(np.float32)}

@@ -1,0 +1,596 @@
+from concourse.bass import DstId, RemoteDMATransfer
+from concourse.mybir import AluOpType, AxisListType, ActivationFunctionType
+
+A = AluOpType
+ID = ActivationFunctionType.Identity
+RELU = ActivationFunctionType.Relu
+N, M, J, RACES, S, V = 4, 80, 3, 3, 4, 4096
+L = J * M
+NA = 8
+ND = 15 - NA
+WIN = V + 256
+BIG = 2.0 ** 19
+
+SCRATCH = {
+    "xw": ("sbuf", [128, WIN], "bfloat16"), "kw": ("sbuf", [128, WIN], "float32"), "kin": ("sbuf", [128, V], "int32"),
+    "iw": ("sbuf", [128, 8192], "float32"),
+    "Y": ("sbuf", [128, 15, 256], "bfloat16"), "zx": ("sbuf", [128, ND * 256], "bfloat16"),
+    "kvu": ("sbuf", [128, 256], "uint16"), "kvf0": ("sbuf", [128, 128], "float32"), "kvf1": ("sbuf", [128, 128], "float32"),
+    "Tt0": ("sbuf", [128, 4, 32], "float32"), "Tt1": ("sbuf", [128, 4, 32], "float32"),
+    "xg0": ("sbuf", [128, 512], "bfloat16"), "xg1": ("sbuf", [128, 512], "bfloat16"),
+    "zT": ("sbuf", [128, 128], "bfloat16"), "E": ("sbuf", [128, 2048], "bfloat16"),
+    "zg": ("sbuf", [128, 2400], "bfloat16"), "sh0": ("sbuf", [128, 128], "float16"), "sh1": ("sbuf", [128, 128], "float16"),
+    "R0": ("sbuf", [128, 128], "float32"), "R1": ("sbuf", [128, 128], "float32"),
+    "eq0": ("sbuf", [128, 128], "float32"), "eq1": ("sbuf", [128, 128], "float32"),
+    "pr0": ("sbuf", [128, 128], "float32"), "pr1": ("sbuf", [128, 128], "float32"),
+    "C0": ("sbuf", [128, 128], "float32"), "C1": ("sbuf", [128, 128], "float32"),
+    "codeI": ("sbuf", [128, 64], "int32"), "vI0": ("sbuf", [128, 80], "int32"), "vI1": ("sbuf", [128, 80], "int32"),
+    "vU0": ("sbuf", [128, 80], "uint16"), "vU1": ("sbuf", [128, 80], "uint16"),
+    "kI": ("sbuf", [128, 64], "int32"), "kU": ("sbuf", [128, 64], "uint16"),
+    "zsT": ("sbuf", [128, 64], "float32"), "cntT": ("sbuf", [128, 64], "float32"),
+    "wz": ("sbuf", [128, 64], "int32"), "u4": ("sbuf", [128, 64], "int32"), "nb": ("sbuf", [128, 64], "float32"),
+    "c1": ("sbuf", [128, 64], "float32"), "m1": ("sbuf", [128, 32], "float32"), "own": ("sbuf", [128, 48], "float32"),
+    "d1": ("sbuf", [128, 64], "float32"), "m2": ("sbuf", [128, 32], "float32"), "dI": ("sbuf", [128, 16], "int32"),
+    "WI": ("sbuf", [128, 16], "int32"), "WU": ("sbuf", [128, 16], "uint16"), "bF": ("sbuf", [128, 16], "float32"),
+    "bI": ("sbuf", [128, 16], "int32"), "bU": ("sbuf", [128, 16], "uint16"),
+    "rcv": ("sbuf", [128, 144], "float32"), "Wm": ("sbuf", [128, 16], "float32"),
+    "x1": ("sbuf", [128, 16], "float32"), "x2": ("sbuf", [128, 16], "float32"), "lost": ("sbuf", [128, 16], "float32"),
+    "won": ("sbuf", [128, 16], "float32"), "wonb": ("sbuf", [128, 16], "bfloat16"), "WmI": ("sbuf", [128, 16], "int32"),
+    "bw": ("sbuf", [128, 16], "int32"), "uwI": ("sbuf", [128, 16], "int32"), "uwU": ("sbuf", [128, 16], "uint16"),
+    "lc": ("sbuf", [128, 16], "float32"), "on": ("sbuf", [128, 64], "float32"), "P1": ("sbuf", [128, 64], "float32"),
+    "Wp": ("sbuf", [128, 16], "float32"), "kk": ("sbuf", [128, 64], "float32"), "kt1": ("sbuf", [128, 16], "float32"),
+    "key": ("sbuf", [128, 64], "float32"), "keyU": ("sbuf", [128, 16], "uint16"),
+    "vall": ("sbuf", [128, 960], "uint16"), "eqm": ("sbuf", [128, 7680], "bfloat16"),
+    "fl": ("sbuf", [128, 240], "bfloat16"), "Fs": ("sbuf", [128, 960], "bfloat16"), "fo": ("sbuf", [128, 80], "float32"),
+    "vD": ("sbuf", [128, 80], "float32"), "of": ("sbuf", [128, 80], "float32"), "offU": ("sbuf", [128, 80], "uint16"),
+    "urep": ("sbuf", [128, 240], "float32"), "xs": ("sbuf", [128, 960], "float32"), "Bs": ("sbuf", [128, 960], "float32"),
+    "kp": ("sbuf", [128, 240], "float32"), "kt": ("sbuf", [128, 240], "float32"), "kz": ("sbuf", [128, 240], "int32"),
+    "kn": ("sbuf", [128, 240], "int32"),
+    "xW": ("sbuf", [128, 240], "bfloat16"), "xs2": ("sbuf", [128, 240], "float16"), "xt2": ("sbuf", [128, 240], "float16"),
+    "xn": ("sbuf", [128, 240], "bfloat16"), "tot": ("sbuf", [128, 1], "float32"), "totI": ("sbuf", [128, 1], "int32"),
+    "thr": ("sbuf", [128, 1], "float32"),
+    "zs": ("sbuf", [128, 240], "bfloat16"), "vs": ("sbuf", [128, 45], "int32"), "zl": ("sbuf", [128, 720], "bfloat16"),
+    "vl": ("sbuf", [128, 135], "int32"),
+    "pI": ("sbuf", [128, 8], "int32"), "pF": ("sbuf", [128, 24], "float32"),
+    "idb": ("sbuf", [128, 128], "bfloat16"), "Pm": ("sbuf", [128, 512], "float32"), "U": ("sbuf", [128, 144], "bfloat16"),
+    "bo1": ("sbuf", [128, 128], "bfloat16"), "bo2": ("sbuf", [128, 128], "bfloat16"), "BO": ("sbuf", [128, 128], "bfloat16"),
+    "BW": ("sbuf", [128, 128], "bfloat16"), "Wt": ("sbuf", [128, 1920], "bfloat16"), "W2d": ("sbuf", [128, 240], "float32"),
+    "dg": ("sbuf", [128, 16], "float32"), "Wk": ("sbuf", [128, 16], "bfloat16"), "rm": ("sbuf", [128, 256], "float32"),
+    "rmb": ("sbuf", [128, 256], "bfloat16"), "kc": ("sbuf", [128, 128], "bfloat16"), "base": ("sbuf", [128, 64], "float32"),
+    "bs": ("sbuf", [128, 64], "float32"), "Dm": ("sbuf", [128, 64], "float32"), "ln": ("sbuf", [128, 16], "float32"),
+    "idx": ("sbuf", [128, 1024], "bfloat16"), "idk": ("sbuf", [128, 512], "float32"),
+    "ox": ("sbuf", [128, 512], "float32"), "ok": ("sbuf", [128, 512], "float32"),
+    "pe0": ("psum", [128, 512], "float32"), "pe1": ("psum", [128, 512], "float32"),
+    "pk0": ("psum", [128, 16, 32], "float32"), "pk1": ("psum", [128, 16, 32], "float32"),
+    "pa0": ("psum", [128, 2, 256], "float32"), "pa1": ("psum", [128, 2, 256], "float32"),
+    "pz": ("psum", [128, 512], "float32"), "pc": ("psum", [128, 512], "float32"),
+}
+SEMAPHORES = ["qV", "qS", "qT", "qG", "zin", "vin", "k0", "k1", "k2", "k3", "x0", "x1", "az", "av", "a0", "a1", "a2",
+              "lz", "lv", "l0", "l1", "l2", "oy", "ok"]
+
+
+def tracker(g, T):
+    queues = {"V": g.vector, "S": g.scalar, "T": g.tensor, "G": g, "Y": g.sync}
+    cnt = {"V": 0, "S": 0, "T": 0, "G": 0}
+    clk = {q: {} for q in queues}
+    snap = {}
+    recs = {}
+
+    def is_psum(b):
+        return SCRATCH[b][0] == "psum" if b in SCRATCH else False
+
+    def waits(q, R, W, waw=True):
+        need = {}
+
+        def add(r):
+            if need.get(r[4], 0) < r[5]:
+                need[r[4]] = r[5]
+        for b, lo, hi in R:
+            ps = is_psum(b)
+            for r in recs.get(b, []):
+                if ps:
+                    if r[3] != q or (r[2] and r[0] < hi and lo < r[1]):
+                        add(r)
+                elif r[2] and r[0] < hi and lo < r[1]:
+                    add(r)
+        for b, lo, hi in W:
+            ps = is_psum(b)
+            for r in recs.get(b, []):
+                if not (ps or (r[0] < hi and lo < r[1])):
+                    continue
+                if r[3] != q or (q in "VSG" and (waw or not r[2])):
+                    add(r)
+        c = clk[q]
+        items = [(s, v) for s, v in need.items() if c.get(s, 0) < v]
+        keep = []
+        for s, v in items:
+            if not any(o != (s, v) and snap.get(o, {}).get(s, 0) >= v for o in items):
+                keep.append((s, v))
+        for s, v in (keep if keep else items):
+            queues[q].wait_ge(T.sem[s], v)
+        for s, v in items:
+            c[s] = max(c.get(s, 0), v)
+            for k2, v2 in snap.get((s, v), {}).items():
+                if c.get(k2, 0) < v2:
+                    c[k2] = v2
+
+    def note(q, R, W, sem, val):
+        snap[(sem, val)] = dict(clk[q]) if q in clk else {}
+        for b, lo, hi in W:
+            old = recs.setdefault(b, [])
+            recs[b] = [r for r in old if not (lo <= r[0] and r[1] <= hi)] + [(lo, hi, True, q, sem, val)]
+        for b, lo, hi in R:
+            old = recs.setdefault(b, [])
+            recs[b] = [r for r in old if not (not r[2] and r[3] == q and lo <= r[0] and r[1] <= hi)] + [(lo, hi, False, q, sem, val)]
+
+    def op(q, fn, R, W, waw=True):
+        waits(q, R, W, waw)
+        cnt[q] += 1
+        sem = "q" + q
+        fn(queues[q]).then_inc(T.sem[sem], 1)
+        note(q, R, W, sem, cnt[q])
+
+    def dma(q, sem, out, in_, R, W, val=16):
+        waits(q, R, W)
+        queues[q].dma_start(out, in_).then_inc(T.sem[sem], 16)
+        snap_q = dict(clk[q])
+        note("dma" + sem, R, W, sem, val)
+        snap[(sem, val)] = snap_q
+
+    def ready(q, R, W):
+        waits(q, R, W)
+
+    def arrival(sem, val, R, W):
+        note("net" + sem, R, W, sem, val)
+    return op, dma, ready, arrival, cnt, queues
+
+
+def rank_program(g, core, T, topo):
+    rank = T.rank_of(core)
+    if rank is None:
+        return
+    op, dma, ready, arrival, cnt, queues = tracker(g, T)
+    peers = [T.cores[(rank + j) % N] for j in (1, 2, 3)]
+
+    def iota(name, lo, hi, pattern, base, cm):
+        flag = SCRATCH[name][2] != "int32"
+        if flag:
+            op("G", lambda e: e.iota(T[name][:, lo:hi], pattern, base, cm, allow_small_or_imprecise_dtypes=True), [], [(name, lo, hi)])
+        else:
+            op("G", lambda e: e.iota(T[name][:, lo:hi], pattern, base, cm), [], [(name, lo, hi)])
+
+    def ts(out, W, in0, R, s1, s2, o0, o1=None):
+        if o1 is None:
+            op("V", lambda e: e.tensor_scalar(out, in0, s1, None, o0), R, W)
+        else:
+            op("V", lambda e: e.tensor_scalar(out, in0, s1, s2, o0, o1), R, W)
+
+    def tt(out, W, in0, in1, R, o):
+        op("V", lambda e: e.tensor_tensor(out, in0, in1, o), R, W)
+
+    def cp(out, W, in_, R):
+        op("V", lambda e: e.tensor_copy(out, in_), R, W)
+
+    def act(out, W, in_, R, f=ID, bias=0.0, scale=1.0):
+        op("S", lambda e: e.activation(out, in_, f, bias=bias, scale=scale), R, W)
+
+    def mm(out, W, lhsT, rhs, R, start, stop):
+        op("T", lambda e: e.matmul(out, lhsT, rhs, start, stop), R, W)
+
+    def ms(name, lo, hi, val):
+        op("V", lambda e: e.memset(T[name][:, lo:hi], val), [], [(name, lo, hi)])
+
+    dma("Y", "zin", T.zs[:], T.z0[:], [], [("zs", 0, 240)])
+    dma("S", "vin", T.vs[:], T.v0[:], [], [("vs", 0, 45)])
+    for i in range(4):
+        dma("YS"[i % 2], "k%d" % i, T.kin[:, 1024 * i:1024 * i + 1024], T.k0[:, 1024 * i:1024 * i + 1024], [], [("kin", 1024 * i, 1024 * i + 1024)])
+    for i in range(2):
+        dma("YS"[i], "x%d" % i, T.xw[:, 2048 * i:2048 * i + 2048], T.x0[:, 2048 * i:2048 * i + 2048], [], [("xw", 2048 * i, 2048 * i + 2048)])
+
+    def send(name, src, dsts, R, rsem, lsem):
+        ready("G", R, [])
+        ids = []
+        m = 0xFFFF
+        for p in peers:
+            a = topo.addr(p)
+            ids.append(DstId(rid=a[0], pnc=a[1]))
+            m &= topo.mask(core, p)
+        g.remote_dma_fused([RemoteDMATransfer(dst_ids=ids, dma_engine_mask=m, remote_sem=T.sem[rsem], srcs=[src], dsts=dsts, alu_op=0)], local_sem=T.sem[lsem])
+        ne = sum(m >> e & 1 for e in range(16))
+        arrival(lsem, ne, R, [])
+        return ne
+
+    iota("pI", 0, 1, [[0, 1]], 0, 1)
+    iota("iw", 0, 256, [[1, 256]], 0, 0)
+    ne = send("z", T.zs[:], [T.zl[:, 240 * j:240 * j + 240] for j in range(3)], [("zs", 0, 240)], "az", "lz")
+    arrival("az", 3 * ne, [], [("zl", 0, 720)])
+    send("v", T.vs[:], [T.vl[:, 45 * j:45 * j + 45] for j in range(3)], [("vs", 0, 45)], "av", "lv")
+    arrival("av", 3 * ne, [], [("vl", 0, 135)])
+    iota("kc", 0, 128, [[0, 8], [-1, 16]], 15, 0)
+    iota("rm", 0, 256, [[0, 16], [1, 16]], 0, 0)
+    iota("E", 0, 2048, [[1, 128], [0, 16]], 0, 0)
+
+    def col(i):
+        return T.pF[:, i:i + 1]
+
+    def cR(i):
+        return ("pF", i, i + 1)
+    ts(T.pI[:, 1:2], [("pI", 1, 2)], T.pI[:, 0:1], [("pI", 0, 1)], 15, None, A.bitwise_and)
+    ts(T.pI[:, 2:3], [("pI", 2, 3)], T.pI[:, 0:1], [("pI", 0, 1)], 112, None, A.bitwise_and)
+    ts(T.pI[:, 3:4], [("pI", 3, 4)], T.pI[:, 0:1], [("pI", 0, 1)], 4, 1, A.arith_shift_right, A.bitwise_and)
+    cp(T.pF[:, 0:4], [("pF", 0, 4)], T.pI[:, 0:4], [("pI", 0, 4)])
+    ts(col(4), [cR(4)], col(3), [cR(3)], -1.0, 1.0, A.mult, A.add)
+    ts(col(5), [cR(5)], col(0), [cR(0)], 16.0, None, A.add)
+    ts(col(6), [cR(6)], col(0), [cR(0)], -16.0, None, A.add)
+    ts(col(7), [cR(7)], col(2), [cR(2)], 15.0, None, A.add)
+    ts(col(8), [cR(8)], col(1), [cR(1)], 4096.0, None, A.mult)
+    ts(T.idb[:], [("idb", 0, 128)], T.iw[:, 0:128], [("iw", 0, 128), cR(0)], col(0), None, A.is_equal)
+    for h in range(2):
+        for q in range(2):
+            sc = {0: 0, 1: 5, -1: 6}[q - h]
+            hc = 3 if h else 4
+            o = 128 * (2 * h + q)
+            ts(T.Pm[:, o:o + 128], [("Pm", o, o + 128)], T.iw[:, 0:128], [("iw", 0, 128), cR(sc), cR(hc)], col(sc), col(hc), A.is_equal, A.mult)
+    ts(T.U[:], [("U", 0, 144)], T.iw[:, 0:144], [("iw", 0, 144), cR(7)], col(7), 16.0, A.is_equal, A.mult)
+    ts(T.rm[:], [("rm", 0, 256)], T.rm[:], [("rm", 0, 256)], 1.0, None, A.min)
+    ts(T.E[:], [("E", 0, 2048)], T.E[:], [("E", 0, 2048), cR(0)], col(0), None, A.is_equal)
+    ms("codeI", 0, 64, 0)
+    ms("vI0", 0, 80, 0)
+    ms("vI1", 0, 80, 0)
+    ms("vU0", 0, 80, 0)
+    ms("vU1", 0, 80, 0)
+    ms("zsT", 0, 64, 0.0)
+    ms("cntT", 0, 64, 0.0)
+    ms("kvf0", 0, 128, 0.0)
+    ms("kvf1", 0, 128, 0.0)
+    ms("own", 0, 48, 0.0)
+    op("V", lambda e: e.memset(T.thr[:], 12.0), [], [("thr", 0, 1)])
+
+    def late_constants():
+        iota("bs", 0, 64, [[4096, 4], [0, 16]], 4096, 0)
+        iota("Dm", 0, 64, [[0, 4], [16, 16]], 4096, 0)
+        ms("base", 0, 64, 2.0 ** 20)
+        for s in range(S):
+            iota("base", 16 * s, 16 * s + 15, [[4096, 3], [0, 5]], 16384 * (s + 1) + 4096, 0)
+        iota("iw", 256, 8192, [[1, 7936]], 256, 0)
+        cp(T.rmb[:], [("rmb", 0, 256)], T.rm[:], [("rm", 0, 256)])
+        ts(T.bo1[:], [("bo1", 0, 128)], T.iw[:, 0:128], [("iw", 0, 128), cR(2)], col(2), None, A.is_ge)
+        ts(T.bo2[:], [("bo2", 0, 128)], T.iw[:, 0:128], [("iw", 0, 128), cR(7)], col(7), None, A.is_le)
+        tt(T.BO[:], [("BO", 0, 128)], T.bo1[:], T.bo2[:], [("bo1", 0, 128), ("bo2", 0, 128)], A.mult)
+        for i in range(4):
+            ts(T.pI[:, 4 + i:5 + i], [("pI", 4 + i, 5 + i)], T.pI[:, 1:2], [("pI", 1, 2)], i, 1, A.arith_shift_right, A.bitwise_and)
+        for i in range(4):
+            ts(col(9 + i), [cR(9 + i)], T.pI[:, 4 + i:5 + i], [("pI", 4 + i, 5 + i)], 2.0 ** -(2 ** i) - 1.0, 1.0, A.mult, A.add)
+        tt(col(13), [cR(13)], col(9), col(10), [cR(9), cR(10)], A.mult)
+        tt(col(14), [cR(14)], col(11), col(12), [cR(11), cR(12)], A.mult)
+        tt(col(15), [cR(15)], col(13), col(14), [cR(13), cR(14)], A.mult)
+        ts(T.BW[:], [("BW", 0, 128)], T.BO[:], [("BO", 0, 128), cR(15)], col(15), 2.0 ** 60, A.mult, A.mult)
+        ts(T.dg[:], [("dg", 0, 16)], T.iw[:, 0:16], [("iw", 0, 16), cR(1), cR(15)], col(1), col(15), A.is_equal, A.mult)
+        for a in range(15):
+            e = (60 - 16 * a) // 2
+            ts(T.Wt[:, 128 * a:128 * a + 128], [("Wt", 128 * a, 128 * a + 128)], T.BW[:], [("BW", 0, 128)], 2.0 ** e, 2.0 ** e, A.mult, A.mult)
+            e = (120 - 16 * a) // 2
+            ts(T.W2d[:, 16 * a:16 * a + 16], [("W2d", 16 * a, 16 * a + 16)], T.dg[:], [("dg", 0, 16)], 2.0 ** e, 2.5 * 2.0 ** e, A.mult, A.mult)
+        ts(T.Wk[:], [("Wk", 0, 16)], T.iw[:, 0:16], [("iw", 0, 16), cR(1)], col(1), 1.0 / 32.0, A.is_equal, A.mult)
+        ts(T.Dm[:], [("Dm", 0, 64)], T.Dm[:], [("Dm", 0, 64), cR(1)], col(1), None, A.add)
+        ts(T.ln[:], [("ln", 0, 16)], T.Dm[:, 0:16], [("Dm", 0, 16)], -4096.0, None, A.add)
+
+    def z_start(t):
+        for j in range(3):
+            cp(T.zg[:, 80 * j:80 * j + 80], [("zg", 80 * j, 80 * j + 80)], T.zl[:, 240 * j + 80 * t:240 * j + 80 * t + 80], [("zl", 0, 720)])
+
+    def v_start(t):
+        vI, vU = "vI%d" % (t % 2), "vU%d" % (t % 2)
+        for j in range(3):
+            o = 45 * j + 15 * t + 5 * j
+            cp(T[vI][:, 5 * j:5 * j + 5], [(vI, 5 * j, 5 * j + 5)], T.vl[:, o:o + 5], [("vl", 0, 135)])
+        cp(T[vU][:, 0:15], [(vU, 0, 15)], T[vI][:, 0:15], [(vI, 0, 15)])
+
+    ms("zg", 0, 2400, 0.0)
+    ms("fo", 0, 80, 0.0)
+    op("V", lambda e: e.memset(T.ones[:], 1.0), [], [("ones", 0, 128)])
+    late_constants()
+    v_start(0)
+    z_start(0)
+    for i in range(4):
+        lo, hi = 1024 * i, 1024 * i + 1024
+        ts(T.kw[:, lo:hi], [("kw", lo, hi)], T.kin[:, lo:hi], [("kin", lo, hi)], 32.0, None, A.mult)
+
+    KW = ("kw", 0, V)
+    XW = ("xw", 0, V)
+    a0s, a1s = (0, NA), (NA, 15)
+
+    def knew(t, gr, s):
+        vU = "vU%d" % (t % 2)
+        a0, a1 = a0s[gr], a1s[gr]
+        lo, hi, o = 16 * a0, 16 * a1, 16 * (s - 1)
+        ts(T.kvu[:, lo:hi], [("kvu", lo, hi)], T.kw[:, 0:V].indirect(T[vU][:, o + a0:o + a1]), [KW, (vU, o + a0, o + a1)], 1.0 / 32.0, None, A.mult)
+
+    def kact(t, gr, s):
+        vU = "vU%d" % (t % 2)
+        a0, a1 = a0s[gr], a1s[gr]
+        n, o, kvf = 16 * (a1 - a0), 16 * (s - 1), "kvf%d" % gr
+        act(T[kvf][:, 0:n], [(kvf, 0, n)], T.kw[:, 0:V].indirect(T[vU][:, o + a0:o + a1]), [KW, (vU, o + a0, o + a1), cR(8)], ID, bias=col(8), scale=1.0 / 32.0)
+
+    def ktr(gr):
+        kvf, Tt = "kvf%d" % gr, "Tt%d" % gr
+        op("V", lambda e: e.transpose(T[Tt][:, :, :], T[kvf][:]), [(kvf, 0, 128)], [(Tt, 0, 128)])
+
+    def kswap(gr):
+        Tt, pk = "Tt%d" % gr, "pk%d" % gr
+        for h in range(2):
+            for q in range(2):
+                o = 128 * (2 * h + q)
+                mm(T[pk][:, 0:4, 16 * h:16 * h + 16], [(pk, 0, 512)], T.Pm[:, o:o + 128], T[Tt][:, :, 16 * q:16 * q + 16], [("Pm", o, o + 128), (Tt, 0, 128)], q == 0, q == 1)
+
+    def score(gr, al, ah, first, last):
+        pe, a0 = "pe%d" % gr, a0s[gr]
+        if first:
+            mm(T[pe][:, 0:128], [(pe, 0, 512)], T.idb[:], T.kc[:], [("idb", 0, 128), ("kc", 0, 128)], True, False)
+        for c in range(16):
+            mm(T[pe][:, 16 * (al - a0):16 * (ah - a0)], [(pe, 0, 512)], T.U[:, 15 - c:143 - c], T.Y[:, al:ah, 16 * c:16 * c + 16],
+               [("U", 0, 144), ("Y", 256 * al, 256 * ah)], False, last and c == 15)
+
+    def xgat(i):
+        xg = "xg%d" % (i % 2)
+        act(T[xg][:], [(xg, 0, 512)], T.xw[:, 0:V].indirect(T.kvu[:, 32 * i:32 * i + 32]), [XW, ("kvu", 32 * i, 32 * i + 32)])
+
+    def xsub(i):
+        xg, pa = "xg%d" % (i % 2), "pa%d" % (i % 2)
+        mm(T[pa][:, :, :], [(pa, 0, 512)], T.idb[:], T[xg][:], [("idb", 0, 128), (xg, 0, 512)], True, False)
+        mm(T[pa][:, :, :], [(pa, 0, 512)], T.zT[:], T.E[:, 512 * i:512 * i + 512], [("zT", 0, 128), ("E", 0, 2048)], False, True)
+
+    def xrelu(i):
+        pa = "pa%d" % (i % 2)
+        act(T.Y[:, 2 * i:2 * i + 2, :], [("Y", 512 * i, 512 * i + 512)], T[pa][:, :, :], [(pa, 0, 512)], RELU)
+
+    def zt_mm(s):
+        o = 480 * (s - 1)
+        mm(T.pz[:, 0:128], [("pz", 0, 512)], T.zg[:, o:o + 128], T.idb[:], [("zg", o, o + 128), ("idb", 0, 128)], True, True)
+
+    def zt_act():
+        act(T.zT[:], [("zT", 0, 128)], T.pz[:, 0:128], [("pz", 0, 512)], ID, scale=-1.0)
+
+    def count_mm(s):
+        o = 480 * s
+        for c in range(16):
+            mm(T.pc[:, 0:30], [("pc", 0, 512)], T.U[:, 15 - c:143 - c], T.zg[:, o + c:o + 480:16], [("U", 0, 144), ("zg", o, o + 480)], c == 0, c == 15)
+
+    def count_act(s):
+        o = 16 * (s - 1)
+        act(T.zsT[:, o:o + 15], [("zsT", o, o + 15)], T.pc[:, 0:15], [("pc", 0, 512)], ID, scale=1.0 / 16.0)
+        act(T.cntT[:, o:o + 15], [("cntT", o, o + 15)], T.pc[:, 15:30], [("pc", 0, 512)], ID, scale=1.0 / 16.0)
+
+    def stretch(s):
+        o = 480 * (s - 1)
+        for k in range(16):
+            op("V", lambda e: e.tensor_copy(T.zx[:, k::16], T.zg[:, o + 16 * NA:o + 240]), [("zg", o + 16 * NA, o + 240)], [("zx", 0, ND * 256)], waw=False)
+
+    def xmax(a):
+        r = 256 * (a - NA)
+        tt(T.Y[:, a, :], [("Y", 256 * a, 256 * a + 256)], T.xw[:, 0:V].indirect(T.kvu[:, 16 * a:16 * a + 16]), T.zx[:, r:r + 256],
+           [XW, ("kvu", 16 * a, 16 * a + 16), ("zx", r, r + 256)], A.max)
+
+    def pick(t, gr, s):
+        vI, vU = "vI%d" % (t % 2), "vU%d" % (t % 2)
+        a0, a1, o = a0s[gr], a1s[gr], 16 * s
+        pe, pk, R, eq, pr, C = ["%s%d" % (x, gr) for x in ("pe", "pk", "R", "eq", "pr", "C")]
+        op("V", lambda e: e.tensor_tensor_scan(T[R][:], T.rm[:, 0:128], T[pe][:, 0:128], 0.0, A.mult, A.max), [("rm", 0, 128), (pe, 0, 512)], [(R, 0, 128)])
+        tt(T[eq][:], [(eq, 0, 128)], T[R][:], T[pe][:, 0:128], [(R, 0, 128), (pe, 0, 512)], A.is_equal)
+        tt(T[pr][:], [(pr, 0, 128)], T[eq][:], T[pk][:, 0:4, :], [(eq, 0, 128), (pk, 0, 512)], A.mult)
+        op("V", lambda e: e.tensor_tensor_scan(T[C][:], T.rm[:, 0:128], T[pr][:], 0.0, A.mult, A.max), [("rm", 0, 128), (pr, 0, 128)], [(C, 0, 128)])
+        cp(T.codeI[:, o - 16 + a0:o - 16 + a1], [("codeI", o - 16 + a0, o - 16 + a1)], T[C][:, 15:16 * (a1 - a0):16], [(C, 0, 128)])
+        ts(T[vI][:, o + a0:o + a1], [(vI, o + a0, o + a1)], T.codeI[:, o - 16 + a0:o - 16 + a1], [("codeI", o - 16 + a0, o - 16 + a1)], 4095, None, A.bitwise_and)
+        cp(T[vU][:, o + a0:o + a1], [(vU, o + a0, o + a1)], T[vI][:, o + a0:o + a1], [(vI, o + a0, o + a1)])
+
+    def zstep(t, gr, s):
+        vU = "vU%d" % (t % 2)
+        a0, a1 = a0s[gr], a1s[gr]
+        lo, hi, n, o = 16 * a0, 16 * a1, 16 * (a1 - a0), 480 * (s - 1)
+        sh = th = "sh%d" % gr
+        lst = T.xw[:, 0:V].indirect(T[vU][:, 16 * s + a0:16 * s + a1])
+        rd = [XW, (vU, 16 * s + a0, 16 * s + a1), ("zg", o + lo, o + hi)]
+        zp = T.zg[:, o + lo:o + hi]
+        tt(T[sh][:, 0:n], [(sh, 0, n)], lst, zp, rd, A.add)
+        tt(T.zg[:, o + 720 + lo:o + 720 + hi], [("zg", o + 720 + lo, o + 720 + hi)], lst, zp, rd, A.is_gt)
+        ts(T[th][:, 0:n], [(th, 0, n)], T[sh][:, 0:n], [(sh, 0, n)], 0.5, 1023.75, A.mult, A.add)
+        ts(T.zg[:, o + 480 + lo:o + 480 + hi], [("zg", o + 480 + lo, o + 480 + hi)], T[th][:, 0:n], [(th, 0, n)], -1024.0, None, A.add)
+
+    def race(t):
+        vI, vU = "vI%d" % (t % 2), "vU%d" % (t % 2)
+        for gr in range(2):
+            knew(t, gr, 1)
+            kact(t, gr, 1)
+        ktr(0)
+        for s in range(1, S + 1):
+            zt_mm(s)
+            kswap(0)
+            xgat(0)
+            zt_act()
+            stretch(s)
+            xgat(1)
+            for a in range(NA, NA + 4):
+                xmax(a)
+            xsub(0)
+            xrelu(0)
+            xsub(1)
+            score(1, NA, NA + 4, True, False)
+            if s > 1:
+                count_mm(s - 1)
+                kact(t, 1, s)
+            xgat(2)
+            xrelu(1)
+            for a in range(NA + 4, 15):
+                xmax(a)
+            ktr(1)
+            xsub(2)
+            score(0, 0, 4, True, False)
+            xgat(3)
+            xrelu(2)
+            xsub(3)
+            xrelu(3)
+            if s > 1:
+                count_act(s - 1)
+            score(1, NA + 4, 15, False, True)
+            kswap(1)
+            score(0, 4, 8, False, True)
+            for gr in range(2):
+                pick(t, gr, s)
+                if s < S:
+                    knew(t, gr, s + 1)
+                    if gr == 0:
+                        kact(t, gr, s + 1)
+                zstep(t, gr, s)
+                if s < S and gr == 0:
+                    ktr(0)
+        count_mm(S)
+        count_act(S)
+        finish(t, vI, vU)
+
+    def finish(t, vI, vU):
+        f64, f16 = (0, 64), (0, 16)
+        tt(T.wz[:], [("wz",) + f64], T[vI][:, 16:80], T.zsT[:], [(vI, 16, 80), ("zsT",) + f64], A.mult)
+        ts(T.nb[:], [("nb",) + f64], T.cntT[:], [("cntT",) + f64, ("thr", 0, 1)], T.thr[:], BIG, A.is_lt, A.mult)
+        ts(T.u4[:], [("u4",) + f64], T.wz[:], [("wz",) + f64], 4095, None, A.bitwise_and)
+        tt(T.nb[:], [("nb",) + f64], T.nb[:], T.base[:], [("nb",) + f64, ("base",) + f64], A.add)
+        tt(T.c1[:], [("c1",) + f64], T.u4[:], T.nb[:], [("u4",) + f64, ("nb",) + f64], A.add)
+        tt(T.m1[:], [("m1", 0, 32)], T.c1[:, 0:32], T.c1[:, 32:64], [("c1",) + f64], A.min)
+        oo = 16 * t
+        OW = ("own", oo, oo + 16)
+        own = T.own[:, oo:oo + 16]
+        tt(own, [OW], T.m1[:, 0:16], T.m1[:, 16:32], [("m1", 0, 32)], A.min)
+        rs = 48 * t
+        ne = send("w", own, [T.rcv[:, rs + 16 * j:rs + 16 * j + 16] for j in range(3)], [OW], "a%d" % t, "l%d" % t)
+        arrival("a%d" % t, 3 * ne, [], [("rcv", rs, rs + 48)])
+        ts(T.nb[:], [("nb",) + f64], T.cntT[:], [("cntT",) + f64, ("thr", 0, 1)], T.thr[:], BIG, A.is_lt, A.mult)
+        tt(T.d1[:], [("d1",) + f64], T[vI][:, 16:80], T.bs[:], [(vI, 16, 80), ("bs",) + f64], A.add)
+        tt(T.d1[:], [("d1",) + f64], T.d1[:], T.nb[:], [("d1",) + f64, ("nb",) + f64], A.add)
+        tt(T.m2[:], [("m2", 0, 32)], T.d1[:, 0:32], T.d1[:, 32:64], [("d1",) + f64], A.min)
+        tt(T.dI[:], [("dI",) + f16], T.m2[:, 0:16], T.m2[:, 16:32], [("m2", 0, 32)], A.min)
+        ts(T.WI[:], [("WI",) + f16], T.dI[:], [("dI",) + f16], 4095, None, A.bitwise_and)
+        ts(T.bI[:], [("bI",) + f16], T.dI[:], [("dI",) + f16], 12, 7, A.arith_shift_right, A.bitwise_and)
+        ts(T.kI[:], [("kI",) + f64], T.codeI[:], [("codeI",) + f64], 12, None, A.arith_shift_right)
+        cp(T.WU[:], [("WU",) + f16], T.WI[:], [("WI",) + f16])
+        ts(T.bF[:], [("bF",) + f16], T.bI[:], [("bI",) + f16], 4.0, 480.0, A.min, A.mult)
+        cp(T.kU[:], [("kU",) + f64], T.kI[:], [("kI",) + f64])
+        tt(T.bF[:], [("bF",) + f16], T.bF[:], T.ln[:], [("bF",) + f16, ("ln",) + f16], A.add)
+        cp(T.bU[:], [("bU",) + f16], T.bF[:], [("bF",) + f16])
+        ts(T.P1[:], [("P1",) + f64], T[vI][:, 0:64], [(vI, 0, 64)], 1.0, None, A.add)
+        ts(T.Wp[:], [("Wp",) + f16], T.WI[:], [("WI",) + f16], 4097.0, None, A.add)
+        tt(T.vD[:, 0:64], [("vD", 0, 64)], T[vI][:, 0:64], T.Dm[:], [(vI, 0, 64), ("Dm",) + f64], A.subtract)
+        tt(T.vD[:, 64:80], [("vD", 64, 80)], T.WI[:], T.Dm[:, 0:16], [("WI",) + f16, ("Dm", 0, 16)], A.subtract)
+        act(T.xW[:], [("xW", 0, 240)], T.xw[:, 0:V].indirect(T.WU[:, 0:15]), [XW, ("WU",) + f16])
+        for s in range(S, 0, -1):
+            act(T.Bs[:, 240 * s - 240:240 * s], [("Bs", 240 * s - 240, 240 * s)], T.Wk[:].indirect(T.kU[:, 16 * s - 16:16 * s - 1]),
+                [("Wk",) + f16, ("kU",) + f64], ID, bias=-131072.0, scale=1024.0 * s)
+        for s in range(2, S + 1):
+            cp(T.vall[:, 240 * s - 240:240 * s], [("vall", 240 * s - 240, 240 * s)], T.iw[:].indirect(T[vU][:, 16 * s - 16:16 * s - 1]), [("iw", 0, 8192), (vU, 16 * s - 16, 16 * s)])
+        tt(T.xs2[:], [("xs2", 0, 240)], T.zg[:].indirect(T.bU[:, 0:15]), T.xW[:], [("zg", 0, 2400), ("bU",) + f16, ("xW", 0, 240)], A.add)
+        ts(T.xt2[:], [("xt2", 0, 240)], T.xs2[:], [("xs2", 0, 240)], 0.5, 1023.75, A.mult, A.add)
+        ts(T.xn[:], [("xn", 0, 240)], T.xt2[:], [("xt2", 0, 240)], -1024.0, None, A.add)
+        if t + 1 < RACES:
+            v_start(t + 1)
+            z_start(t + 1)
+        def rc(j, lo, hi):
+            o = rs + 16 * (j - 1)
+            return T.rcv[:, o + lo:o + hi]
+        RC, WM = ("rcv", rs, rs + 48), ("Wm", 0, 16)
+        cp(T.Wm[:], [WM], own, [OW])
+        tt(T.Wm[:, 0:10], [("Wm", 0, 10)], T.own[:, oo:oo + 10], rc(3, 5, 15), [OW, RC], A.min)
+        tt(T.Wm[:, 10:15], [("Wm", 10, 15)], T.own[:, oo + 10:oo + 15], rc(2, 0, 5), [OW, RC], A.min)
+        tt(T.Wm[:, 0:5], [("Wm", 0, 5)], T.Wm[:, 0:5], rc(2, 10, 15), [WM, RC], A.min)
+        tt(T.Wm[:, 5:15], [("Wm", 5, 15)], T.Wm[:, 5:15], rc(1, 0, 10), [WM, RC], A.min)
+        ts(T.x1[:], [("x1",) + f16], T.Wm[:], [WM], BIG, None, A.is_lt)
+        tt(T.x2[:], [("x2",) + f16], T.Wm[:], own, [WM, OW], A.not_equal)
+        cp(T.WmI[:], [("WmI",) + f16], T.Wm[:], [WM])
+        tt(T.lost[:], [("lost",) + f16], T.x1[:], T.x2[:], [("x1",) + f16, ("x2",) + f16], A.mult)
+        ts(T.bw[:], [("bw",) + f16], T.WmI[:], [("WmI",) + f16], 14, 7, A.arith_shift_right, A.bitwise_and)
+        ts(T.uwI[:], [("uwI",) + f16], T.WmI[:], [("WmI",) + f16], 4095, None, A.bitwise_and)
+        tt(T.lc[:], [("lc",) + f16], T.bw[:], T.lost[:], [("bw",) + f16, ("lost",) + f16], A.mult)
+        tt(T.won[:], [("won",) + f16], T.x1[:], T.lost[:], [("x1",) + f16, ("lost",) + f16], A.subtract)
+        cp(T.uwU[:], [("uwU",) + f16], T.uwI[:], [("uwI",) + f16])
+        for s in range(1, S + 1):
+            ts(T.on[:, 16 * s - 16:16 * s], [("on", 16 * s - 16, 16 * s)], T.lc[:], [("lc",) + f16], float(s), None, A.is_ge)
+        tt(T.kt1[:], [("kt1",) + f16], T.won[:], T.Wp[:], [("won",) + f16, ("Wp",) + f16], A.mult)
+        tt(T.kk[:], [("kk",) + f64], T.P1[:], T.on[:], [("P1",) + f64, ("on",) + f64], A.mult)
+        tt(T.kk[:, 0:16], [("kk", 0, 16)], T.kk[:, 0:16], T.kt1[:], [("kk", 0, 16), ("kt1",) + f16], A.add)
+        ts(T.key[:], [("key",) + f64], T.kk[:], [("kk",) + f64], -1.0, None, A.add)
+        cp(T.keyU[:], [("keyU",) + f16], T.key[:, 0:16], [("key", 0, 16)])
+        cp(T.wonb[:], [("wonb",) + f16], T.won[:], [("won",) + f16])
+        cp(T.vall[:, 0:240], [("vall", 0, 240)], T.iw[:].indirect(T.keyU[:, 0:15]), [("iw", 0, 8192), ("keyU",) + f16])
+        bank = {4: "pe0", 3: "pe1", 2: "pa0", 1: "pz"}
+
+        def flat(b, lo, hi):
+            return T[b][:, 0, lo:hi] if b == "pa0" else T[b][:, lo:hi]
+        for s in range(S, 0, -1):
+            o = 1920 * (s - 1)
+            for a in range(15):
+                n = 240 - 16 * a
+                ts(T.eqm[:, o:o + n], [("eqm", o, o + n)], T.vall[:, 240 * s - n:240 * s], [("vall", 240 * s - n, 240 * s), ("key",) + f64],
+                   T.key[:, 16 * s - 16 + a:16 * s - 15 + a], None, A.is_equal)
+                mm(flat(bank[s], 16 * a, 240), [(bank[s], 0, 512)], T.Wt[:, 128 * a:128 * a + 128], T.eqm[:, o:o + n], [("Wt", 0, 1920), ("eqm", o, o + n)], a == 0, a == 14)
+                o += n
+            if s == S:
+                cp(T.urep[:], [("urep", 0, 240)], T.iw[:].indirect(T.uwU[:, 0:15]), [("iw", 0, 8192), ("uwU",) + f16])
+            r = 240 * s - 240
+            tt(T.xs[:, r:r + 240], [("xs", r, r + 240)], T.Wk[:].indirect(T.kU[:, 16 * s - 16:16 * s - 1]), T.urep[:], [("Wk",) + f16, ("kU",) + f64, ("urep", 0, 240)], A.mult)
+        mm(T.pc[:, 0:15], [("pc", 0, 512)], T.ones[:], T.wonb[:, 0:15], [("ones", 0, 128), ("wonb",) + f16], True, True)
+        for s in range(S, 0, -1):
+            r = 240 * s - 240
+            tt(T.fl[:], [("fl", 0, 240)], flat(bank[s], 0, 240), T.W2d[:], [(bank[s], 0, 512), ("W2d", 0, 240)], A.is_lt)
+            op("V", lambda e: e.tensor_tensor_scan(T.Fs[:, r:r + 240], T.rmb[:, 0:240], T.fl[:], 0.0, A.mult, A.add), [("rmb", 0, 240), ("fl", 0, 240)], [("Fs", r, r + 240)])
+        fs = T.Fs[:, 15:960:16]
+        for s in range(1, S + 1):
+            o = 16 * s - 16
+            tt(T.fo[:, o:o + 15], [("fo", o, o + 15)], T.Fs[:, 15 * o + 15:15 * o + 240:16], T.on[:, o:o + 15], [("Fs", 15 * o, 15 * o + 240), ("on",) + f64], A.mult)
+        tt(T.fo[:, 64:79], [("fo", 64, 79)], T.Fs[:, 15:240:16], T.won[:, 0:15], [("Fs", 0, 240), ("won",) + f16], A.mult)
+        tt(T.of[:], [("of", 0, 80)], T.fo[:], T.vD[:], [("fo", 0, 80), ("vD", 0, 80)], A.mult)
+        tt(T.of[:, 0:64], [("of", 0, 64)], T.of[:, 0:64], T.Dm[:], [("of", 0, 64), ("Dm",) + f64], A.add)
+        tt(T.of[:, 64:80], [("of", 64, 80)], T.of[:, 64:80], T.Dm[:, 0:16], [("of", 64, 80), ("Dm", 0, 16)], A.add)
+        cp(T.offU[:], [("offU", 0, 80)], T.of[:], [("of", 0, 80)])
+        cp(T.xw[:].indirect(T.offU[:, 64:79]), [("xw", 0, WIN)], T.xn[:], [("xn", 0, 240), ("offU", 0, 80)])
+        for s in range(S, 0, -1):
+            r = 240 * s - 240
+            lst = T.kw[:, 0:V].indirect(T[vU][:, 16 * s - 16:16 * s - 1])
+            RD = [KW, (vU, 16 * s - 16, 16 * s)]
+            tt(T.kp[:], [("kp", 0, 240)], lst, T.xs[:, r:r + 240], RD + [("xs", r, r + 240)], A.mult)
+            tt(T.kt[:], [("kt", 0, 240)], lst, T.Bs[:, r:r + 240], RD + [("Bs", r, r + 240)], A.add)
+            tt(T.kz[:], [("kz", 0, 240)], T.kp[:], T.kt[:], [("kp", 0, 240), ("kt", 0, 240)], A.add)
+            ts(T.kn[:], [("kn", 0, 240)], T.kz[:], [("kz", 0, 240)], 131040, None, A.bitwise_and)
+            cp(T.kw[:].indirect(T.offU[:, 16 * s - 16:16 * s - 1]), [("kw", 0, WIN)], T.kn[:], [("kn", 0, 240), ("offU", 0, 80)])
+        if t + 1 < RACES:
+            op("V", lambda e: e.tensor_reduce(T.tot[:], T.pc[:, 0:15], AxisListType.X, A.add), [("pc", 0, 512)], [("tot", 0, 1)])
+            cp(T.totI[:], [("totI", 0, 1)], T.tot[:], [("tot", 0, 1)])
+            ts(T.totI[:], [("totI", 0, 1)], T.totI[:], [("totI", 0, 1)], 1, None, A.bitwise_and)
+            ts(T.thr[:], [("thr", 0, 1)], T.totI[:], [("totI", 0, 1)], 12.0, None, A.add)
+
+    for t in range(RACES):
+        race(t)
+    for a in range(8):
+        act(T.idx[:, 128 * a:128 * a + 128], [("idx", 128 * a, 128 * a + 128)], T.idb[:], [("idb", 0, 128)], ID, scale=float(a + 1))
+    for a in range(4):
+        act(T.idk[:, 128 * a:128 * a + 128], [("idk", 128 * a, 128 * a + 128)], T.idb[:], [("idb", 0, 128)], ID, scale=(a + 1) / 32.0)
+    for a in range(8):
+        mm(T.pe0[:], [("pe0", 0, 512)], T.idx[:, 128 * a:128 * a + 128], T.xw[:, 512 * a:512 * a + 512], [("idx", 0, 1024), ("xw", 512 * a, 512 * a + 512)], a == 0, a == 7)
+    act(T.ox[:], [("ox", 0, 512)], T.pe0[:], [("pe0", 0, 512)])
+    dma("Y", "oy", T.yx[:], T.ox[:], [("ox", 0, 512)], [])
+    for a in range(4):
+        mm(T.pe1[:], [("pe1", 0, 512)], T.idk[:, 128 * a:128 * a + 128], T.kw[:, 512 * a:512 * a + 512], [("idk", 0, 512), ("kw", 512 * a, 512 * a + 512)], a == 0, a == 3)
+    pb = {4: "pk0", 5: "pk1", 6: "pz", 7: "pc"}
+    for a in range(4, 8):
+        out = T[pb[a]][:, :, :] if a < 6 else T[pb[a]][:]
+        act(out, [(pb[a], 0, 512)], T.kw[:, 512 * a:512 * a + 512], [("kw", 512 * a, 512 * a + 512)], ID, scale=(a + 1) / 32.0)
+    cp(T.ok[:], [("ok", 0, 512)], T.pk0[:, :, :], [("pk0", 0, 512)])
+    tt(T.ok[:], [("ok", 0, 512)], T.ok[:], T.pk1[:, :, :], [("ok", 0, 512), ("pk1", 0, 512)], A.add)
+    for b in ("pz", "pc", "pe1"):
+        tt(T.ok[:], [("ok", 0, 512)], T.ok[:], T[b][:], [("ok", 0, 512), (b, 0, 512)], A.add)
+    dma("Y", "ok", T.yk[:], T.ok[:], [("ok", 0, 512)], [])
+    g.sync.wait_ge(T.sem.oy, 16)
+    g.sync.wait_ge(T.sem.ok, 16)
+    for q in "VSTG":
+        g.wait_ge(T.sem["q" + q], cnt[q])
+    for l in ("lz", "lv", "l0", "l1", "l2"):
+        g.wait_ge(T.sem[l], ne)
+
+
+SCRATCH["ones"] = ("sbuf", [128, 128], "bfloat16")

@@ -4,211 +4,272 @@ from concourse.mybir import AluOpType, AxisListType, ActivationFunctionType
 A = AluOpType
 ID = ActivationFunctionType.Identity
 RELU = ActivationFunctionType.Relu
+ABS = ActivationFunctionType.Abs
+SIGN = ActivationFunctionType.Sign
 N, M, J, RACES, S, V = 4, 80, 3, 3, 4, 4096
 L = J * M
-NA = 8
-ND = 15 - NA
+GROUPS = ((0, 4, True), (4, 8, True), (8, 15, False))
+BIAS = (4000.0, 1000.0, 1500.0)
+ND = 7
+NX = 3
+ACT_EVENTS = (1,)
 WIN = V + 256
 BIG = 2.0 ** 19
+CYC, LAT, GAMMA, SIGMA = 0.9, 160.0, 1.8, 3.5
 
-SCRATCH = {
-    "xw": ("sbuf", [128, WIN], "bfloat16"), "kw": ("sbuf", [128, WIN], "float32"), "kin": ("sbuf", [128, V], "int32"),
-    "iw": ("sbuf", [128, 8192], "float32"),
-    "Y": ("sbuf", [128, 15, 256], "bfloat16"), "zx": ("sbuf", [128, ND * 256], "bfloat16"),
-    "kvu": ("sbuf", [128, 256], "uint16"), "kvf0": ("sbuf", [128, 128], "float32"), "kvf1": ("sbuf", [128, 128], "float32"),
-    "Tt0": ("sbuf", [128, 4, 32], "float32"), "Tt1": ("sbuf", [128, 4, 32], "float32"),
-    "xg0": ("sbuf", [128, 512], "bfloat16"), "xg1": ("sbuf", [128, 512], "bfloat16"),
-    "zT": ("sbuf", [128, 128], "bfloat16"), "E": ("sbuf", [128, 2048], "bfloat16"),
-    "zg": ("sbuf", [128, 2400], "bfloat16"), "sh0": ("sbuf", [128, 128], "float16"), "sh1": ("sbuf", [128, 128], "float16"),
-    "R0": ("sbuf", [128, 128], "float32"), "R1": ("sbuf", [128, 128], "float32"),
-    "eq0": ("sbuf", [128, 128], "float32"), "eq1": ("sbuf", [128, 128], "float32"),
-    "pr0": ("sbuf", [128, 128], "float32"), "pr1": ("sbuf", [128, 128], "float32"),
-    "C0": ("sbuf", [128, 128], "float32"), "C1": ("sbuf", [128, 128], "float32"),
-    "codeI": ("sbuf", [128, 64], "int32"), "vI0": ("sbuf", [128, 80], "int32"), "vI1": ("sbuf", [128, 80], "int32"),
-    "vU0": ("sbuf", [128, 80], "uint16"), "vU1": ("sbuf", [128, 80], "uint16"),
-    "kI": ("sbuf", [128, 64], "int32"), "kU": ("sbuf", [128, 64], "uint16"),
-    "zsT": ("sbuf", [128, 64], "float32"), "cntT": ("sbuf", [128, 64], "float32"),
-    "wz": ("sbuf", [128, 64], "int32"), "u4": ("sbuf", [128, 64], "int32"), "nb": ("sbuf", [128, 64], "float32"),
-    "c1": ("sbuf", [128, 64], "float32"), "m1": ("sbuf", [128, 32], "float32"), "own": ("sbuf", [128, 48], "float32"),
-    "d1": ("sbuf", [128, 64], "float32"), "m2": ("sbuf", [128, 32], "float32"), "dI": ("sbuf", [128, 16], "int32"),
-    "WI": ("sbuf", [128, 16], "int32"), "WU": ("sbuf", [128, 16], "uint16"), "bF": ("sbuf", [128, 16], "float32"),
-    "bI": ("sbuf", [128, 16], "int32"), "bU": ("sbuf", [128, 16], "uint16"),
-    "rcv": ("sbuf", [128, 144], "float32"), "Wm": ("sbuf", [128, 16], "float32"),
-    "x1": ("sbuf", [128, 16], "float32"), "x2": ("sbuf", [128, 16], "float32"), "lost": ("sbuf", [128, 16], "float32"),
-    "won": ("sbuf", [128, 16], "float32"), "wonb": ("sbuf", [128, 16], "bfloat16"), "WmI": ("sbuf", [128, 16], "int32"),
-    "bw": ("sbuf", [128, 16], "int32"), "uwI": ("sbuf", [128, 16], "int32"), "uwU": ("sbuf", [128, 16], "uint16"),
-    "lc": ("sbuf", [128, 16], "float32"), "on": ("sbuf", [128, 64], "float32"), "P1": ("sbuf", [128, 64], "float32"),
-    "Wp": ("sbuf", [128, 16], "float32"), "kk": ("sbuf", [128, 64], "float32"), "kt1": ("sbuf", [128, 16], "float32"),
-    "key": ("sbuf", [128, 64], "float32"), "keyU": ("sbuf", [128, 16], "uint16"),
-    "vall": ("sbuf", [128, 960], "uint16"), "eqm": ("sbuf", [128, 7680], "bfloat16"),
-    "fl": ("sbuf", [128, 240], "bfloat16"), "Fs": ("sbuf", [128, 960], "bfloat16"), "fo": ("sbuf", [128, 80], "float32"),
-    "vD": ("sbuf", [128, 80], "float32"), "of": ("sbuf", [128, 80], "float32"), "offU": ("sbuf", [128, 80], "uint16"),
-    "urep": ("sbuf", [128, 240], "float32"), "xs": ("sbuf", [128, 960], "float32"), "Bs": ("sbuf", [128, 960], "float32"),
-    "kp": ("sbuf", [128, 240], "float32"), "kt": ("sbuf", [128, 240], "float32"), "kz": ("sbuf", [128, 240], "int32"),
-    "kn": ("sbuf", [128, 240], "int32"),
-    "xW": ("sbuf", [128, 240], "bfloat16"), "xs2": ("sbuf", [128, 240], "float16"), "xt2": ("sbuf", [128, 240], "float16"),
-    "xn": ("sbuf", [128, 240], "bfloat16"), "tot": ("sbuf", [128, 1], "float32"), "totI": ("sbuf", [128, 1], "int32"),
-    "thr": ("sbuf", [128, 1], "float32"),
-    "zs": ("sbuf", [128, 240], "bfloat16"), "vs": ("sbuf", [128, 45], "int32"), "zl": ("sbuf", [128, 720], "bfloat16"),
-    "vl": ("sbuf", [128, 135], "int32"),
-    "pI": ("sbuf", [128, 8], "int32"), "pF": ("sbuf", [128, 24], "float32"),
-    "idb": ("sbuf", [128, 128], "bfloat16"), "Pm": ("sbuf", [128, 512], "float32"), "U": ("sbuf", [128, 144], "bfloat16"),
-    "bo1": ("sbuf", [128, 128], "bfloat16"), "bo2": ("sbuf", [128, 128], "bfloat16"), "BO": ("sbuf", [128, 128], "bfloat16"),
-    "BW": ("sbuf", [128, 128], "bfloat16"), "Wt": ("sbuf", [128, 1920], "bfloat16"), "W2d": ("sbuf", [128, 240], "float32"),
-    "dg": ("sbuf", [128, 16], "float32"), "Wk": ("sbuf", [128, 16], "bfloat16"), "rm": ("sbuf", [128, 256], "float32"),
-    "rmb": ("sbuf", [128, 256], "bfloat16"), "kc": ("sbuf", [128, 128], "bfloat16"), "base": ("sbuf", [128, 64], "float32"),
-    "bs": ("sbuf", [128, 64], "float32"), "Dm": ("sbuf", [128, 64], "float32"), "ln": ("sbuf", [128, 16], "float32"),
-    "idx": ("sbuf", [128, 1024], "bfloat16"), "idk": ("sbuf", [128, 512], "float32"),
-    "ox": ("sbuf", [128, 512], "float32"), "ok": ("sbuf", [128, 512], "float32"),
-    "pe0": ("psum", [128, 512], "float32"), "pe1": ("psum", [128, 512], "float32"),
-    "pk0": ("psum", [128, 16, 32], "float32"), "pk1": ("psum", [128, 16, 32], "float32"),
-    "pa0": ("psum", [128, 2, 256], "float32"), "pa1": ("psum", [128, 2, 256], "float32"),
-    "pz": ("psum", [128, 512], "float32"), "pc": ("psum", [128, 512], "float32"),
-}
+SCRATCH = {}
+for _n, _w, _d in (
+        ("xw", WIN, "bfloat16"), ("kw", WIN, "float32"), ("kin", V, "int32"), ("iw", 8192, "float32"), ("zx", ND * 256, "bfloat16"),
+        ("kvu", 256, "uint16"), ("kvf", 384, "float32"), ("sh", 384, "float16"), ("xq", 384, "bfloat16"), ("R", 384, "float32"),
+        ("eq", 384, "float32"), ("pr", 384, "float32"), ("C", 384, "float32"), ("zT0", 128, "bfloat16"), ("zT1", 128, "bfloat16"),
+        ("E", 1024, "bfloat16"), ("xg0", 512, "bfloat16"), ("xg1", 512, "bfloat16"), ("xg2", 512, "bfloat16"), ("zg", 2400, "bfloat16"),
+        ("codeI", 64, "int32"), ("vI0", 80, "int32"), ("vI1", 80, "int32"), ("vU0", 80, "uint16"), ("vU1", 80, "uint16"),
+        ("kI", 64, "int32"), ("kU", 64, "uint16"), ("zsT", 64, "float32"), ("cntT", 64, "float32"), ("wz", 64, "int32"),
+        ("u4", 64, "int32"), ("nb", 64, "float32"), ("c1", 64, "float32"), ("m1", 32, "float32"), ("own", 48, "float32"),
+        ("d1", 64, "float32"), ("dI", 16, "int32"), ("WI", 16, "int32"), ("WU", 16, "uint16"), ("bF", 16, "float32"),
+        ("bI", 16, "int32"), ("bU", 16, "uint16"), ("rcv", 144, "float32"), ("Wm", 16, "float32"), ("x1", 16, "float32"),
+        ("x2", 16, "float32"), ("lost", 16, "float32"), ("won", 16, "float32"), ("wonb", 16, "bfloat16"), ("WmI", 16, "int32"),
+        ("bw", 16, "int32"), ("uwI", 16, "int32"), ("uwU", 16, "uint16"), ("lc", 16, "float32"), ("on", 64, "float32"),
+        ("P1", 64, "float32"), ("Wp", 16, "float32"), ("kk", 64, "float32"), ("kt1", 16, "float32"), ("key", 64, "float32"),
+        ("nkey", 64, "float32"), ("keyU", 16, "uint16"), ("vall", 960, "uint16"), ("valf", 240, "float32"), ("eqm", 7680, "bfloat16"),
+        ("fl", 960, "bfloat16"), ("Fs", 960, "bfloat16"), ("fo", 80, "float32"), ("vD", 80, "float32"), ("of", 80, "float32"),
+        ("offU", 80, "uint16"), ("urep", 240, "float32"), ("xs", 960, "float32"), ("Bs", 960, "bfloat16"), ("kp", 240, "float32"),
+        ("kt", 240, "float32"), ("kz", 240, "int32"), ("kn", 240, "int32"), ("xW", 240, "bfloat16"), ("xs2", 240, "float16"),
+        ("xt2", 240, "float16"), ("xn", 240, "bfloat16"), ("tot", 1, "float32"), ("totI", 1, "int32"), ("thr", 1, "float32"),
+        ("zs", 240, "bfloat16"), ("vs", 45, "int32"), ("zl", 720, "bfloat16"), ("vl", 135, "int32"), ("pI", 8, "int32"),
+        ("pF", 24, "float32"), ("idb", 128, "bfloat16"), ("idn", 128, "bfloat16"), ("idf", 128, "float32"), ("idS", 512, "bfloat16"),
+        ("Pm", 512, "float32"), ("U", 144, "bfloat16"), ("bo1", 128, "bfloat16"), ("BO", 128, "bfloat16"), ("BW", 128, "bfloat16"),
+        ("Wt", 1920, "bfloat16"), ("W2d", 240, "float32"), ("dg", 16, "float32"), ("Wk", 16, "bfloat16"), ("rm", 256, "float32"),
+        ("rmb", 256, "bfloat16"), ("kc", 128, "bfloat16"), ("base", 64, "float32"), ("bs", 64, "float32"), ("Dm", 64, "float32"),
+        ("ln", 16, "float32"), ("idx", 1024, "bfloat16"), ("idk", 512, "float32"), ("ox", 512, "float32"), ("ok", 512, "float32"),
+        ("ones", 128, "bfloat16")):
+    SCRATCH[_n] = ("sbuf", [128, _w], _d)
+SCRATCH["Y"] = ("sbuf", [128, 16, 256], "bfloat16")
+SCRATCH["Tt"] = ("sbuf", [128, 12, 32], "float32")
+for _n in ("ps", "pz", "pc"):
+    SCRATCH[_n] = ("psum", [128, 512], "float32")
+for _n in ("pb0", "pb1", "pb2"):
+    SCRATCH[_n] = ("psum", [128, 4, 128], "float32")
+for _n in ("pa0", "pa1"):
+    SCRATCH[_n] = ("psum", [128, 2, 256], "float32")
 SEMAPHORES = ["qV", "qS", "qT", "qG", "zin", "vin", "k0", "k1", "k2", "k3", "x0", "x1", "az", "av", "a0", "a1", "a2",
               "lz", "lv", "l0", "l1", "l2", "oy", "ok"]
 
 
-def tracker(g, T):
+def planner(g, T):
     queues = {"V": g.vector, "S": g.scalar, "T": g.tensor, "G": g, "Y": g.sync}
-    cnt = {"V": 0, "S": 0, "T": 0, "G": 0}
-    clk = {q: {} for q in queues}
-    snap = {}
-    recs = {}
+    ops = []
+    plan = {}
+    bias = [0.0]
 
     def is_psum(b):
-        return SCRATCH[b][0] == "psum" if b in SCRATCH else False
+        return b in SCRATCH and SCRATCH[b][0] == "psum"
 
-    def waits(q, R, W, waw=True):
-        need = {}
-
-        def add(r):
-            if need.get(r[4], 0) < r[5]:
-                need[r[4]] = r[5]
+    def hazards(recs, q, R, W):
+        out = []
         for b, lo, hi in R:
             ps = is_psum(b)
             for r in recs.get(b, []):
-                if ps:
-                    if r[3] != q or (r[2] and r[0] < hi and lo < r[1]):
-                        add(r)
-                elif r[2] and r[0] < hi and lo < r[1]:
-                    add(r)
+                if r[0] < hi and lo < r[1] and r[2] or ps and r[3] != q:
+                    out.append(r)
         for b, lo, hi in W:
             ps = is_psum(b)
             for r in recs.get(b, []):
-                if not (ps or (r[0] < hi and lo < r[1])):
+                if ps or (r[0] < hi and lo < r[1]):
+                    out.append(r)
+        return out
+
+    def note(recs, q, R, W, tag):
+        for b, lo, hi in W:
+            recs[b] = [r for r in recs.get(b, []) if not (lo <= r[0] and r[1] <= hi)] + [(lo, hi, True, q, tag)]
+        for b, lo, hi in R:
+            recs[b] = [r for r in recs.get(b, []) if not (not r[2] and r[3] == q and lo <= r[0] and r[1] <= hi and q in "VSTG")] + [(lo, hi, False, q, tag)]
+
+    def rec(q, kind, fn, R, W, dur, lat, sem=None, val=0, after=None):
+        i = len(ops)
+        rq = q if kind == "c" else kind + str(i)
+        deps = {}
+        for r in hazards(plan, rq, R, W):
+            x = 0 if (q == "T" and ops[r[4]]["q"] == "T") else ops[r[4]]["lat"]
+            deps[r[4]] = max(deps.get(r[4], 0), x)
+        if after is not None:
+            deps[after] = 0
+        note(plan, rq, R, W, i)
+        ops.append({"q": q, "kind": kind, "fn": fn, "R": R, "W": W, "dur": dur, "lat": lat, "sem": sem, "val": val, "deps": deps, "rq": rq, "bias": bias[0]})
+        return i
+
+    def emit():
+        n = len(ops)
+        succ = [[] for _ in range(n)]
+        left = [len(o["deps"]) for o in ops]
+        for i, o in enumerate(ops):
+            for d, x in o["deps"].items():
+                succ[d].append((i, x))
+        prio = [0.0] * n
+        for i in range(n - 1, -1, -1):
+            prio[i] = ops[i]["dur"] + max([x + prio[k] for k, x in succ[i]] + [0.0])
+        free = {q: 0.0 for q in queues}
+        when = [0.0] * n
+        ready = {q: [i for i in range(n) if not left[i] and ops[i]["q"] == q] for q in list(queues) + ["N"]}
+        order = []
+
+        def done(i, t):
+            for k, x in succ[i]:
+                when[k] = max(when[k], t + ops[i]["dur"] + x)
+                left[k] -= 1
+                if not left[k]:
+                    ready[ops[k]["q"]].append(k)
+        while len(order) < n:
+            while ready["N"]:
+                i = ready["N"].pop()
+                order.append((when[i], len(order), i))
+                done(i, when[i])
+            best = None
+            for q in queues:
+                if ready[q]:
+                    t = max(free[q], min(when[i] for i in ready[q]))
+                    if best is None or t < best[0]:
+                        best = (t, q)
+            if best is None:
+                continue
+            t, q = best
+            i = max((i for i in ready[q] if when[i] <= t + 1.0), key=lambda i: (prio[i] + ops[i]["bias"], -i))
+            ready[q].remove(i)
+            st = max(t, when[i])
+            free[q] = st + ops[i]["dur"]
+            order.append((st, len(order), i))
+            done(i, st)
+        order.sort()
+        cnt = {q: 0 for q in queues}
+        clk = {q: {} for q in queues}
+        snap = {}
+        live = {}
+        for _, _, i in order:
+            o = ops[i]
+            q = o["q"]
+            if o["kind"] == "n":
+                snap[(o["sem"], o["val"])] = {}
+                note(live, o["rq"], o["R"], o["W"], (o["sem"], o["val"]))
+                continue
+            need = {}
+            for r in hazards(live, o["rq"], o["R"], o["W"]):
+                if q == "T" and r[3] == "T":
                     continue
-                if r[3] != q or (q in "VSG" and (waw or not r[2])):
-                    add(r)
-        c = clk[q]
-        items = [(s, v) for s, v in need.items() if c.get(s, 0) < v]
-        keep = []
-        for s, v in items:
-            if not any(o != (s, v) and snap.get(o, {}).get(s, 0) >= v for o in items):
-                keep.append((s, v))
-        for s, v in (keep if keep else items):
-            queues[q].wait_ge(T.sem[s], v)
-        for s, v in items:
-            c[s] = max(c.get(s, 0), v)
-            for k2, v2 in snap.get((s, v), {}).items():
-                if c.get(k2, 0) < v2:
-                    c[k2] = v2
-
-    def note(q, R, W, sem, val):
-        snap[(sem, val)] = dict(clk[q]) if q in clk else {}
-        for b, lo, hi in W:
-            old = recs.setdefault(b, [])
-            recs[b] = [r for r in old if not (lo <= r[0] and r[1] <= hi)] + [(lo, hi, True, q, sem, val)]
-        for b, lo, hi in R:
-            old = recs.setdefault(b, [])
-            recs[b] = [r for r in old if not (not r[2] and r[3] == q and lo <= r[0] and r[1] <= hi)] + [(lo, hi, False, q, sem, val)]
-
-    def op(q, fn, R, W, waw=True):
-        waits(q, R, W, waw)
-        cnt[q] += 1
-        sem = "q" + q
-        fn(queues[q]).then_inc(T.sem[sem], 1)
-        note(q, R, W, sem, cnt[q])
-
-    def dma(q, sem, out, in_, R, W, val=16):
-        waits(q, R, W)
-        queues[q].dma_start(out, in_).then_inc(T.sem[sem], 16)
-        snap_q = dict(clk[q])
-        note("dma" + sem, R, W, sem, val)
-        snap[(sem, val)] = snap_q
-
-    def ready(q, R, W):
-        waits(q, R, W)
-
-    def arrival(sem, val, R, W):
-        note("net" + sem, R, W, sem, val)
-    return op, dma, ready, arrival, cnt, queues
+                sm, v = r[4]
+                if need.get(sm, 0) < v:
+                    need[sm] = v
+            c = clk[q]
+            items = [(sm, v) for sm, v in need.items() if c.get(sm, 0) < v]
+            for it in items:
+                if not any(x != it and snap.get(x, {}).get(it[0], 0) >= it[1] for x in items):
+                    queues[q].wait_ge(T.sem[it[0]], it[1])
+            for it in items:
+                for k2, v2 in list(snap.get(it, {}).items()) + [it]:
+                    if c.get(k2, 0) < v2:
+                        c[k2] = v2
+            ins = o["fn"](queues[q])
+            if o["kind"] == "c":
+                cnt[q] += 1
+                ins.then_inc(T.sem["q" + q], 1)
+                tag = ("q" + q, cnt[q])
+            else:
+                if o["kind"] == "d":
+                    ins.then_inc(T.sem[o["sem"]], 16)
+                tag = (o["sem"], o["val"])
+            snap[tag] = dict(c)
+            note(live, o["rq"], o["R"], o["W"], tag)
+        return cnt
+    return rec, emit, bias
 
 
 def rank_program(g, core, T, topo):
     rank = T.rank_of(core)
     if rank is None:
         return
-    op, dma, ready, arrival, cnt, queues = tracker(g, T)
+    rec, emit, bias = planner(g, T)
     peers = [T.cores[(rank + j) % N] for j in (1, 2, 3)]
 
+    def width(b):
+        return 2 if b not in SCRATCH or SCRATCH[b][2] in ("bfloat16", "float16", "uint16") else 4
+
+    def cost(W, R, two=False):
+        n = W[0][2] - W[0][1]
+        if W[0] in (("kw", 0, WIN), ("xw", 0, WIN)):
+            return 50 + SIGMA * L * CYC
+        if any(r[0] in ("kw", "xw", "Wk") or r[1:] == (0, 8192) for r in R):
+            return 50 + GAMMA * n * CYC
+        if two:
+            return max(64, n * (1 if any(SCRATCH[r[0]][0] == "psum" for r in R) else 2)) * CYC
+        return max(64, n * (0.5 if all(width(r[0]) == 2 for r in W[:1] + R[:1]) else 1)) * CYC
+
+    def op(q, fn, R, W, dur):
+        rec(q, "c", fn, R, W, dur, LAT)
+
     def iota(name, lo, hi, pattern, base, cm):
-        flag = SCRATCH[name][2] != "int32"
-        if flag:
-            op("G", lambda e: e.iota(T[name][:, lo:hi], pattern, base, cm, allow_small_or_imprecise_dtypes=True), [], [(name, lo, hi)])
+        if SCRATCH[name][2] != "int32":
+            fn = lambda e: e.iota(T[name][:, lo:hi], pattern, base, cm, allow_small_or_imprecise_dtypes=True)
         else:
-            op("G", lambda e: e.iota(T[name][:, lo:hi], pattern, base, cm), [], [(name, lo, hi)])
+            fn = lambda e: e.iota(T[name][:, lo:hi], pattern, base, cm)
+        op("G", fn, [], [(name, lo, hi)], 130 + 2 * (hi - lo) * CYC)
 
     def ts(out, W, in0, R, s1, s2, o0, o1=None):
         if o1 is None:
-            op("V", lambda e: e.tensor_scalar(out, in0, s1, None, o0), R, W)
+            op("V", lambda e: e.tensor_scalar(out, in0, s1, None, o0), R, W, cost(W, R))
         else:
-            op("V", lambda e: e.tensor_scalar(out, in0, s1, s2, o0, o1), R, W)
+            op("V", lambda e: e.tensor_scalar(out, in0, s1, s2, o0, o1), R, W, cost(W, R))
 
     def tt(out, W, in0, in1, R, o):
-        op("V", lambda e: e.tensor_tensor(out, in0, in1, o), R, W)
+        op("V", lambda e: e.tensor_tensor(out, in0, in1, o), R, W, cost(W, R, True))
 
     def cp(out, W, in_, R):
-        op("V", lambda e: e.tensor_copy(out, in_), R, W)
+        op("V", lambda e: e.tensor_copy(out, in_), R, W, cost(W, R))
+
+    def scan(out, W, d0, d1, R, o0, o1):
+        op("V", lambda e: e.tensor_tensor_scan(out, d0, d1, 0.0, o0, o1), R, W, cost(W, R))
 
     def act(out, W, in_, R, f=ID, bias=0.0, scale=1.0):
-        op("S", lambda e: e.activation(out, in_, f, bias=bias, scale=scale), R, W)
+        n = W[0][2] - W[0][1]
+        op("S", lambda e: e.activation(out, in_, f, bias=bias, scale=scale), R, W, max(cost(W, R), n * CYC))
 
-    def mm(out, W, lhsT, rhs, R, start, stop):
-        op("T", lambda e: e.matmul(out, lhsT, rhs, start, stop), R, W)
+    def mm(out, W, lhsT, rhs, R, start, stop, n=None):
+        n = n or R[-1][2] - R[-1][1]
+        op("T", lambda e: e.matmul(out, lhsT, rhs, start, stop), R, W, max(64, n) * 0.5 * (4 if SCRATCH[R[0][0]][2] == "float32" else 1))
 
     def ms(name, lo, hi, val):
-        op("V", lambda e: e.memset(T[name][:, lo:hi], val), [], [(name, lo, hi)])
+        op("V", lambda e: e.memset(T[name][:, lo:hi], val), [], [(name, lo, hi)], max(64, hi - lo) * CYC)
 
-    dma("Y", "zin", T.zs[:], T.z0[:], [], [("zs", 0, 240)])
-    dma("S", "vin", T.vs[:], T.v0[:], [], [("vs", 0, 45)])
-    for i in range(4):
-        dma("YS"[i % 2], "k%d" % i, T.kin[:, 1024 * i:1024 * i + 1024], T.k0[:, 1024 * i:1024 * i + 1024], [], [("kin", 1024 * i, 1024 * i + 1024)])
-    for i in range(2):
-        dma("YS"[i], "x%d" % i, T.xw[:, 2048 * i:2048 * i + 2048], T.x0[:, 2048 * i:2048 * i + 2048], [], [("xw", 2048 * i, 2048 * i + 2048)])
+    last = {}
 
-    def send(name, src, dsts, R, rsem, lsem):
-        ready("G", R, [])
+    def dma(q, sem, out, in_, R, W, lat):
+        last[q] = rec(q, "d", lambda e: e.dma_start(out, in_), R, W, 60.0, lat, sem, 16, after=last.get(q))
+
+    def send(src, dsts, R, W, rsem, lsem):
         ids = []
-        m = 0xFFFF
+        m = None
         for p in peers:
             a = topo.addr(p)
             ids.append(DstId(rid=a[0], pnc=a[1]))
-            m &= topo.mask(core, p)
-        g.remote_dma_fused([RemoteDMATransfer(dst_ids=ids, dma_engine_mask=m, remote_sem=T.sem[rsem], srcs=[src], dsts=dsts, alu_op=0)], local_sem=T.sem[lsem])
-        ne = sum(m >> e & 1 for e in range(16))
-        arrival(lsem, ne, R, [])
-        return ne
+            m = topo.mask(core, p) if m is None else m & topo.mask(core, p)
+        tr = RemoteDMATransfer(dst_ids=ids, dma_engine_mask=m, remote_sem=T.sem[rsem], srcs=[src], dsts=dsts, alu_op=0)
+        n = sum(m >> e & 1 for e in range(16))
+        i = rec("G", "s", lambda e: e.remote_dma_fused([tr], local_sem=T.sem[lsem]), R, [], 900.0, 1500.0, lsem, n)
+        rec("N", "n", None, [], W, 2500.0, LAT, rsem, 3 * n, after=i)
+        return n
+
+    dma("S", "zin", T.zs[:], T.z0[:], [], [("zs", 0, 240)], 2000.0)
+    dma("S", "vin", T.vs[:], T.v0[:], [], [("vs", 0, 45)], 2000.0)
+    for i in range(4):
+        dma("YS"[i % 2], "k%d" % i, T.kin[:, 1024 * i:1024 * i + 1024], T.k0[:, 1024 * i:1024 * i + 1024], [], [("kin", 1024 * i, 1024 * i + 1024)], 8000.0 + 3000.0 * i)
+    for i in range(2):
+        dma("YS"[i], "x%d" % i, T.xw[:, 2048 * i:2048 * i + 2048], T.x0[:, 2048 * i:2048 * i + 2048], [], [("xw", 2048 * i, 2048 * i + 2048)], 20000.0)
 
     iota("pI", 0, 1, [[0, 1]], 0, 1)
     iota("iw", 0, 256, [[1, 256]], 0, 0)
-    ne = send("z", T.zs[:], [T.zl[:, 240 * j:240 * j + 240] for j in range(3)], [("zs", 0, 240)], "az", "lz")
-    arrival("az", 3 * ne, [], [("zl", 0, 720)])
-    send("v", T.vs[:], [T.vl[:, 45 * j:45 * j + 45] for j in range(3)], [("vs", 0, 45)], "av", "lv")
-    arrival("av", 3 * ne, [], [("vl", 0, 135)])
+    ne = send(T.zs[:], [T.zl[:, 240 * j:240 * j + 240] for j in range(3)], [("zs", 0, 240)], [("zl", 0, 720)], "az", "lz")
+    send(T.vs[:], [T.vl[:, 45 * j:45 * j + 45] for j in range(3)], [("vs", 0, 45)], [("vl", 0, 135)], "av", "lv")
     iota("kc", 0, 128, [[0, 8], [-1, 16]], 15, 0)
     iota("rm", 0, 256, [[0, 16], [1, 16]], 0, 0)
-    iota("E", 0, 2048, [[1, 128], [0, 16]], 0, 0)
+    iota("E", 0, 1024, [[1, 64], [0, 16]], 0, 0)
 
     def col(i):
         return T.pF[:, i:i + 1]
@@ -225,6 +286,10 @@ def rank_program(g, core, T, topo):
     ts(col(7), [cR(7)], col(2), [cR(2)], 15.0, None, A.add)
     ts(col(8), [cR(8)], col(1), [cR(1)], 4096.0, None, A.mult)
     ts(T.idb[:], [("idb", 0, 128)], T.iw[:, 0:128], [("iw", 0, 128), cR(0)], col(0), None, A.is_equal)
+    ts(T.idf[:], [("idf", 0, 128)], T.iw[:, 0:128], [("iw", 0, 128), cR(0)], col(0), None, A.is_equal)
+    for s in range(S):
+        act(T.idS[:, 128 * s:128 * s + 128], [("idS", 128 * s, 128 * s + 128)], T.idb[:], [("idb", 0, 128)], ID, scale=1024.0 * (s + 1))
+    ts(T.idn[:], [("idn", 0, 128)], T.iw[:, 0:128], [("iw", 0, 128), cR(0)], col(0), -1.0, A.is_equal, A.mult)
     for h in range(2):
         for q in range(2):
             sc = {0: 0, 1: 5, -1: 6}[q - h]
@@ -233,47 +298,41 @@ def rank_program(g, core, T, topo):
             ts(T.Pm[:, o:o + 128], [("Pm", o, o + 128)], T.iw[:, 0:128], [("iw", 0, 128), cR(sc), cR(hc)], col(sc), col(hc), A.is_equal, A.mult)
     ts(T.U[:], [("U", 0, 144)], T.iw[:, 0:144], [("iw", 0, 144), cR(7)], col(7), 16.0, A.is_equal, A.mult)
     ts(T.rm[:], [("rm", 0, 256)], T.rm[:], [("rm", 0, 256)], 1.0, None, A.min)
-    ts(T.E[:], [("E", 0, 2048)], T.E[:], [("E", 0, 2048), cR(0)], col(0), None, A.is_equal)
-    ms("codeI", 0, 64, 0)
-    ms("vI0", 0, 80, 0)
-    ms("vI1", 0, 80, 0)
-    ms("vU0", 0, 80, 0)
-    ms("vU1", 0, 80, 0)
-    ms("zsT", 0, 64, 0.0)
-    ms("cntT", 0, 64, 0.0)
-    ms("kvf0", 0, 128, 0.0)
-    ms("kvf1", 0, 128, 0.0)
-    ms("own", 0, 48, 0.0)
-    op("V", lambda e: e.memset(T.thr[:], 12.0), [], [("thr", 0, 1)])
-
-    def late_constants():
-        iota("bs", 0, 64, [[4096, 4], [0, 16]], 4096, 0)
-        iota("Dm", 0, 64, [[0, 4], [16, 16]], 4096, 0)
-        ms("base", 0, 64, 2.0 ** 20)
-        for s in range(S):
-            iota("base", 16 * s, 16 * s + 15, [[4096, 3], [0, 5]], 16384 * (s + 1) + 4096, 0)
-        iota("iw", 256, 8192, [[1, 7936]], 256, 0)
-        cp(T.rmb[:], [("rmb", 0, 256)], T.rm[:], [("rm", 0, 256)])
-        ts(T.bo1[:], [("bo1", 0, 128)], T.iw[:, 0:128], [("iw", 0, 128), cR(2)], col(2), None, A.is_ge)
-        ts(T.bo2[:], [("bo2", 0, 128)], T.iw[:, 0:128], [("iw", 0, 128), cR(7)], col(7), None, A.is_le)
-        tt(T.BO[:], [("BO", 0, 128)], T.bo1[:], T.bo2[:], [("bo1", 0, 128), ("bo2", 0, 128)], A.mult)
-        for i in range(4):
-            ts(T.pI[:, 4 + i:5 + i], [("pI", 4 + i, 5 + i)], T.pI[:, 1:2], [("pI", 1, 2)], i, 1, A.arith_shift_right, A.bitwise_and)
-        for i in range(4):
-            ts(col(9 + i), [cR(9 + i)], T.pI[:, 4 + i:5 + i], [("pI", 4 + i, 5 + i)], 2.0 ** -(2 ** i) - 1.0, 1.0, A.mult, A.add)
-        tt(col(13), [cR(13)], col(9), col(10), [cR(9), cR(10)], A.mult)
-        tt(col(14), [cR(14)], col(11), col(12), [cR(11), cR(12)], A.mult)
-        tt(col(15), [cR(15)], col(13), col(14), [cR(13), cR(14)], A.mult)
-        ts(T.BW[:], [("BW", 0, 128)], T.BO[:], [("BO", 0, 128), cR(15)], col(15), 2.0 ** 60, A.mult, A.mult)
-        ts(T.dg[:], [("dg", 0, 16)], T.iw[:, 0:16], [("iw", 0, 16), cR(1), cR(15)], col(1), col(15), A.is_equal, A.mult)
-        for a in range(15):
-            e = (60 - 16 * a) // 2
-            ts(T.Wt[:, 128 * a:128 * a + 128], [("Wt", 128 * a, 128 * a + 128)], T.BW[:], [("BW", 0, 128)], 2.0 ** e, 2.0 ** e, A.mult, A.mult)
-            e = (120 - 16 * a) // 2
-            ts(T.W2d[:, 16 * a:16 * a + 16], [("W2d", 16 * a, 16 * a + 16)], T.dg[:], [("dg", 0, 16)], 2.0 ** e, 2.5 * 2.0 ** e, A.mult, A.mult)
-        ts(T.Wk[:], [("Wk", 0, 16)], T.iw[:, 0:16], [("iw", 0, 16), cR(1)], col(1), 1.0 / 32.0, A.is_equal, A.mult)
-        ts(T.Dm[:], [("Dm", 0, 64)], T.Dm[:], [("Dm", 0, 64), cR(1)], col(1), None, A.add)
-        ts(T.ln[:], [("ln", 0, 16)], T.Dm[:, 0:16], [("Dm", 0, 16)], -4096.0, None, A.add)
+    ts(T.E[:], [("E", 0, 1024)], T.E[:], [("E", 0, 1024), cR(0)], col(0), None, A.is_equal)
+    for name, n in (("codeI", 64), ("vI0", 80), ("vI1", 80), ("vU0", 80), ("vU1", 80), ("offU", 80)):
+        ms(name, 0, n, 0)
+    for name, n in (("zsT", 64), ("cntT", 64), ("kvf", 384), ("own", 48), ("zg", 2400), ("fo", 80)):
+        ms(name, 0, n, 0.0)
+    op("V", lambda e: e.memset(T.Y[:, 15, :], 0.0), [], [("Y", 3840, 4096)], 300.0)
+    ms("thr", 0, 1, 12.0)
+    ms("ones", 0, 128, 1.0)
+    iota("bs", 0, 64, [[4096, 4], [0, 16]], 4096, 0)
+    iota("Dm", 0, 64, [[0, 4], [16, 16]], 4096, 0)
+    ms("base", 0, 64, 2.0 ** 20)
+    for s in range(S):
+        iota("base", 16 * s, 16 * s + 15, [[4096, 3], [0, 5]], 16384 * (s + 1) + 4096, 0)
+    iota("iw", 256, 8192, [[1, 7936]], 256, 0)
+    cp(T.rmb[:], [("rmb", 0, 256)], T.rm[:], [("rm", 0, 256)])
+    ts(T.bo1[:], [("bo1", 0, 128)], T.iw[:, 0:128], [("iw", 0, 128), cR(2)], col(2), None, A.is_ge)
+    ts(T.BW[:], [("BW", 0, 128)], T.iw[:, 0:128], [("iw", 0, 128), cR(7)], col(7), None, A.is_le)
+    tt(T.BO[:], [("BO", 0, 128)], T.bo1[:], T.BW[:], [("bo1", 0, 128), ("BW", 0, 128)], A.mult)
+    for i in range(4):
+        ts(T.pI[:, 4 + i:5 + i], [("pI", 4 + i, 5 + i)], T.pI[:, 1:2], [("pI", 1, 2)], i, 1, A.arith_shift_right, A.bitwise_and)
+    for i in range(4):
+        ts(col(9 + i), [cR(9 + i)], T.pI[:, 4 + i:5 + i], [("pI", 4 + i, 5 + i)], 2.0 ** -(2 ** i) - 1.0, 1.0, A.mult, A.add)
+    tt(col(13), [cR(13)], col(9), col(10), [cR(9), cR(10)], A.mult)
+    tt(col(14), [cR(14)], col(11), col(12), [cR(11), cR(12)], A.mult)
+    tt(col(15), [cR(15)], col(13), col(14), [cR(13), cR(14)], A.mult)
+    ts(T.BW[:], [("BW", 0, 128)], T.BO[:], [("BO", 0, 128), cR(15)], col(15), 2.0 ** 60, A.mult, A.mult)
+    ts(T.dg[:], [("dg", 0, 16)], T.iw[:, 0:16], [("iw", 0, 16), cR(1), cR(15)], col(1), col(15), A.is_equal, A.mult)
+    for a in range(15):
+        e2 = (60 - 16 * a) // 2
+        ts(T.Wt[:, 128 * a:128 * a + 128], [("Wt", 128 * a, 128 * a + 128)], T.BW[:], [("BW", 0, 128)], 2.0 ** e2, 2.0 ** e2, A.mult, A.mult)
+        e2 = (120 - 16 * a) // 2
+        ts(T.W2d[:, 16 * a:16 * a + 16], [("W2d", 16 * a, 16 * a + 16)], T.dg[:], [("dg", 0, 16)], 2.0 ** e2, 2.5 * 2.0 ** e2, A.mult, A.mult)
+    ts(T.Wk[:], [("Wk", 0, 16)], T.iw[:, 0:16], [("iw", 0, 16), cR(1)], col(1), 1.0 / 32.0, A.is_equal, A.mult)
+    ts(T.Dm[:], [("Dm", 0, 64)], T.Dm[:], [("Dm", 0, 64), cR(1)], col(1), None, A.add)
+    ts(T.ln[:], [("ln", 0, 16)], T.Dm[:, 0:16], [("Dm", 0, 16)], -4096.0, None, A.add)
 
     def z_start(t):
         for j in range(3):
@@ -286,10 +345,6 @@ def rank_program(g, core, T, topo):
             cp(T[vI][:, 5 * j:5 * j + 5], [(vI, 5 * j, 5 * j + 5)], T.vl[:, o:o + 5], [("vl", 0, 135)])
         cp(T[vU][:, 0:15], [(vU, 0, 15)], T[vI][:, 0:15], [(vI, 0, 15)])
 
-    ms("zg", 0, 2400, 0.0)
-    ms("fo", 0, 80, 0.0)
-    op("V", lambda e: e.memset(T.ones[:], 1.0), [], [("ones", 0, 128)])
-    late_constants()
     v_start(0)
     z_start(0)
     for i in range(4):
@@ -298,154 +353,123 @@ def rank_program(g, core, T, topo):
 
     KW = ("kw", 0, V)
     XW = ("xw", 0, V)
-    a0s, a1s = (0, NA), (NA, 15)
 
     def knew(t, gr, s):
         vU = "vU%d" % (t % 2)
-        a0, a1 = a0s[gr], a1s[gr]
+        a0, a1 = GROUPS[gr][:2]
         lo, hi, o = 16 * a0, 16 * a1, 16 * (s - 1)
         ts(T.kvu[:, lo:hi], [("kvu", lo, hi)], T.kw[:, 0:V].indirect(T[vU][:, o + a0:o + a1]), [KW, (vU, o + a0, o + a1)], 1.0 / 32.0, None, A.mult)
 
-    def kact(t, gr, s):
+    def kpick(t, gr, s):
         vU = "vU%d" % (t % 2)
-        a0, a1 = a0s[gr], a1s[gr]
-        n, o, kvf = 16 * (a1 - a0), 16 * (s - 1), "kvf%d" % gr
-        act(T[kvf][:, 0:n], [(kvf, 0, n)], T.kw[:, 0:V].indirect(T[vU][:, o + a0:o + a1]), [KW, (vU, o + a0, o + a1), cR(8)], ID, bias=col(8), scale=1.0 / 32.0)
+        a0, a1 = GROUPS[gr][:2]
+        n, o, q = 16 * (a1 - a0), 16 * (s - 1), 128 * gr
+        nb = (n + 31) // 32
+        act(T.kvf[:, q:q + n], [("kvf", q, q + n)], T.kw[:, 0:V].indirect(T[vU][:, o + a0:o + a1]), [KW, (vU, o + a0, o + a1), cR(8)], ID, bias=col(8), scale=1.0 / 32.0)
+        op("V", lambda e: e.transpose(T.Tt[:, 4 * gr:4 * gr + nb, :], T.kvf[:, q:q + 32 * nb]), [("kvf", q, q + 32 * nb)], [("Tt", q, q + 32 * nb)], max(64, 32 * nb) * CYC)
+        pb = "pb%d" % gr
+        for b in range(0, nb, 2):
+            for h in range(2):
+                for w in range(2):
+                    p = 128 * (2 * h + w)
+                    mm(T[pb][:, 1:3, 16 * b + 16 * h:16 * b + 16 * h + 16], [(pb, 0, 512)], T.Pm[:, p:p + 128], T.Tt[:, 4 * gr + b:4 * gr + b + 2, 16 * w:16 * w + 16],
+                       [("Pm", p, p + 128), ("Tt", q, q + 32 * nb)], w == 0, w == 1, n=32)
 
-    def ktr(gr):
-        kvf, Tt = "kvf%d" % gr, "Tt%d" % gr
-        op("V", lambda e: e.transpose(T[Tt][:, :, :], T[kvf][:]), [(kvf, 0, 128)], [(Tt, 0, 128)])
-
-    def kswap(gr):
-        Tt, pk = "Tt%d" % gr, "pk%d" % gr
-        for h in range(2):
-            for q in range(2):
-                o = 128 * (2 * h + q)
-                mm(T[pk][:, 0:4, 16 * h:16 * h + 16], [(pk, 0, 512)], T.Pm[:, o:o + 128], T[Tt][:, :, 16 * q:16 * q + 16], [("Pm", o, o + 128), (Tt, 0, 128)], q == 0, q == 1)
-
-    def score(gr, al, ah, first, last):
-        pe, a0 = "pe%d" % gr, a0s[gr]
-        if first:
-            mm(T[pe][:, 0:128], [(pe, 0, 512)], T.idb[:], T.kc[:], [("idb", 0, 128), ("kc", 0, 128)], True, False)
+    def score(gr, al, ah):
+        pb = "pb%d" % gr
+        a0, a1 = GROUPS[gr][:2]
+        nb = (a1 - a0 + 1) // 2
+        if al == a0:
+            mm(T[pb][:, 0, 0:32 * nb], [(pb, 0, 512)], T.idb[:], T.kc[:, 0:32 * nb], [("idb", 0, 128), ("kc", 0, 32 * nb)], True, False)
+        end = ah + (ah - al) % 2
+        l, h = 16 * (al - a0), 16 * (end - a0)
         for c in range(16):
-            mm(T[pe][:, 16 * (al - a0):16 * (ah - a0)], [(pe, 0, 512)], T.U[:, 15 - c:143 - c], T.Y[:, al:ah, 16 * c:16 * c + 16],
-               [("U", 0, 144), ("Y", 256 * al, 256 * ah)], False, last and c == 15)
+            mm(T[pb][:, 0, l:h], [(pb, 0, 512)], T.U[:, 15 - c:143 - c], T.Y[:, al:end, 16 * c:16 * c + 16],
+               [("U", 0, 144), ("Y", 256 * al, 256 * end)], False, ah == a1 and c == 15, n=16 * (end - al))
 
-    def xgat(i):
-        xg = "xg%d" % (i % 2)
-        act(T[xg][:], [(xg, 0, 512)], T.xw[:, 0:V].indirect(T.kvu[:, 32 * i:32 * i + 32]), [XW, ("kvu", 32 * i, 32 * i + 32)])
+    chunk = [0]
 
-    def xsub(i):
-        xg, pa = "xg%d" % (i % 2), "pa%d" % (i % 2)
-        mm(T[pa][:, :, :], [(pa, 0, 512)], T.idb[:], T[xg][:], [("idb", 0, 128), (xg, 0, 512)], True, False)
-        mm(T[pa][:, :, :], [(pa, 0, 512)], T.zT[:], T.E[:, 512 * i:512 * i + 512], [("zT", 0, 128), ("E", 0, 2048)], False, True)
+    def xact(t, gr, s):
+        a0, a1 = GROUPS[gr][:2]
+        n, o = 16 * (a1 - a0), 480 * (s - 1) + 16 * a0
+        zT = "zT%d" % gr
+        mm(T.pz[0:n, 0:128], [("pz", 0, 512)], T.zg[:, o:o + n], T.idb[:], [("zg", o, o + n), ("idb", 0, 128)], True, True)
+        act(T[zT][0:n, :], [(zT, 0, 128)], T.pz[0:n, 0:128], [("pz", 0, 512)], ID, scale=-1.0)
+        for i in range((a1 - a0) // 2):
+            a = a0 + 2 * i
+            xg, pa = "xg%d" % (chunk[0] % NX), "pa%d" % (chunk[0] % 2)
+            chunk[0] += 1
+            act(T[xg][:], [(xg, 0, 512)], T.xw[:, 0:V].indirect(T.kvu[:, 16 * a:16 * a + 32]), [XW, ("kvu", 16 * a, 16 * a + 32)])
+            mm(T[pa][:, :, :], [(pa, 0, 512)], T.idb[:], T[xg][:], [("idb", 0, 128), (xg, 0, 512)], True, False)
+            mm(T[pa][:, :, :], [(pa, 0, 512)], T[zT][0:n, :], T.E[0:n, 512 * i:512 * i + 512], [(zT, 0, 128), ("E", 0, 1024)], False, True, n=512)
+            act(T.Y[:, a:a + 2, :], [("Y", 256 * a, 256 * a + 512)], T[pa][:, :, :], [(pa, 0, 512)], RELU)
+        score(gr, a0, a1)
 
-    def xrelu(i):
-        pa = "pa%d" % (i % 2)
-        act(T.Y[:, 2 * i:2 * i + 2, :], [("Y", 512 * i, 512 * i + 512)], T[pa][:, :, :], [(pa, 0, 512)], RELU)
-
-    def zt_mm(s):
-        o = 480 * (s - 1)
-        mm(T.pz[:, 0:128], [("pz", 0, 512)], T.zg[:, o:o + 128], T.idb[:], [("zg", o, o + 128), ("idb", 0, 128)], True, True)
-
-    def zt_act():
-        act(T.zT[:], [("zT", 0, 128)], T.pz[:, 0:128], [("pz", 0, 512)], ID, scale=-1.0)
-
-    def count_mm(s):
-        o = 480 * s
-        for c in range(16):
-            mm(T.pc[:, 0:30], [("pc", 0, 512)], T.U[:, 15 - c:143 - c], T.zg[:, o + c:o + 480:16], [("U", 0, 144), ("zg", o, o + 480)], c == 0, c == 15)
-
-    def count_act(s):
-        o = 16 * (s - 1)
-        act(T.zsT[:, o:o + 15], [("zsT", o, o + 15)], T.pc[:, 0:15], [("pc", 0, 512)], ID, scale=1.0 / 16.0)
-        act(T.cntT[:, o:o + 15], [("cntT", o, o + 15)], T.pc[:, 15:30], [("pc", 0, 512)], ID, scale=1.0 / 16.0)
-
-    def stretch(s):
+    def xvec(t, gr, s):
+        a0, a1 = GROUPS[gr][:2]
         o = 480 * (s - 1)
         for k in range(16):
-            op("V", lambda e: e.tensor_copy(T.zx[:, k::16], T.zg[:, o + 16 * NA:o + 240]), [("zg", o + 16 * NA, o + 240)], [("zx", 0, ND * 256)], waw=False)
+            cp(T.zx[:, k:256 * (a1 - a0):16], [("zxv", k, k + 1)], T.zg[:, o + 16 * a0:o + 16 * a1], [("zg", o + 16 * a0, o + 16 * a1)])
+        for a in range(a0, a1):
+            r = 256 * (a - a0)
+            tt(T.Y[:, a, :], [("Y", 256 * a, 256 * a + 256)], T.xw[:, 0:V].indirect(T.kvu[:, 16 * a:16 * a + 16]), T.zx[:, r:r + 256],
+               [XW, ("kvu", 16 * a, 16 * a + 16), ("zxv", 0, 16)], A.max)
+        score(gr, a0, a0 + 4)
+        score(gr, a0 + 4, a1)
 
-    def xmax(a):
-        r = 256 * (a - NA)
-        tt(T.Y[:, a, :], [("Y", 256 * a, 256 * a + 256)], T.xw[:, 0:V].indirect(T.kvu[:, 16 * a:16 * a + 16]), T.zx[:, r:r + 256],
-           [XW, ("kvu", 16 * a, 16 * a + 16), ("zx", r, r + 256)], A.max)
+    def count(s):
+        o, q = 480 * s, 16 * (s - 1)
+        for c in range(16):
+            mm(T.pc[:, 0:30], [("pc", 0, 512)], T.U[:, 15 - c:143 - c], T.zg[:, o + c:o + 480:16], [("U", 0, 144), ("zg", o, o + 480)], c == 0, c == 15, n=30)
+        act(T.zsT[:, q:q + 15], [("zsT", q, q + 15)], T.pc[:, 0:15], [("pc", 0, 512)], ID, scale=1.0 / 16.0)
+        act(T.cntT[:, q:q + 15], [("cntT", q, q + 15)], T.pc[:, 15:30], [("pc", 0, 512)], ID, bias=8.0, scale=1.0 / 32.0)
 
     def pick(t, gr, s):
         vI, vU = "vI%d" % (t % 2), "vU%d" % (t % 2)
-        a0, a1, o = a0s[gr], a1s[gr], 16 * s
-        pe, pk, R, eq, pr, C = ["%s%d" % (x, gr) for x in ("pe", "pk", "R", "eq", "pr", "C")]
-        op("V", lambda e: e.tensor_tensor_scan(T[R][:], T.rm[:, 0:128], T[pe][:, 0:128], 0.0, A.mult, A.max), [("rm", 0, 128), (pe, 0, 512)], [(R, 0, 128)])
-        tt(T[eq][:], [(eq, 0, 128)], T[R][:], T[pe][:, 0:128], [(R, 0, 128), (pe, 0, 512)], A.is_equal)
-        tt(T[pr][:], [(pr, 0, 128)], T[eq][:], T[pk][:, 0:4, :], [(eq, 0, 128), (pk, 0, 512)], A.mult)
-        op("V", lambda e: e.tensor_tensor_scan(T[C][:], T.rm[:, 0:128], T[pr][:], 0.0, A.mult, A.max), [("rm", 0, 128), (pr, 0, 128)], [(C, 0, 128)])
-        cp(T.codeI[:, o - 16 + a0:o - 16 + a1], [("codeI", o - 16 + a0, o - 16 + a1)], T[C][:, 15:16 * (a1 - a0):16], [(C, 0, 128)])
-        ts(T[vI][:, o + a0:o + a1], [(vI, o + a0, o + a1)], T.codeI[:, o - 16 + a0:o - 16 + a1], [("codeI", o - 16 + a0, o - 16 + a1)], 4095, None, A.bitwise_and)
+        a0, a1 = GROUPS[gr][:2]
+        nb = (a1 - a0 + 1) // 2
+        o, q, n, pb = 16 * s, 128 * gr, 32 * nb, "pb%d" % gr
+
+        def r(x):
+            return (x, q, q + n)
+        scan(T.R[:, q:q + n], [r("R")], T.rm[:, 0:n], T[pb][:, 0, 0:n], [("rm", 0, n), (pb, 0, 512)], A.mult, A.max)
+        tt(T.eq[:, q:q + n], [r("eq")], T.R[:, q:q + n], T[pb][:, 0, 0:n], [r("R"), (pb, 0, 512)], A.is_equal)
+        for b in range(0, nb, 2):
+            p = q + 32 * b
+            tt(T.pr[:, p:p + 64], [("pr", p, p + 64)], T.eq[:, p:p + 64], T[pb][:, 1:3, 16 * b:16 * b + 32], [("eq", p, p + 64), (pb, 0, 512)], A.mult)
+        scan(T.C[:, q:q + n], [r("C")], T.rm[:, 0:n], T.pr[:, q:q + n], [("rm", 0, n), r("pr")], A.mult, A.max)
+        cI = ("codeI", o - 16 + a0, o - 16 + a1)
+        cp(T.codeI[:, o - 16 + a0:o - 16 + a1], [cI], T.C[:, q + 15:q + 16 * (a1 - a0):16], [r("C")])
+        ts(T[vI][:, o + a0:o + a1], [(vI, o + a0, o + a1)], T.codeI[:, o - 16 + a0:o - 16 + a1], [cI], 4095, None, A.bitwise_and)
         cp(T[vU][:, o + a0:o + a1], [(vU, o + a0, o + a1)], T[vI][:, o + a0:o + a1], [(vI, o + a0, o + a1)])
 
     def zstep(t, gr, s):
         vU = "vU%d" % (t % 2)
-        a0, a1 = a0s[gr], a1s[gr]
-        lo, hi, n, o = 16 * a0, 16 * a1, 16 * (a1 - a0), 480 * (s - 1)
-        sh = th = "sh%d" % gr
+        a0, a1 = GROUPS[gr][:2]
+        lo, hi, n, o, q = 16 * a0, 16 * a1, 16 * (a1 - a0), 480 * (s - 1), 128 * gr
         lst = T.xw[:, 0:V].indirect(T[vU][:, 16 * s + a0:16 * s + a1])
-        rd = [XW, (vU, 16 * s + a0, 16 * s + a1), ("zg", o + lo, o + hi)]
-        zp = T.zg[:, o + lo:o + hi]
-        tt(T[sh][:, 0:n], [(sh, 0, n)], lst, zp, rd, A.add)
-        tt(T.zg[:, o + 720 + lo:o + 720 + hi], [("zg", o + 720 + lo, o + 720 + hi)], lst, zp, rd, A.is_gt)
-        ts(T[th][:, 0:n], [(th, 0, n)], T[sh][:, 0:n], [(sh, 0, n)], 0.5, 1023.75, A.mult, A.add)
-        ts(T.zg[:, o + 480 + lo:o + 480 + hi], [("zg", o + 480 + lo, o + 480 + hi)], T[th][:, 0:n], [(th, 0, n)], -1024.0, None, A.add)
+        RD = [XW, (vU, 16 * s + a0, 16 * s + a1)]
+        zp, ZP, SH, XQ = T.zg[:, o + lo:o + hi], ("zg", o + lo, o + hi), ("sh", q, q + n), ("xq", q, q + n)
+        tt(T.sh[:, q:q + n], [SH], lst, zp, RD + [ZP], A.add)
+        ts(T.sh[:, q:q + n], [SH], T.sh[:, q:q + n], [SH], 0.5, 1023.75, A.mult, A.add)
+        ts(T.zg[:, o + 480 + lo:o + 480 + hi], [("zg", o + 480 + lo, o + 480 + hi)], T.sh[:, q:q + n], [SH], -1024.0, None, A.add)
+        act(T.xq[:, q:q + n], [XQ], lst, RD)
+        mm(T.ps[:, 0:n], [("ps", 0, 512)], T.idb[:], T.xq[:, q:q + n], [("idb", 0, 128), XQ], True, False)
+        mm(T.ps[:, 0:n], [("ps", 0, 512)], T.idn[:], zp, [("idn", 0, 128), ZP], False, True)
+        op("S", lambda e: e.activation(T.zg[:, o + 720 + lo:o + 720 + hi], T.ps[:, 0:n], SIGN, bias=-0.5), [("ps", 0, 512)], [("zg", o + 720 + lo, o + 720 + hi)], n * CYC)
 
     def race(t):
-        vI, vU = "vI%d" % (t % 2), "vU%d" % (t % 2)
-        for gr in range(2):
-            knew(t, gr, 1)
-            kact(t, gr, 1)
-        ktr(0)
         for s in range(1, S + 1):
-            zt_mm(s)
-            kswap(0)
-            xgat(0)
-            zt_act()
-            stretch(s)
-            xgat(1)
-            for a in range(NA, NA + 4):
-                xmax(a)
-            xsub(0)
-            xrelu(0)
-            xsub(1)
-            score(1, NA, NA + 4, True, False)
-            if s > 1:
-                count_mm(s - 1)
-                kact(t, 1, s)
-            xgat(2)
-            xrelu(1)
-            for a in range(NA + 4, 15):
-                xmax(a)
-            ktr(1)
-            xsub(2)
-            score(0, 0, 4, True, False)
-            xgat(3)
-            xrelu(2)
-            xsub(3)
-            xrelu(3)
-            if s > 1:
-                count_act(s - 1)
-            score(1, NA + 4, 15, False, True)
-            kswap(1)
-            score(0, 4, 8, False, True)
-            for gr in range(2):
+            for gr in range(len(GROUPS)):
+                bias[0] = BIAS[gr]
+                knew(t, gr, s)
+                kpick(t, gr, s)
+                (xact if GROUPS[gr][2] else xvec)(t, gr, s)
                 pick(t, gr, s)
-                if s < S:
-                    knew(t, gr, s + 1)
-                    if gr == 0:
-                        kact(t, gr, s + 1)
                 zstep(t, gr, s)
-                if s < S and gr == 0:
-                    ktr(0)
-        count_mm(S)
-        count_act(S)
-        finish(t, vI, vU)
+            bias[0] = 0.0
+            count(s)
+        finish(t, "vI%d" % (t % 2), "vU%d" % (t % 2))
 
     def finish(t, vI, vU):
         f64, f16 = (0, 64), (0, 16)
@@ -460,13 +484,12 @@ def rank_program(g, core, T, topo):
         own = T.own[:, oo:oo + 16]
         tt(own, [OW], T.m1[:, 0:16], T.m1[:, 16:32], [("m1", 0, 32)], A.min)
         rs = 48 * t
-        ne = send("w", own, [T.rcv[:, rs + 16 * j:rs + 16 * j + 16] for j in range(3)], [OW], "a%d" % t, "l%d" % t)
-        arrival("a%d" % t, 3 * ne, [], [("rcv", rs, rs + 48)])
+        send(own, [T.rcv[:, rs + 16 * j:rs + 16 * j + 16] for j in range(3)], [OW], [("rcv", rs, rs + 48)], "a%d" % t, "l%d" % t)
         ts(T.nb[:], [("nb",) + f64], T.cntT[:], [("cntT",) + f64, ("thr", 0, 1)], T.thr[:], BIG, A.is_lt, A.mult)
         tt(T.d1[:], [("d1",) + f64], T[vI][:, 16:80], T.bs[:], [(vI, 16, 80), ("bs",) + f64], A.add)
         tt(T.d1[:], [("d1",) + f64], T.d1[:], T.nb[:], [("d1",) + f64, ("nb",) + f64], A.add)
-        tt(T.m2[:], [("m2", 0, 32)], T.d1[:, 0:32], T.d1[:, 32:64], [("d1",) + f64], A.min)
-        tt(T.dI[:], [("dI",) + f16], T.m2[:, 0:16], T.m2[:, 16:32], [("m2", 0, 32)], A.min)
+        tt(T.c1[:, 0:32], [("c1", 0, 32)], T.d1[:, 0:32], T.d1[:, 32:64], [("d1",) + f64], A.min)
+        tt(T.dI[:], [("dI",) + f16], T.c1[:, 0:16], T.c1[:, 16:32], [("c1", 0, 32)], A.min)
         ts(T.WI[:], [("WI",) + f16], T.dI[:], [("dI",) + f16], 4095, None, A.bitwise_and)
         ts(T.bI[:], [("bI",) + f16], T.dI[:], [("dI",) + f16], 12, 7, A.arith_shift_right, A.bitwise_and)
         ts(T.kI[:], [("kI",) + f64], T.codeI[:], [("codeI",) + f64], 12, None, A.arith_shift_right)
@@ -481,9 +504,8 @@ def rank_program(g, core, T, topo):
         tt(T.vD[:, 64:80], [("vD", 64, 80)], T.WI[:], T.Dm[:, 0:16], [("WI",) + f16, ("Dm", 0, 16)], A.subtract)
         act(T.xW[:], [("xW", 0, 240)], T.xw[:, 0:V].indirect(T.WU[:, 0:15]), [XW, ("WU",) + f16])
         for s in range(S, 0, -1):
-            act(T.Bs[:, 240 * s - 240:240 * s], [("Bs", 240 * s - 240, 240 * s)], T.Wk[:].indirect(T.kU[:, 16 * s - 16:16 * s - 1]),
-                [("Wk",) + f16, ("kU",) + f64], ID, bias=-131072.0, scale=1024.0 * s)
-        for s in range(2, S + 1):
+            act(T.Bs[:, 240 * s - 240:240 * s], [("Bs", 240 * s - 240, 240 * s)], T.Wk[:].indirect(T.kU[:, 16 * s - 16:16 * s - 1]), [("Wk",) + f16, ("kU",) + f64])
+        for s in [x for x in range(S, 1, -1) if x not in ACT_EVENTS]:
             cp(T.vall[:, 240 * s - 240:240 * s], [("vall", 240 * s - 240, 240 * s)], T.iw[:].indirect(T[vU][:, 16 * s - 16:16 * s - 1]), [("iw", 0, 8192), (vU, 16 * s - 16, 16 * s)])
         tt(T.xs2[:], [("xs2", 0, 240)], T.zg[:].indirect(T.bU[:, 0:15]), T.xW[:], [("zg", 0, 2400), ("bU",) + f16, ("xW", 0, 240)], A.add)
         ts(T.xt2[:], [("xt2", 0, 240)], T.xs2[:], [("xs2", 0, 240)], 0.5, 1023.75, A.mult, A.add)
@@ -491,6 +513,7 @@ def rank_program(g, core, T, topo):
         if t + 1 < RACES:
             v_start(t + 1)
             z_start(t + 1)
+
         def rc(j, lo, hi):
             o = rs + 16 * (j - 1)
             return T.rcv[:, o + lo:o + hi]
@@ -515,54 +538,74 @@ def rank_program(g, core, T, topo):
         tt(T.kk[:], [("kk",) + f64], T.P1[:], T.on[:], [("P1",) + f64, ("on",) + f64], A.mult)
         tt(T.kk[:, 0:16], [("kk", 0, 16)], T.kk[:, 0:16], T.kt1[:], [("kk", 0, 16), ("kt1",) + f16], A.add)
         ts(T.key[:], [("key",) + f64], T.kk[:], [("kk",) + f64], -1.0, None, A.add)
+        ts(T.nkey[:], [("nkey",) + f64], T.kk[:], [("kk",) + f64], -1.0, 1.0, A.mult, A.add)
         cp(T.keyU[:], [("keyU",) + f16], T.key[:, 0:16], [("key", 0, 16)])
         cp(T.wonb[:], [("wonb",) + f16], T.won[:], [("won",) + f16])
-        cp(T.vall[:, 0:240], [("vall", 0, 240)], T.iw[:].indirect(T.keyU[:, 0:15]), [("iw", 0, 8192), ("keyU",) + f16])
-        bank = {4: "pe0", 3: "pe1", 2: "pa0", 1: "pz"}
+        if 1 not in ACT_EVENTS:
+            cp(T.vall[:, 0:240], [("vall", 0, 240)], T.iw[:].indirect(T.keyU[:, 0:15]), [("iw", 0, 8192), ("keyU",) + f16])
+        mm(T.pc[:, 480:495], [("pc", 0, 512)], T.ones[:], T.wonb[:, 0:15], [("ones", 0, 128), ("wonb",) + f16], True, True)
+        if t + 1 < RACES:
+            op("V", lambda e: e.tensor_reduce(T.tot[:], T.pc[:, 480:495], AxisListType.X, A.add), [("pc", 0, 512)], [("tot", 0, 1)], 64 * CYC)
+            cp(T.totI[:], [("totI", 0, 1)], T.tot[:], [("tot", 0, 1)])
+            ts(T.totI[:], [("totI", 0, 1)], T.totI[:], [("totI", 0, 1)], 1, None, A.bitwise_and)
+            ts(T.thr[:], [("thr", 0, 1)], T.totI[:], [("totI", 0, 1)], 12.0, None, A.add)
+        bank = {4: "ps", 3: "pa1", 2: "pa0", 1: "pz"}
 
         def flat(b, lo, hi):
-            return T[b][:, 0, lo:hi] if b == "pa0" else T[b][:, lo:hi]
-        for s in range(S, 0, -1):
+            return T[b][:, 0, lo:hi] if b[:2] == "pa" else T[b][:, lo:hi]
+
+        def event(s):
+            o, r, k0 = 1920 * (s - 1), 240 * s - 240, 16 * s - 16
+            on_act = s in ACT_EVENTS
+            if on_act:
+                lst, src = (T.keyU[:, 0:15], ("keyU",) + f16) if s == 1 else (T[vU][:, k0:k0 + 15], (vU, k0, k0 + 16))
+                act(T.valf[:], [("valf", 0, 240)], T.iw[:].indirect(lst), [("iw", 0, 8192), src])
+            for a in range(15):
+                n = 240 - 16 * a
+                if on_act:
+                    act(T.eqm[:, o:o + n], [("eqm", o, o + n)], T.valf[:, 240 - n:240], [("valf", 0, 240), ("nkey", k0, k0 + 16)], ABS, bias=T.nkey[:, k0 + a:k0 + a + 1])
+                    if a in (7, 14):
+                        e0 = 1920 * (s - 1) + (0 if a == 7 else 1472)
+                        act(T.eqm[:, e0:o + n], [("eqm", e0, o + n)], T.eqm[:, e0:o + n], [("eqm", e0, o + n)], RELU, bias=1.0, scale=-1.0)
+                else:
+                    ts(T.eqm[:, o:o + n], [("eqm", o, o + n)], T.vall[:, r + 240 - n:r + 240], [("vall", r + 240 - n, r + 240), ("key", k0, k0 + 16)],
+                       T.key[:, k0 + a:k0 + a + 1], None, A.is_equal)
+                o += n
             o = 1920 * (s - 1)
             for a in range(15):
                 n = 240 - 16 * a
-                ts(T.eqm[:, o:o + n], [("eqm", o, o + n)], T.vall[:, 240 * s - n:240 * s], [("vall", 240 * s - n, 240 * s), ("key",) + f64],
-                   T.key[:, 16 * s - 16 + a:16 * s - 15 + a], None, A.is_equal)
                 mm(flat(bank[s], 16 * a, 240), [(bank[s], 0, 512)], T.Wt[:, 128 * a:128 * a + 128], T.eqm[:, o:o + n], [("Wt", 0, 1920), ("eqm", o, o + n)], a == 0, a == 14)
                 o += n
-            if s == S:
-                cp(T.urep[:], [("urep", 0, 240)], T.iw[:].indirect(T.uwU[:, 0:15]), [("iw", 0, 8192), ("uwU",) + f16])
-            r = 240 * s - 240
-            tt(T.xs[:, r:r + 240], [("xs", r, r + 240)], T.Wk[:].indirect(T.kU[:, 16 * s - 16:16 * s - 1]), T.urep[:], [("Wk",) + f16, ("kU",) + f64, ("urep", 0, 240)], A.mult)
-        mm(T.pc[:, 0:15], [("pc", 0, 512)], T.ones[:], T.wonb[:, 0:15], [("ones", 0, 128), ("wonb",) + f16], True, True)
+            tt(T.fl[:, r:r + 240], [("fl", r, r + 240)], flat(bank[s], 0, 240), T.W2d[:], [(bank[s], 0, 512), ("W2d", 0, 240)], A.is_lt)
+            scan(T.Fs[:, r:r + 240], [("Fs", r, r + 240)], T.rmb[:, 0:240], T.fl[:, r:r + 240], [("rmb", 0, 240), ("fl", r, r + 240)], A.mult, A.add)
+
+            def place(k, on, ON):
+                fo, of = T.fo[:, k:k + 15], T.of[:, k:k + 15]
+                tt(fo, [("fo", k, k + 15)], T.Fs[:, r + 15:r + 240:16], on, [("Fs", r, r + 240), ON], A.mult)
+                tt(of, [("of", k, k + 15)], fo, T.vD[:, k:k + 15], [("fo", k, k + 15), ("vD", k, k + 15)], A.mult)
+                tt(of, [("of", k, k + 15)], of, T.Dm[:, 0:15], [("of", k, k + 15), ("Dm", 0, 15)], A.add)
+                cp(T.offU[:, k:k + 15], [("offU", k, k + 15)], of, [("of", k, k + 15)])
+            place(k0, T.on[:, k0:k0 + 15], ("on", k0, k0 + 15))
+            if s == 1:
+                place(64, T.won[:, 0:15], ("won",) + f16)
+
+        cp(T.urep[:], [("urep", 0, 240)], T.iw[:].indirect(T.uwU[:, 0:15]), [("iw", 0, 8192), ("uwU",) + f16])
         for s in range(S, 0, -1):
             r = 240 * s - 240
-            tt(T.fl[:], [("fl", 0, 240)], flat(bank[s], 0, 240), T.W2d[:], [(bank[s], 0, 512), ("W2d", 0, 240)], A.is_lt)
-            op("V", lambda e: e.tensor_tensor_scan(T.Fs[:, r:r + 240], T.rmb[:, 0:240], T.fl[:], 0.0, A.mult, A.add), [("rmb", 0, 240), ("fl", 0, 240)], [("Fs", r, r + 240)])
-        fs = T.Fs[:, 15:960:16]
-        for s in range(1, S + 1):
-            o = 16 * s - 16
-            tt(T.fo[:, o:o + 15], [("fo", o, o + 15)], T.Fs[:, 15 * o + 15:15 * o + 240:16], T.on[:, o:o + 15], [("Fs", 15 * o, 15 * o + 240), ("on",) + f64], A.mult)
-        tt(T.fo[:, 64:79], [("fo", 64, 79)], T.Fs[:, 15:240:16], T.won[:, 0:15], [("Fs", 0, 240), ("won",) + f16], A.mult)
-        tt(T.of[:], [("of", 0, 80)], T.fo[:], T.vD[:], [("fo", 0, 80), ("vD", 0, 80)], A.mult)
-        tt(T.of[:, 0:64], [("of", 0, 64)], T.of[:, 0:64], T.Dm[:], [("of", 0, 64), ("Dm",) + f64], A.add)
-        tt(T.of[:, 64:80], [("of", 64, 80)], T.of[:, 64:80], T.Dm[:, 0:16], [("of", 64, 80), ("Dm", 0, 16)], A.add)
-        cp(T.offU[:], [("offU", 0, 80)], T.of[:], [("of", 0, 80)])
-        cp(T.xw[:].indirect(T.offU[:, 64:79]), [("xw", 0, WIN)], T.xn[:], [("xn", 0, 240), ("offU", 0, 80)])
+            tt(T.xs[:, r:r + 240], [("xs", r, r + 240)], T.Wk[:].indirect(T.kU[:, 16 * s - 16:16 * s - 1]), T.urep[:], [("Wk",) + f16, ("kU",) + f64, ("urep", 0, 240)], A.mult)
+            event(s)
+        cp(T.xw[:].indirect(T.offU[:, 64:79]), [("xw", 0, WIN)], T.xn[:], [("xn", 0, 240), ("offU", 64, 80)])
         for s in range(S, 0, -1):
             r = 240 * s - 240
             lst = T.kw[:, 0:V].indirect(T[vU][:, 16 * s - 16:16 * s - 1])
             RD = [KW, (vU, 16 * s - 16, 16 * s)]
+            mm(T.pc[:, 0:240], [("pc", 0, 512)], T.idS[:, 128 * s - 128:128 * s], T.Bs[:, r:r + 240], [("idS", 0, 512), ("Bs", r, r + 240)], True, False)
+            act(T.kt[:], [("kt", 0, 240)], lst, RD, ID, bias=-131072.0)
+            mm(T.pc[:, 0:240], [("pc", 0, 512)], T.idf[:], T.kt[:], [("idf", 0, 128), ("kt", 0, 240)], False, True)
             tt(T.kp[:], [("kp", 0, 240)], lst, T.xs[:, r:r + 240], RD + [("xs", r, r + 240)], A.mult)
-            tt(T.kt[:], [("kt", 0, 240)], lst, T.Bs[:, r:r + 240], RD + [("Bs", r, r + 240)], A.add)
-            tt(T.kz[:], [("kz", 0, 240)], T.kp[:], T.kt[:], [("kp", 0, 240), ("kt", 0, 240)], A.add)
+            tt(T.kz[:], [("kz", 0, 240)], T.kp[:], T.pc[:, 0:240], [("kp", 0, 240), ("pc", 0, 512)], A.add)
             ts(T.kn[:], [("kn", 0, 240)], T.kz[:], [("kz", 0, 240)], 131040, None, A.bitwise_and)
-            cp(T.kw[:].indirect(T.offU[:, 16 * s - 16:16 * s - 1]), [("kw", 0, WIN)], T.kn[:], [("kn", 0, 240), ("offU", 0, 80)])
-        if t + 1 < RACES:
-            op("V", lambda e: e.tensor_reduce(T.tot[:], T.pc[:, 0:15], AxisListType.X, A.add), [("pc", 0, 512)], [("tot", 0, 1)])
-            cp(T.totI[:], [("totI", 0, 1)], T.tot[:], [("tot", 0, 1)])
-            ts(T.totI[:], [("totI", 0, 1)], T.totI[:], [("totI", 0, 1)], 1, None, A.bitwise_and)
-            ts(T.thr[:], [("thr", 0, 1)], T.totI[:], [("totI", 0, 1)], 12.0, None, A.add)
+            cp(T.kw[:].indirect(T.offU[:, 16 * s - 16:16 * s - 1]), [("kw", 0, WIN)], T.kn[:], [("kn", 0, 240), ("offU", 16 * s - 16, 16 * s - 1)])
 
     for t in range(RACES):
         race(t)
@@ -571,26 +614,23 @@ def rank_program(g, core, T, topo):
     for a in range(4):
         act(T.idk[:, 128 * a:128 * a + 128], [("idk", 128 * a, 128 * a + 128)], T.idb[:], [("idb", 0, 128)], ID, scale=(a + 1) / 32.0)
     for a in range(8):
-        mm(T.pe0[:], [("pe0", 0, 512)], T.idx[:, 128 * a:128 * a + 128], T.xw[:, 512 * a:512 * a + 512], [("idx", 0, 1024), ("xw", 512 * a, 512 * a + 512)], a == 0, a == 7)
-    act(T.ox[:], [("ox", 0, 512)], T.pe0[:], [("pe0", 0, 512)])
-    dma("Y", "oy", T.yx[:], T.ox[:], [("ox", 0, 512)], [])
+        mm(T.ps[:], [("ps", 0, 512)], T.idx[:, 128 * a:128 * a + 128], T.xw[:, 512 * a:512 * a + 512], [("idx", 0, 1024), ("xw", 512 * a, 512 * a + 512)], a == 0, a == 7)
+    act(T.ox[:], [("ox", 0, 512)], T.ps[:], [("ps", 0, 512)])
+    dma("Y", "oy", T.yx[:], T.ox[:], [("ox", 0, 512)], [], 2000.0)
     for a in range(4):
-        mm(T.pe1[:], [("pe1", 0, 512)], T.idk[:, 128 * a:128 * a + 128], T.kw[:, 512 * a:512 * a + 512], [("idk", 0, 512), ("kw", 512 * a, 512 * a + 512)], a == 0, a == 3)
-    pb = {4: "pk0", 5: "pk1", 6: "pz", 7: "pc"}
+        mm(T.pz[:], [("pz", 0, 512)], T.idk[:, 128 * a:128 * a + 128], T.kw[:, 512 * a:512 * a + 512], [("idk", 0, 512), ("kw", 512 * a, 512 * a + 512)], a == 0, a == 3)
     for a in range(4, 8):
-        out = T[pb[a]][:, :, :] if a < 6 else T[pb[a]][:]
-        act(out, [(pb[a], 0, 512)], T.kw[:, 512 * a:512 * a + 512], [("kw", 512 * a, 512 * a + 512)], ID, scale=(a + 1) / 32.0)
-    cp(T.ok[:], [("ok", 0, 512)], T.pk0[:, :, :], [("pk0", 0, 512)])
-    tt(T.ok[:], [("ok", 0, 512)], T.ok[:], T.pk1[:, :, :], [("ok", 0, 512), ("pk1", 0, 512)], A.add)
-    for b in ("pz", "pc", "pe1"):
-        tt(T.ok[:], [("ok", 0, 512)], T.ok[:], T[b][:], [("ok", 0, 512), (b, 0, 512)], A.add)
-    dma("Y", "ok", T.yk[:], T.ok[:], [("ok", 0, 512)], [])
+        b = "pb%d" % (a - 4) if a < 7 else "pc"
+        act(T[b][:, :, :] if a < 7 else T[b][:], [(b, 0, 512)], T.kw[:, 512 * a:512 * a + 512], [("kw", 512 * a, 512 * a + 512)], ID, scale=(a + 1) / 32.0)
+    OK = ("ok", 0, 512)
+    cp(T.ok[:], [OK], T.pb0[:, :, :], [("pb0", 0, 512)])
+    for b in ("pb1", "pb2", "pc", "pz"):
+        tt(T.ok[:], [OK], T.ok[:], T[b][:, :, :] if b[1] == "b" else T[b][:], [OK, (b, 0, 512)], A.add)
+    dma("Y", "ok", T.yk[:], T.ok[:], [OK], [], 2000.0)
+    cnt = emit()
     g.sync.wait_ge(T.sem.oy, 16)
     g.sync.wait_ge(T.sem.ok, 16)
     for q in "VSTG":
         g.wait_ge(T.sem["q" + q], cnt[q])
     for l in ("lz", "lv", "l0", "l1", "l2"):
         g.wait_ge(T.sem[l], ne)
-
-
-SCRATCH["ones"] = ("sbuf", [128, 128], "bfloat16")

@@ -9,7 +9,7 @@ SIGN = ActivationFunctionType.Sign
 N, M, J, RACES, S, V = 4, 80, 3, 3, 4, 4096
 L = J * M
 GROUPS = ((0, 4, True), (4, 8, True), (8, 15, False))
-BIAS = (4000.0, 1000.0, 1500.0)
+BIAS = ((5400.0, 2700.0, 1700.0, 2200.0, 2200.0), (400.0, 8000.0, 1300.0, 2000.0, 1400.0), (3100.0, 2500.0, 1300.0, 4300.0, -1500.0), (1200.0, 4100.0, 1800.0, 6100.0, -2100.0))
 ND = 7
 NX = 3
 ACT_EVENTS = (1,)
@@ -21,7 +21,7 @@ SCRATCH = {}
 for _n, _w, _d in (
         ("xw", WIN, "bfloat16"), ("kw", WIN, "float32"), ("kin", V, "int32"), ("iw", 8192, "float32"), ("zx", ND * 256, "bfloat16"),
         ("kvu", 256, "uint16"), ("kvf", 384, "float32"), ("sh", 384, "float16"), ("xq", 384, "bfloat16"), ("R", 384, "float32"),
-        ("eq", 384, "float32"), ("pr", 384, "float32"), ("C", 384, "float32"), ("zT0", 128, "bfloat16"), ("zT1", 128, "bfloat16"),
+        ("eq", 384, "float32"), ("ne", 384, "float32"), ("pr", 384, "float32"), ("C", 384, "float32"), ("zT0", 128, "bfloat16"), ("zT1", 128, "bfloat16"),
         ("E", 1024, "bfloat16"), ("xg0", 512, "bfloat16"), ("xg1", 512, "bfloat16"), ("xg2", 512, "bfloat16"), ("zg", 2400, "bfloat16"),
         ("codeI", 64, "int32"), ("vI0", 80, "int32"), ("vI1", 80, "int32"), ("vU0", 80, "uint16"), ("vU1", 80, "uint16"),
         ("kI", 64, "int32"), ("kU", 64, "uint16"), ("zsT", 64, "float32"), ("cntT", 64, "float32"), ("wz", 64, "int32"),
@@ -284,7 +284,6 @@ def rank_program(g, core, T, topo):
     ts(col(5), [cR(5)], col(0), [cR(0)], 16.0, None, A.add)
     ts(col(6), [cR(6)], col(0), [cR(0)], -16.0, None, A.add)
     ts(col(7), [cR(7)], col(2), [cR(2)], 15.0, None, A.add)
-    ts(col(8), [cR(8)], col(1), [cR(1)], 4096.0, None, A.mult)
     ts(T.idb[:], [("idb", 0, 128)], T.iw[:, 0:128], [("iw", 0, 128), cR(0)], col(0), None, A.is_equal)
     ts(T.idf[:], [("idf", 0, 128)], T.iw[:, 0:128], [("iw", 0, 128), cR(0)], col(0), None, A.is_equal)
     for s in range(S):
@@ -305,6 +304,7 @@ def rank_program(g, core, T, topo):
         ms(name, 0, n, 0.0)
     op("V", lambda e: e.memset(T.Y[:, 15, :], 0.0), [], [("Y", 3840, 4096)], 300.0)
     ms("thr", 0, 1, 12.0)
+    ms("Wm", 0, 16, 2.0 ** 20)
     ms("ones", 0, 128, 1.0)
     iota("bs", 0, 64, [[4096, 4], [0, 16]], 4096, 0)
     iota("Dm", 0, 64, [[0, 4], [16, 16]], 4096, 0)
@@ -365,7 +365,7 @@ def rank_program(g, core, T, topo):
         a0, a1 = GROUPS[gr][:2]
         n, o, q = 16 * (a1 - a0), 16 * (s - 1), 128 * gr
         nb = (n + 31) // 32
-        act(T.kvf[:, q:q + n], [("kvf", q, q + n)], T.kw[:, 0:V].indirect(T[vU][:, o + a0:o + a1]), [KW, (vU, o + a0, o + a1), cR(8)], ID, bias=col(8), scale=1.0 / 32.0)
+        act(T.kvf[:, q:q + n], [("kvf", q, q + n)], T.kw[:, 0:V].indirect(T[vU][:, o + a0:o + a1]), [KW, (vU, o + a0, o + a1)], ID, scale=1.0 / 32.0)
         op("V", lambda e: e.transpose(T.Tt[:, 4 * gr:4 * gr + nb, :], T.kvf[:, q:q + 32 * nb]), [("kvf", q, q + 32 * nb)], [("Tt", q, q + 32 * nb)], max(64, 32 * nb) * CYC)
         pb = "pb%d" % gr
         for b in range(0, nb, 2):
@@ -408,8 +408,14 @@ def rank_program(g, core, T, topo):
     def xvec(t, gr, s):
         a0, a1 = GROUPS[gr][:2]
         o = 480 * (s - 1)
+        zp, ZP = T.zg[:, o + 16 * a0:o + 16 * a1], ("zg", o + 16 * a0, o + 16 * a1)
         for k in range(16):
-            cp(T.zx[:, k:256 * (a1 - a0):16], [("zxv", k, k + 1)], T.zg[:, o + 16 * a0:o + 16 * a1], [("zg", o + 16 * a0, o + 16 * a1)])
+            W = [("zxv", k, k + 1)]
+            if s == 1:
+                cp(T.zx[:, k:256 * (a1 - a0):16], W, zp, [ZP])
+            else:
+                q = 128 * gr
+                ts(T.zx[:, k:256 * (a1 - a0):16], W, T.sh[:, q:q + 16 * (a1 - a0)], [("sh", q, q + 16 * (a1 - a0))], -1024.0, None, A.add)
         for a in range(a0, a1):
             r = 256 * (a - a0)
             tt(T.Y[:, a, :], [("Y", 256 * a, 256 * a + 256)], T.xw[:, 0:V].indirect(T.kvu[:, 16 * a:16 * a + 16]), T.zx[:, r:r + 256],
@@ -422,7 +428,7 @@ def rank_program(g, core, T, topo):
         for c in range(16):
             mm(T.pc[:, 0:30], [("pc", 0, 512)], T.U[:, 15 - c:143 - c], T.zg[:, o + c:o + 480:16], [("U", 0, 144), ("zg", o, o + 480)], c == 0, c == 15, n=30)
         act(T.zsT[:, q:q + 15], [("zsT", q, q + 15)], T.pc[:, 0:15], [("pc", 0, 512)], ID, scale=1.0 / 16.0)
-        act(T.cntT[:, q:q + 15], [("cntT", q, q + 15)], T.pc[:, 15:30], [("pc", 0, 512)], ID, bias=8.0, scale=1.0 / 32.0)
+        act(T.cntT[:, q:q + 15], [("cntT", q, q + 15)], T.pc[:, 15:30], [("pc", 0, 512)], ID, bias=0.0 if s == S else 8.0, scale=1.0 / (16.0 if s == S else 32.0))
 
     def pick(t, gr, s):
         vI, vU = "vI%d" % (t % 2), "vU%d" % (t % 2)
@@ -437,11 +443,12 @@ def rank_program(g, core, T, topo):
         for b in range(0, nb, 2):
             p = q + 32 * b
             tt(T.pr[:, p:p + 64], [("pr", p, p + 64)], T.eq[:, p:p + 64], T[pb][:, 1:3, 16 * b:16 * b + 32], [("eq", p, p + 64), (pb, 0, 512)], A.mult)
-        scan(T.C[:, q:q + n], [r("C")], T.rm[:, 0:n], T.pr[:, q:q + n], [("rm", 0, n), r("pr")], A.mult, A.max)
-        cI = ("codeI", o - 16 + a0, o - 16 + a1)
-        cp(T.codeI[:, o - 16 + a0:o - 16 + a1], [cI], T.C[:, q + 15:q + 16 * (a1 - a0):16], [r("C")])
-        ts(T[vI][:, o + a0:o + a1], [(vI, o + a0, o + a1)], T.codeI[:, o - 16 + a0:o - 16 + a1], [cI], 4095, None, A.bitwise_and)
-        cp(T[vU][:, o + a0:o + a1], [(vU, o + a0, o + a1)], T[vI][:, o + a0:o + a1], [(vI, o + a0, o + a1)])
+        tt(T.ne[:, q:q + n], [r("ne")], T.R[:, q:q + n], T[pb][:, 0, 0:n], [r("R"), (pb, 0, 512)], A.not_equal)
+        scan(T.C[:, q:q + n], [r("C")], T.ne[:, q:q + n], T.pr[:, q:q + n], [r("ne"), r("pr")], A.mult, A.add)
+        last_k = slice(q + 15, q + 16 * (a1 - a0), 16)
+        cp(T[vU][:, o + a0:o + a1], [(vU, o + a0, o + a1)], T.C[:, last_k], [r("C")])
+        cp(T[vI][:, o + a0:o + a1], [(vI, o + a0, o + a1)], T.C[:, last_k], [r("C")])
+        cp(T.codeI[:, o - 16 + a0:o - 16 + a1], [("codeI", o - 16 + a0, o - 16 + a1)], T.R[:, last_k], [r("R")])
 
     def zstep(t, gr, s):
         vU = "vU%d" % (t % 2)
@@ -453,6 +460,9 @@ def rank_program(g, core, T, topo):
         tt(T.sh[:, q:q + n], [SH], lst, zp, RD + [ZP], A.add)
         ts(T.sh[:, q:q + n], [SH], T.sh[:, q:q + n], [SH], 0.5, 1023.75, A.mult, A.add)
         ts(T.zg[:, o + 480 + lo:o + 480 + hi], [("zg", o + 480 + lo, o + 480 + hi)], T.sh[:, q:q + n], [SH], -1024.0, None, A.add)
+        if s == S:
+            tt(T.zg[:, o + 720 + lo:o + 720 + hi], [("zg", o + 720 + lo, o + 720 + hi)], lst, zp, RD + [ZP], A.is_gt)
+            return
         act(T.xq[:, q:q + n], [XQ], lst, RD)
         mm(T.ps[:, 0:n], [("ps", 0, 512)], T.idb[:], T.xq[:, q:q + n], [("idb", 0, 128), XQ], True, False)
         mm(T.ps[:, 0:n], [("ps", 0, 512)], T.idn[:], zp, [("idn", 0, 128), ZP], False, True)
@@ -461,14 +471,13 @@ def rank_program(g, core, T, topo):
     def race(t):
         for s in range(1, S + 1):
             for gr in range(len(GROUPS)):
-                bias[0] = BIAS[gr]
-                knew(t, gr, s)
-                kpick(t, gr, s)
-                (xact if GROUPS[gr][2] else xvec)(t, gr, s)
-                pick(t, gr, s)
-                zstep(t, gr, s)
-            bias[0] = 0.0
+                steps = (knew, kpick, xact if GROUPS[gr][2] else xvec, pick, zstep)
+                for i in range(5):
+                    bias[0] = BIAS[gr][i]
+                    steps[i](t, gr, s)
+            bias[0] = BIAS[3][0]
             count(s)
+        bias[0] = 0.0
         finish(t, "vI%d" % (t % 2), "vU%d" % (t % 2))
 
     def finish(t, vI, vU):
@@ -485,6 +494,7 @@ def rank_program(g, core, T, topo):
         tt(own, [OW], T.m1[:, 0:16], T.m1[:, 16:32], [("m1", 0, 32)], A.min)
         rs = 48 * t
         send(own, [T.rcv[:, rs + 16 * j:rs + 16 * j + 16] for j in range(3)], [OW], [("rcv", rs, rs + 48)], "a%d" % t, "l%d" % t)
+        bias[0] = BIAS[3][2]
         ts(T.nb[:], [("nb",) + f64], T.cntT[:], [("cntT",) + f64, ("thr", 0, 1)], T.thr[:], BIG, A.is_lt, A.mult)
         tt(T.d1[:], [("d1",) + f64], T[vI][:, 16:80], T.bs[:], [(vI, 16, 80), ("bs",) + f64], A.add)
         tt(T.d1[:], [("d1",) + f64], T.d1[:], T.nb[:], [("d1",) + f64, ("nb",) + f64], A.add)
@@ -492,10 +502,10 @@ def rank_program(g, core, T, topo):
         tt(T.dI[:], [("dI",) + f16], T.c1[:, 0:16], T.c1[:, 16:32], [("c1", 0, 32)], A.min)
         ts(T.WI[:], [("WI",) + f16], T.dI[:], [("dI",) + f16], 4095, None, A.bitwise_and)
         ts(T.bI[:], [("bI",) + f16], T.dI[:], [("dI",) + f16], 12, 7, A.arith_shift_right, A.bitwise_and)
-        ts(T.kI[:], [("kI",) + f64], T.codeI[:], [("codeI",) + f64], 12, None, A.arith_shift_right)
+        ts(T.kI[:], [("kI",) + f64], T.codeI[:], [("codeI",) + f64], 15, None, A.bitwise_and)
         cp(T.WU[:], [("WU",) + f16], T.WI[:], [("WI",) + f16])
         ts(T.bF[:], [("bF",) + f16], T.bI[:], [("bI",) + f16], 4.0, 480.0, A.min, A.mult)
-        cp(T.kU[:], [("kU",) + f64], T.kI[:], [("kI",) + f64])
+        ts(T.kU[:], [("kU",) + f64], T.kI[:], [("kI",) + f64], -1.0, 15.0, A.mult, A.add)
         tt(T.bF[:], [("bF",) + f16], T.bF[:], T.ln[:], [("bF",) + f16, ("ln",) + f16], A.add)
         cp(T.bU[:], [("bU",) + f16], T.bF[:], [("bF",) + f16])
         ts(T.P1[:], [("P1",) + f64], T[vI][:, 0:64], [(vI, 0, 64)], 1.0, None, A.add)
@@ -514,11 +524,11 @@ def rank_program(g, core, T, topo):
             v_start(t + 1)
             z_start(t + 1)
 
+        bias[0] = BIAS[3][1]
         def rc(j, lo, hi):
             o = rs + 16 * (j - 1)
             return T.rcv[:, o + lo:o + hi]
         RC, WM = ("rcv", rs, rs + 48), ("Wm", 0, 16)
-        cp(T.Wm[:], [WM], own, [OW])
         tt(T.Wm[:, 0:10], [("Wm", 0, 10)], T.own[:, oo:oo + 10], rc(3, 5, 15), [OW, RC], A.min)
         tt(T.Wm[:, 10:15], [("Wm", 10, 15)], T.own[:, oo + 10:oo + 15], rc(2, 0, 5), [OW, RC], A.min)
         tt(T.Wm[:, 0:5], [("Wm", 0, 5)], T.Wm[:, 0:5], rc(2, 10, 15), [WM, RC], A.min)
@@ -537,9 +547,12 @@ def rank_program(g, core, T, topo):
         tt(T.kt1[:], [("kt1",) + f16], T.won[:], T.Wp[:], [("won",) + f16, ("Wp",) + f16], A.mult)
         tt(T.kk[:], [("kk",) + f64], T.P1[:], T.on[:], [("P1",) + f64, ("on",) + f64], A.mult)
         tt(T.kk[:, 0:16], [("kk", 0, 16)], T.kk[:, 0:16], T.kt1[:], [("kk", 0, 16), ("kt1",) + f16], A.add)
-        ts(T.key[:], [("key",) + f64], T.kk[:], [("kk",) + f64], -1.0, None, A.add)
+        ts(T.key[:, 16:64], [("key", 16, 64)], T.kk[:, 16:64], [("kk", 16, 64)], -1.0, None, A.add)
+        ts(T.key[:, 0:16], [("key", 0, 16)], T.kk[:, 0:16], [("kk", 0, 16)], -1.0, None, A.add)
         ts(T.nkey[:], [("nkey",) + f64], T.kk[:], [("kk",) + f64], -1.0, 1.0, A.mult, A.add)
         cp(T.keyU[:], [("keyU",) + f16], T.key[:, 0:16], [("key", 0, 16)])
+        tt(T.fo[:, 0:64], [("fo", 0, 64)], T.on[:], T.vD[:, 0:64], [("on",) + f64, ("vD", 0, 64)], A.mult)
+        tt(T.fo[:, 64:80], [("fo", 64, 80)], T.won[:], T.vD[:, 64:80], [("won",) + f16, ("vD", 64, 80)], A.mult)
         cp(T.wonb[:], [("wonb",) + f16], T.won[:], [("won",) + f16])
         if 1 not in ACT_EVENTS:
             cp(T.vall[:, 0:240], [("vall", 0, 240)], T.iw[:].indirect(T.keyU[:, 0:15]), [("iw", 0, 8192), ("keyU",) + f16])
@@ -579,21 +592,22 @@ def rank_program(g, core, T, topo):
             tt(T.fl[:, r:r + 240], [("fl", r, r + 240)], flat(bank[s], 0, 240), T.W2d[:], [(bank[s], 0, 512), ("W2d", 0, 240)], A.is_lt)
             scan(T.Fs[:, r:r + 240], [("Fs", r, r + 240)], T.rmb[:, 0:240], T.fl[:, r:r + 240], [("rmb", 0, 240), ("fl", r, r + 240)], A.mult, A.add)
 
-            def place(k, on, ON):
-                fo, of = T.fo[:, k:k + 15], T.of[:, k:k + 15]
-                tt(fo, [("fo", k, k + 15)], T.Fs[:, r + 15:r + 240:16], on, [("Fs", r, r + 240), ON], A.mult)
-                tt(of, [("of", k, k + 15)], fo, T.vD[:, k:k + 15], [("fo", k, k + 15), ("vD", k, k + 15)], A.mult)
+            def place(k):
+                of = T.of[:, k:k + 15]
+                tt(of, [("of", k, k + 15)], T.Fs[:, r + 15:r + 240:16], T.fo[:, k:k + 15], [("Fs", r, r + 240), ("fo", k, k + 15)], A.mult)
                 tt(of, [("of", k, k + 15)], of, T.Dm[:, 0:15], [("of", k, k + 15), ("Dm", 0, 15)], A.add)
                 cp(T.offU[:, k:k + 15], [("offU", k, k + 15)], of, [("of", k, k + 15)])
-            place(k0, T.on[:, k0:k0 + 15], ("on", k0, k0 + 15))
+            place(k0)
             if s == 1:
-                place(64, T.won[:, 0:15], ("won",) + f16)
+                place(64)
 
         cp(T.urep[:], [("urep", 0, 240)], T.iw[:].indirect(T.uwU[:, 0:15]), [("iw", 0, 8192), ("uwU",) + f16])
         for s in range(S, 0, -1):
             r = 240 * s - 240
             tt(T.xs[:, r:r + 240], [("xs", r, r + 240)], T.Wk[:].indirect(T.kU[:, 16 * s - 16:16 * s - 1]), T.urep[:], [("Wk",) + f16, ("kU",) + f64, ("urep", 0, 240)], A.mult)
+            bias[0] = BIAS[3][3] if s == S else BIAS[3][4]
             event(s)
+        bias[0] = 0.0
         cp(T.xw[:].indirect(T.offU[:, 64:79]), [("xw", 0, WIN)], T.xn[:], [("xn", 0, 240), ("offU", 64, 80)])
         for s in range(S, 0, -1):
             r = 240 * s - 240

from concourse.bass import DstId, RemoteDMATransfer
from concourse.mybir import AluOpType, AxisListType, ActivationFunctionType

A = AluOpType
ID = ActivationFunctionType.Identity
RELU = ActivationFunctionType.Relu
ABS = ActivationFunctionType.Abs
SIGN = ActivationFunctionType.Sign
N, M, J, RACES, S, V = 4, 80, 3, 3, 4, 4096
L = J * M
GROUPS = ((0, 4, True), (4, 8, True), (8, 15, False))
BIAS = ((5400.0, 2700.0, 1700.0, 2200.0, 2200.0), (400.0, 8000.0, 1300.0, 2000.0, 1400.0), (3100.0, 2500.0, 1300.0, 4300.0, -1500.0), (1200.0, 4100.0, 1800.0, 6100.0, -2100.0))
ND = 7
NX = 3
ACT_EVENTS = (1,)
WIN = V + 256
BIG = 2.0 ** 19
CYC, LAT, GAMMA, SIGMA = 0.9, 160.0, 1.8, 3.5

SCRATCH = {}
for _n, _w, _d in (
        ("xw", WIN, "bfloat16"), ("kw", WIN, "float32"), ("kin", V, "int32"), ("iw", 8192, "float32"), ("zx", ND * 256, "bfloat16"),
        ("kvu", 256, "uint16"), ("kvf", 384, "float32"), ("sh", 384, "float16"), ("xq", 384, "bfloat16"), ("R", 384, "float32"),
        ("eq", 384, "float32"), ("ne", 384, "float32"), ("pr", 384, "float32"), ("C", 384, "float32"), ("zT0", 128, "bfloat16"), ("zT1", 128, "bfloat16"),
        ("E", 1024, "bfloat16"), ("xg0", 512, "bfloat16"), ("xg1", 512, "bfloat16"), ("xg2", 512, "bfloat16"), ("zg", 2400, "bfloat16"),
        ("codeI", 64, "int32"), ("vI0", 80, "int32"), ("vI1", 80, "int32"), ("vU0", 80, "uint16"), ("vU1", 80, "uint16"),
        ("kI", 64, "int32"), ("kU", 64, "uint16"), ("zsT", 64, "float32"), ("cntT", 64, "float32"), ("wz", 64, "int32"),
        ("u4", 64, "int32"), ("nb", 64, "float32"), ("c1", 64, "float32"), ("m1", 32, "float32"), ("own", 48, "float32"),
        ("d1", 64, "float32"), ("dI", 16, "int32"), ("WI", 16, "int32"), ("WU", 16, "uint16"), ("bF", 16, "float32"),
        ("bI", 16, "int32"), ("bU", 16, "uint16"), ("rcv", 144, "float32"), ("Wm", 16, "float32"), ("x1", 16, "float32"),
        ("x2", 16, "float32"), ("lost", 16, "float32"), ("won", 16, "float32"), ("wonb", 16, "bfloat16"), ("WmI", 16, "int32"),
        ("bw", 16, "int32"), ("uwI", 16, "int32"), ("uwU", 16, "uint16"), ("lc", 16, "float32"), ("on", 64, "float32"),
        ("P1", 64, "float32"), ("Wp", 16, "float32"), ("kk", 64, "float32"), ("kt1", 16, "float32"), ("key", 64, "float32"),
        ("nkey", 64, "float32"), ("keyU", 16, "uint16"), ("vall", 960, "uint16"), ("valf", 240, "float32"), ("eqm", 7680, "bfloat16"),
        ("fl", 960, "bfloat16"), ("Fs", 960, "bfloat16"), ("fo", 80, "float32"), ("vD", 80, "float32"), ("of", 80, "float32"),
        ("offU", 80, "uint16"), ("urep", 240, "float32"), ("xs", 960, "float32"), ("Bs", 960, "bfloat16"), ("kp", 240, "float32"),
        ("kt", 240, "float32"), ("kz", 240, "int32"), ("kn", 240, "int32"), ("xW", 240, "bfloat16"), ("xs2", 240, "float16"),
        ("xt2", 240, "float16"), ("xn", 240, "bfloat16"), ("tot", 1, "float32"), ("totI", 1, "int32"), ("thr", 1, "float32"),
        ("zs", 240, "bfloat16"), ("vs", 45, "int32"), ("zl", 720, "bfloat16"), ("vl", 135, "int32"), ("pI", 8, "int32"),
        ("pF", 24, "float32"), ("idb", 128, "bfloat16"), ("idn", 128, "bfloat16"), ("idf", 128, "float32"), ("idS", 512, "bfloat16"),
        ("Pm", 512, "float32"), ("U", 144, "bfloat16"), ("bo1", 128, "bfloat16"), ("BO", 128, "bfloat16"), ("BW", 128, "bfloat16"),
        ("Wt", 1920, "bfloat16"), ("W2d", 240, "float32"), ("dg", 16, "float32"), ("Wk", 16, "bfloat16"), ("rm", 256, "float32"),
        ("rmb", 256, "bfloat16"), ("kc", 128, "bfloat16"), ("base", 64, "float32"), ("bs", 64, "float32"), ("Dm", 64, "float32"),
        ("ln", 16, "float32"), ("idx", 1024, "bfloat16"), ("idk", 512, "float32"), ("ox", 512, "float32"), ("ok", 512, "float32"),
        ("ones", 128, "bfloat16")):
    SCRATCH[_n] = ("sbuf", [128, _w], _d)
SCRATCH["Y"] = ("sbuf", [128, 16, 256], "bfloat16")
SCRATCH["Tt"] = ("sbuf", [128, 12, 32], "float32")
for _n in ("ps", "pz", "pc"):
    SCRATCH[_n] = ("psum", [128, 512], "float32")
for _n in ("pb0", "pb1", "pb2"):
    SCRATCH[_n] = ("psum", [128, 4, 128], "float32")
for _n in ("pa0", "pa1"):
    SCRATCH[_n] = ("psum", [128, 2, 256], "float32")
SEMAPHORES = ["qV", "qS", "qT", "qG", "zin", "vin", "k0", "k1", "k2", "k3", "x0", "x1", "az", "av", "a0", "a1", "a2",
              "lz", "lv", "l0", "l1", "l2", "oy", "ok"]


def planner(g, T):
    queues = {"V": g.vector, "S": g.scalar, "T": g.tensor, "G": g, "Y": g.sync}
    ops = []
    plan = {}
    bias = [0.0]

    def is_psum(b):
        return b in SCRATCH and SCRATCH[b][0] == "psum"

    def hazards(recs, q, R, W):
        out = []
        for b, lo, hi in R:
            ps = is_psum(b)
            for r in recs.get(b, []):
                if r[0] < hi and lo < r[1] and r[2] or ps and r[3] != q:
                    out.append(r)
        for b, lo, hi in W:
            ps = is_psum(b)
            for r in recs.get(b, []):
                if ps or (r[0] < hi and lo < r[1]):
                    out.append(r)
        return out

    def note(recs, q, R, W, tag):
        for b, lo, hi in W:
            recs[b] = [r for r in recs.get(b, []) if not (lo <= r[0] and r[1] <= hi)] + [(lo, hi, True, q, tag)]
        for b, lo, hi in R:
            recs[b] = [r for r in recs.get(b, []) if not (not r[2] and r[3] == q and lo <= r[0] and r[1] <= hi and q in "VSTG")] + [(lo, hi, False, q, tag)]

    def rec(q, kind, fn, R, W, dur, lat, sem=None, val=0, after=None):
        i = len(ops)
        rq = q if kind == "c" else kind + str(i)
        deps = {}
        for r in hazards(plan, rq, R, W):
            x = 0 if (q == "T" and ops[r[4]]["q"] == "T") else ops[r[4]]["lat"]
            deps[r[4]] = max(deps.get(r[4], 0), x)
        if after is not None:
            deps[after] = 0
        note(plan, rq, R, W, i)
        ops.append({"q": q, "kind": kind, "fn": fn, "R": R, "W": W, "dur": dur, "lat": lat, "sem": sem, "val": val, "deps": deps, "rq": rq, "bias": bias[0]})
        return i

    def emit():
        n = len(ops)
        succ = [[] for _ in range(n)]
        left = [len(o["deps"]) for o in ops]
        for i, o in enumerate(ops):
            for d, x in o["deps"].items():
                succ[d].append((i, x))
        prio = [0.0] * n
        for i in range(n - 1, -1, -1):
            prio[i] = ops[i]["dur"] + max([x + prio[k] for k, x in succ[i]] + [0.0])
        free = {q: 0.0 for q in queues}
        when = [0.0] * n
        ready = {q: [i for i in range(n) if not left[i] and ops[i]["q"] == q] for q in list(queues) + ["N"]}
        order = []

        def done(i, t):
            for k, x in succ[i]:
                when[k] = max(when[k], t + ops[i]["dur"] + x)
                left[k] -= 1
                if not left[k]:
                    ready[ops[k]["q"]].append(k)
        while len(order) < n:
            while ready["N"]:
                i = ready["N"].pop()
                order.append((when[i], len(order), i))
                done(i, when[i])
            best = None
            for q in queues:
                if ready[q]:
                    t = max(free[q], min(when[i] for i in ready[q]))
                    if best is None or t < best[0]:
                        best = (t, q)
            if best is None:
                continue
            t, q = best
            i = max((i for i in ready[q] if when[i] <= t + 1.0), key=lambda i: (prio[i] + ops[i]["bias"], -i))
            ready[q].remove(i)
            st = max(t, when[i])
            free[q] = st + ops[i]["dur"]
            order.append((st, len(order), i))
            done(i, st)
        order.sort()
        cnt = {q: 0 for q in queues}
        clk = {q: {} for q in queues}
        snap = {}
        live = {}
        for _, _, i in order:
            o = ops[i]
            q = o["q"]
            if o["kind"] == "n":
                snap[(o["sem"], o["val"])] = {}
                note(live, o["rq"], o["R"], o["W"], (o["sem"], o["val"]))
                continue
            need = {}
            for r in hazards(live, o["rq"], o["R"], o["W"]):
                if q == "T" and r[3] == "T":
                    continue
                sm, v = r[4]
                if need.get(sm, 0) < v:
                    need[sm] = v
            c = clk[q]
            items = [(sm, v) for sm, v in need.items() if c.get(sm, 0) < v]
            for it in items:
                if not any(x != it and snap.get(x, {}).get(it[0], 0) >= it[1] for x in items):
                    queues[q].wait_ge(T.sem[it[0]], it[1])
            for it in items:
                for k2, v2 in list(snap.get(it, {}).items()) + [it]:
                    if c.get(k2, 0) < v2:
                        c[k2] = v2
            ins = o["fn"](queues[q])
            if o["kind"] == "c":
                cnt[q] += 1
                ins.then_inc(T.sem["q" + q], 1)
                tag = ("q" + q, cnt[q])
            else:
                if o["kind"] == "d":
                    ins.then_inc(T.sem[o["sem"]], 16)
                tag = (o["sem"], o["val"])
            snap[tag] = dict(c)
            note(live, o["rq"], o["R"], o["W"], tag)
        return cnt
    return rec, emit, bias


def rank_program(g, core, T, topo):
    rank = T.rank_of(core)
    if rank is None:
        return
    rec, emit, bias = planner(g, T)
    peers = [T.cores[(rank + j) % N] for j in (1, 2, 3)]

    def width(b):
        return 2 if b not in SCRATCH or SCRATCH[b][2] in ("bfloat16", "float16", "uint16") else 4

    def cost(W, R, two=False):
        n = W[0][2] - W[0][1]
        if W[0] in (("kw", 0, WIN), ("xw", 0, WIN)):
            return 50 + SIGMA * L * CYC
        if any(r[0] in ("kw", "xw", "Wk") or r[1:] == (0, 8192) for r in R):
            return 50 + GAMMA * n * CYC
        if two:
            return max(64, n * (1 if any(SCRATCH[r[0]][0] == "psum" for r in R) else 2)) * CYC
        return max(64, n * (0.5 if all(width(r[0]) == 2 for r in W[:1] + R[:1]) else 1)) * CYC

    def op(q, fn, R, W, dur):
        rec(q, "c", fn, R, W, dur, LAT)

    def iota(name, lo, hi, pattern, base, cm):
        if SCRATCH[name][2] != "int32":
            fn = lambda e: e.iota(T[name][:, lo:hi], pattern, base, cm, allow_small_or_imprecise_dtypes=True)
        else:
            fn = lambda e: e.iota(T[name][:, lo:hi], pattern, base, cm)
        op("G", fn, [], [(name, lo, hi)], 130 + 2 * (hi - lo) * CYC)

    def ts(out, W, in0, R, s1, s2, o0, o1=None):
        if o1 is None:
            op("V", lambda e: e.tensor_scalar(out, in0, s1, None, o0), R, W, cost(W, R))
        else:
            op("V", lambda e: e.tensor_scalar(out, in0, s1, s2, o0, o1), R, W, cost(W, R))

    def tt(out, W, in0, in1, R, o):
        op("V", lambda e: e.tensor_tensor(out, in0, in1, o), R, W, cost(W, R, True))

    def cp(out, W, in_, R):
        op("V", lambda e: e.tensor_copy(out, in_), R, W, cost(W, R))

    def scan(out, W, d0, d1, R, o0, o1):
        op("V", lambda e: e.tensor_tensor_scan(out, d0, d1, 0.0, o0, o1), R, W, cost(W, R))

    def act(out, W, in_, R, f=ID, bias=0.0, scale=1.0):
        n = W[0][2] - W[0][1]
        op("S", lambda e: e.activation(out, in_, f, bias=bias, scale=scale), R, W, max(cost(W, R), n * CYC))

    def mm(out, W, lhsT, rhs, R, start, stop, n=None):
        n = n or R[-1][2] - R[-1][1]
        op("T", lambda e: e.matmul(out, lhsT, rhs, start, stop), R, W, max(64, n) * 0.5 * (4 if SCRATCH[R[0][0]][2] == "float32" else 1))

    def ms(name, lo, hi, val):
        op("V", lambda e: e.memset(T[name][:, lo:hi], val), [], [(name, lo, hi)], max(64, hi - lo) * CYC)

    last = {}

    def dma(q, sem, out, in_, R, W, lat):
        last[q] = rec(q, "d", lambda e: e.dma_start(out, in_), R, W, 60.0, lat, sem, 16, after=last.get(q))

    def send(src, dsts, R, W, rsem, lsem):
        ids = []
        m = None
        for p in peers:
            a = topo.addr(p)
            ids.append(DstId(rid=a[0], pnc=a[1]))
            m = topo.mask(core, p) if m is None else m & topo.mask(core, p)
        tr = RemoteDMATransfer(dst_ids=ids, dma_engine_mask=m, remote_sem=T.sem[rsem], srcs=[src], dsts=dsts, alu_op=0)
        n = sum(m >> e & 1 for e in range(16))
        i = rec("G", "s", lambda e: e.remote_dma_fused([tr], local_sem=T.sem[lsem]), R, [], 900.0, 1500.0, lsem, n)
        rec("N", "n", None, [], W, 2500.0, LAT, rsem, 3 * n, after=i)
        return n

    dma("S", "zin", T.zs[:], T.z0[:], [], [("zs", 0, 240)], 2000.0)
    dma("S", "vin", T.vs[:], T.v0[:], [], [("vs", 0, 45)], 2000.0)
    for i in range(4):
        dma("YS"[i % 2], "k%d" % i, T.kin[:, 1024 * i:1024 * i + 1024], T.k0[:, 1024 * i:1024 * i + 1024], [], [("kin", 1024 * i, 1024 * i + 1024)], 8000.0 + 3000.0 * i)
    for i in range(2):
        dma("YS"[i], "x%d" % i, T.xw[:, 2048 * i:2048 * i + 2048], T.x0[:, 2048 * i:2048 * i + 2048], [], [("xw", 2048 * i, 2048 * i + 2048)], 20000.0)

    iota("pI", 0, 1, [[0, 1]], 0, 1)
    iota("iw", 0, 256, [[1, 256]], 0, 0)
    ne = send(T.zs[:], [T.zl[:, 240 * j:240 * j + 240] for j in range(3)], [("zs", 0, 240)], [("zl", 0, 720)], "az", "lz")
    send(T.vs[:], [T.vl[:, 45 * j:45 * j + 45] for j in range(3)], [("vs", 0, 45)], [("vl", 0, 135)], "av", "lv")
    iota("kc", 0, 128, [[0, 8], [-1, 16]], 15, 0)
    iota("rm", 0, 256, [[0, 16], [1, 16]], 0, 0)
    iota("E", 0, 1024, [[1, 64], [0, 16]], 0, 0)

    def col(i):
        return T.pF[:, i:i + 1]

    def cR(i):
        return ("pF", i, i + 1)
    ts(T.pI[:, 1:2], [("pI", 1, 2)], T.pI[:, 0:1], [("pI", 0, 1)], 15, None, A.bitwise_and)
    ts(T.pI[:, 2:3], [("pI", 2, 3)], T.pI[:, 0:1], [("pI", 0, 1)], 112, None, A.bitwise_and)
    ts(T.pI[:, 3:4], [("pI", 3, 4)], T.pI[:, 0:1], [("pI", 0, 1)], 4, 1, A.arith_shift_right, A.bitwise_and)
    cp(T.pF[:, 0:4], [("pF", 0, 4)], T.pI[:, 0:4], [("pI", 0, 4)])
    ts(col(4), [cR(4)], col(3), [cR(3)], -1.0, 1.0, A.mult, A.add)
    ts(col(5), [cR(5)], col(0), [cR(0)], 16.0, None, A.add)
    ts(col(6), [cR(6)], col(0), [cR(0)], -16.0, None, A.add)
    ts(col(7), [cR(7)], col(2), [cR(2)], 15.0, None, A.add)
    ts(T.idb[:], [("idb", 0, 128)], T.iw[:, 0:128], [("iw", 0, 128), cR(0)], col(0), None, A.is_equal)
    ts(T.idf[:], [("idf", 0, 128)], T.iw[:, 0:128], [("iw", 0, 128), cR(0)], col(0), None, A.is_equal)
    for s in range(S):
        act(T.idS[:, 128 * s:128 * s + 128], [("idS", 128 * s, 128 * s + 128)], T.idb[:], [("idb", 0, 128)], ID, scale=1024.0 * (s + 1))
    ts(T.idn[:], [("idn", 0, 128)], T.iw[:, 0:128], [("iw", 0, 128), cR(0)], col(0), -1.0, A.is_equal, A.mult)
    for h in range(2):
        for q in range(2):
            sc = {0: 0, 1: 5, -1: 6}[q - h]
            hc = 3 if h else 4
            o = 128 * (2 * h + q)
            ts(T.Pm[:, o:o + 128], [("Pm", o, o + 128)], T.iw[:, 0:128], [("iw", 0, 128), cR(sc), cR(hc)], col(sc), col(hc), A.is_equal, A.mult)
    ts(T.U[:], [("U", 0, 144)], T.iw[:, 0:144], [("iw", 0, 144), cR(7)], col(7), 16.0, A.is_equal, A.mult)
    ts(T.rm[:], [("rm", 0, 256)], T.rm[:], [("rm", 0, 256)], 1.0, None, A.min)
    ts(T.E[:], [("E", 0, 1024)], T.E[:], [("E", 0, 1024), cR(0)], col(0), None, A.is_equal)
    for name, n in (("codeI", 64), ("vI0", 80), ("vI1", 80), ("vU0", 80), ("vU1", 80), ("offU", 80)):
        ms(name, 0, n, 0)
    for name, n in (("zsT", 64), ("cntT", 64), ("kvf", 384), ("own", 48), ("zg", 2400), ("fo", 80)):
        ms(name, 0, n, 0.0)
    op("V", lambda e: e.memset(T.Y[:, 15, :], 0.0), [], [("Y", 3840, 4096)], 300.0)
    ms("thr", 0, 1, 12.0)
    ms("Wm", 0, 16, 2.0 ** 20)
    ms("ones", 0, 128, 1.0)
    iota("bs", 0, 64, [[4096, 4], [0, 16]], 4096, 0)
    iota("Dm", 0, 64, [[0, 4], [16, 16]], 4096, 0)
    ms("base", 0, 64, 2.0 ** 20)
    for s in range(S):
        iota("base", 16 * s, 16 * s + 15, [[4096, 3], [0, 5]], 16384 * (s + 1) + 4096, 0)
    iota("iw", 256, 8192, [[1, 7936]], 256, 0)
    cp(T.rmb[:], [("rmb", 0, 256)], T.rm[:], [("rm", 0, 256)])
    ts(T.bo1[:], [("bo1", 0, 128)], T.iw[:, 0:128], [("iw", 0, 128), cR(2)], col(2), None, A.is_ge)
    ts(T.BW[:], [("BW", 0, 128)], T.iw[:, 0:128], [("iw", 0, 128), cR(7)], col(7), None, A.is_le)
    tt(T.BO[:], [("BO", 0, 128)], T.bo1[:], T.BW[:], [("bo1", 0, 128), ("BW", 0, 128)], A.mult)
    for i in range(4):
        ts(T.pI[:, 4 + i:5 + i], [("pI", 4 + i, 5 + i)], T.pI[:, 1:2], [("pI", 1, 2)], i, 1, A.arith_shift_right, A.bitwise_and)
    for i in range(4):
        ts(col(9 + i), [cR(9 + i)], T.pI[:, 4 + i:5 + i], [("pI", 4 + i, 5 + i)], 2.0 ** -(2 ** i) - 1.0, 1.0, A.mult, A.add)
    tt(col(13), [cR(13)], col(9), col(10), [cR(9), cR(10)], A.mult)
    tt(col(14), [cR(14)], col(11), col(12), [cR(11), cR(12)], A.mult)
    tt(col(15), [cR(15)], col(13), col(14), [cR(13), cR(14)], A.mult)
    ts(T.BW[:], [("BW", 0, 128)], T.BO[:], [("BO", 0, 128), cR(15)], col(15), 2.0 ** 60, A.mult, A.mult)
    ts(T.dg[:], [("dg", 0, 16)], T.iw[:, 0:16], [("iw", 0, 16), cR(1), cR(15)], col(1), col(15), A.is_equal, A.mult)
    for a in range(15):
        e2 = (60 - 16 * a) // 2
        ts(T.Wt[:, 128 * a:128 * a + 128], [("Wt", 128 * a, 128 * a + 128)], T.BW[:], [("BW", 0, 128)], 2.0 ** e2, 2.0 ** e2, A.mult, A.mult)
        e2 = (120 - 16 * a) // 2
        ts(T.W2d[:, 16 * a:16 * a + 16], [("W2d", 16 * a, 16 * a + 16)], T.dg[:], [("dg", 0, 16)], 2.0 ** e2, 2.5 * 2.0 ** e2, A.mult, A.mult)
    ts(T.Wk[:], [("Wk", 0, 16)], T.iw[:, 0:16], [("iw", 0, 16), cR(1)], col(1), 1.0 / 32.0, A.is_equal, A.mult)
    ts(T.Dm[:], [("Dm", 0, 64)], T.Dm[:], [("Dm", 0, 64), cR(1)], col(1), None, A.add)
    ts(T.ln[:], [("ln", 0, 16)], T.Dm[:, 0:16], [("Dm", 0, 16)], -4096.0, None, A.add)

    def z_start(t):
        for j in range(3):
            cp(T.zg[:, 80 * j:80 * j + 80], [("zg", 80 * j, 80 * j + 80)], T.zl[:, 240 * j + 80 * t:240 * j + 80 * t + 80], [("zl", 0, 720)])

    def v_start(t):
        vI, vU = "vI%d" % (t % 2), "vU%d" % (t % 2)
        for j in range(3):
            o = 45 * j + 15 * t + 5 * j
            cp(T[vI][:, 5 * j:5 * j + 5], [(vI, 5 * j, 5 * j + 5)], T.vl[:, o:o + 5], [("vl", 0, 135)])
        cp(T[vU][:, 0:15], [(vU, 0, 15)], T[vI][:, 0:15], [(vI, 0, 15)])

    v_start(0)
    z_start(0)
    for i in range(4):
        lo, hi = 1024 * i, 1024 * i + 1024
        ts(T.kw[:, lo:hi], [("kw", lo, hi)], T.kin[:, lo:hi], [("kin", lo, hi)], 32.0, None, A.mult)

    KW = ("kw", 0, V)
    XW = ("xw", 0, V)

    def knew(t, gr, s):
        vU = "vU%d" % (t % 2)
        a0, a1 = GROUPS[gr][:2]
        lo, hi, o = 16 * a0, 16 * a1, 16 * (s - 1)
        ts(T.kvu[:, lo:hi], [("kvu", lo, hi)], T.kw[:, 0:V].indirect(T[vU][:, o + a0:o + a1]), [KW, (vU, o + a0, o + a1)], 1.0 / 32.0, None, A.mult)

    def kpick(t, gr, s):
        vU = "vU%d" % (t % 2)
        a0, a1 = GROUPS[gr][:2]
        n, o, q = 16 * (a1 - a0), 16 * (s - 1), 128 * gr
        nb = (n + 31) // 32
        act(T.kvf[:, q:q + n], [("kvf", q, q + n)], T.kw[:, 0:V].indirect(T[vU][:, o + a0:o + a1]), [KW, (vU, o + a0, o + a1)], ID, scale=1.0 / 32.0)
        op("V", lambda e: e.transpose(T.Tt[:, 4 * gr:4 * gr + nb, :], T.kvf[:, q:q + 32 * nb]), [("kvf", q, q + 32 * nb)], [("Tt", q, q + 32 * nb)], max(64, 32 * nb) * CYC)
        pb = "pb%d" % gr
        for b in range(0, nb, 2):
            for h in range(2):
                for w in range(2):
                    p = 128 * (2 * h + w)
                    mm(T[pb][:, 1:3, 16 * b + 16 * h:16 * b + 16 * h + 16], [(pb, 0, 512)], T.Pm[:, p:p + 128], T.Tt[:, 4 * gr + b:4 * gr + b + 2, 16 * w:16 * w + 16],
                       [("Pm", p, p + 128), ("Tt", q, q + 32 * nb)], w == 0, w == 1, n=32)

    def score(gr, al, ah):
        pb = "pb%d" % gr
        a0, a1 = GROUPS[gr][:2]
        nb = (a1 - a0 + 1) // 2
        if al == a0:
            mm(T[pb][:, 0, 0:32 * nb], [(pb, 0, 512)], T.idb[:], T.kc[:, 0:32 * nb], [("idb", 0, 128), ("kc", 0, 32 * nb)], True, False)
        end = ah + (ah - al) % 2
        l, h = 16 * (al - a0), 16 * (end - a0)
        for c in range(16):
            mm(T[pb][:, 0, l:h], [(pb, 0, 512)], T.U[:, 15 - c:143 - c], T.Y[:, al:end, 16 * c:16 * c + 16],
               [("U", 0, 144), ("Y", 256 * al, 256 * end)], False, ah == a1 and c == 15, n=16 * (end - al))

    chunk = [0]

    def xact(t, gr, s):
        a0, a1 = GROUPS[gr][:2]
        n, o = 16 * (a1 - a0), 480 * (s - 1) + 16 * a0
        zT = "zT%d" % gr
        mm(T.pz[0:n, 0:128], [("pz", 0, 512)], T.zg[:, o:o + n], T.idb[:], [("zg", o, o + n), ("idb", 0, 128)], True, True)
        act(T[zT][0:n, :], [(zT, 0, 128)], T.pz[0:n, 0:128], [("pz", 0, 512)], ID, scale=-1.0)
        for i in range((a1 - a0) // 2):
            a = a0 + 2 * i
            xg, pa = "xg%d" % (chunk[0] % NX), "pa%d" % (chunk[0] % 2)
            chunk[0] += 1
            act(T[xg][:], [(xg, 0, 512)], T.xw[:, 0:V].indirect(T.kvu[:, 16 * a:16 * a + 32]), [XW, ("kvu", 16 * a, 16 * a + 32)])
            mm(T[pa][:, :, :], [(pa, 0, 512)], T.idb[:], T[xg][:], [("idb", 0, 128), (xg, 0, 512)], True, False)
            mm(T[pa][:, :, :], [(pa, 0, 512)], T[zT][0:n, :], T.E[0:n, 512 * i:512 * i + 512], [(zT, 0, 128), ("E", 0, 1024)], False, True, n=512)
            act(T.Y[:, a:a + 2, :], [("Y", 256 * a, 256 * a + 512)], T[pa][:, :, :], [(pa, 0, 512)], RELU)
        score(gr, a0, a1)

    def xvec(t, gr, s):
        a0, a1 = GROUPS[gr][:2]
        o = 480 * (s - 1)
        zp, ZP = T.zg[:, o + 16 * a0:o + 16 * a1], ("zg", o + 16 * a0, o + 16 * a1)
        for k in range(16):
            W = [("zxv", k, k + 1)]
            if s == 1:
                cp(T.zx[:, k:256 * (a1 - a0):16], W, zp, [ZP])
            else:
                q = 128 * gr
                ts(T.zx[:, k:256 * (a1 - a0):16], W, T.sh[:, q:q + 16 * (a1 - a0)], [("sh", q, q + 16 * (a1 - a0))], -1024.0, None, A.add)
        for a in range(a0, a1):
            r = 256 * (a - a0)
            tt(T.Y[:, a, :], [("Y", 256 * a, 256 * a + 256)], T.xw[:, 0:V].indirect(T.kvu[:, 16 * a:16 * a + 16]), T.zx[:, r:r + 256],
               [XW, ("kvu", 16 * a, 16 * a + 16), ("zxv", 0, 16)], A.max)
        score(gr, a0, a0 + 4)
        score(gr, a0 + 4, a1)

    def count(s):
        o, q = 480 * s, 16 * (s - 1)
        for c in range(16):
            mm(T.pc[:, 0:30], [("pc", 0, 512)], T.U[:, 15 - c:143 - c], T.zg[:, o + c:o + 480:16], [("U", 0, 144), ("zg", o, o + 480)], c == 0, c == 15, n=30)
        act(T.zsT[:, q:q + 15], [("zsT", q, q + 15)], T.pc[:, 0:15], [("pc", 0, 512)], ID, scale=1.0 / 16.0)
        act(T.cntT[:, q:q + 15], [("cntT", q, q + 15)], T.pc[:, 15:30], [("pc", 0, 512)], ID, bias=0.0 if s == S else 8.0, scale=1.0 / (16.0 if s == S else 32.0))

    def pick(t, gr, s):
        vI, vU = "vI%d" % (t % 2), "vU%d" % (t % 2)
        a0, a1 = GROUPS[gr][:2]
        nb = (a1 - a0 + 1) // 2
        o, q, n, pb = 16 * s, 128 * gr, 32 * nb, "pb%d" % gr

        def r(x):
            return (x, q, q + n)
        scan(T.R[:, q:q + n], [r("R")], T.rm[:, 0:n], T[pb][:, 0, 0:n], [("rm", 0, n), (pb, 0, 512)], A.mult, A.max)
        tt(T.eq[:, q:q + n], [r("eq")], T.R[:, q:q + n], T[pb][:, 0, 0:n], [r("R"), (pb, 0, 512)], A.is_equal)
        for b in range(0, nb, 2):
            p = q + 32 * b
            tt(T.pr[:, p:p + 64], [("pr", p, p + 64)], T.eq[:, p:p + 64], T[pb][:, 1:3, 16 * b:16 * b + 32], [("eq", p, p + 64), (pb, 0, 512)], A.mult)
        tt(T.ne[:, q:q + n], [r("ne")], T.R[:, q:q + n], T[pb][:, 0, 0:n], [r("R"), (pb, 0, 512)], A.not_equal)
        scan(T.C[:, q:q + n], [r("C")], T.ne[:, q:q + n], T.pr[:, q:q + n], [r("ne"), r("pr")], A.mult, A.add)
        last_k = slice(q + 15, q + 16 * (a1 - a0), 16)
        cp(T[vU][:, o + a0:o + a1], [(vU, o + a0, o + a1)], T.C[:, last_k], [r("C")])
        cp(T[vI][:, o + a0:o + a1], [(vI, o + a0, o + a1)], T.C[:, last_k], [r("C")])
        cp(T.codeI[:, o - 16 + a0:o - 16 + a1], [("codeI", o - 16 + a0, o - 16 + a1)], T.R[:, last_k], [r("R")])

    def zstep(t, gr, s):
        vU = "vU%d" % (t % 2)
        a0, a1 = GROUPS[gr][:2]
        lo, hi, n, o, q = 16 * a0, 16 * a1, 16 * (a1 - a0), 480 * (s - 1), 128 * gr
        lst = T.xw[:, 0:V].indirect(T[vU][:, 16 * s + a0:16 * s + a1])
        RD = [XW, (vU, 16 * s + a0, 16 * s + a1)]
        zp, ZP, SH, XQ = T.zg[:, o + lo:o + hi], ("zg", o + lo, o + hi), ("sh", q, q + n), ("xq", q, q + n)
        tt(T.sh[:, q:q + n], [SH], lst, zp, RD + [ZP], A.add)
        ts(T.sh[:, q:q + n], [SH], T.sh[:, q:q + n], [SH], 0.5, 1023.75, A.mult, A.add)
        ts(T.zg[:, o + 480 + lo:o + 480 + hi], [("zg", o + 480 + lo, o + 480 + hi)], T.sh[:, q:q + n], [SH], -1024.0, None, A.add)
        if s == S:
            tt(T.zg[:, o + 720 + lo:o + 720 + hi], [("zg", o + 720 + lo, o + 720 + hi)], lst, zp, RD + [ZP], A.is_gt)
            return
        act(T.xq[:, q:q + n], [XQ], lst, RD)
        mm(T.ps[:, 0:n], [("ps", 0, 512)], T.idb[:], T.xq[:, q:q + n], [("idb", 0, 128), XQ], True, False)
        mm(T.ps[:, 0:n], [("ps", 0, 512)], T.idn[:], zp, [("idn", 0, 128), ZP], False, True)
        op("S", lambda e: e.activation(T.zg[:, o + 720 + lo:o + 720 + hi], T.ps[:, 0:n], SIGN, bias=-0.5), [("ps", 0, 512)], [("zg", o + 720 + lo, o + 720 + hi)], n * CYC)

    def race(t):
        for s in range(1, S + 1):
            for gr in range(len(GROUPS)):
                steps = (knew, kpick, xact if GROUPS[gr][2] else xvec, pick, zstep)
                for i in range(5):
                    bias[0] = BIAS[gr][i]
                    steps[i](t, gr, s)
            bias[0] = BIAS[3][0]
            count(s)
        bias[0] = 0.0
        finish(t, "vI%d" % (t % 2), "vU%d" % (t % 2))

    def finish(t, vI, vU):
        f64, f16 = (0, 64), (0, 16)
        tt(T.wz[:], [("wz",) + f64], T[vI][:, 16:80], T.zsT[:], [(vI, 16, 80), ("zsT",) + f64], A.mult)
        ts(T.nb[:], [("nb",) + f64], T.cntT[:], [("cntT",) + f64, ("thr", 0, 1)], T.thr[:], BIG, A.is_lt, A.mult)
        ts(T.u4[:], [("u4",) + f64], T.wz[:], [("wz",) + f64], 4095, None, A.bitwise_and)
        tt(T.nb[:], [("nb",) + f64], T.nb[:], T.base[:], [("nb",) + f64, ("base",) + f64], A.add)
        tt(T.c1[:], [("c1",) + f64], T.u4[:], T.nb[:], [("u4",) + f64, ("nb",) + f64], A.add)
        tt(T.m1[:], [("m1", 0, 32)], T.c1[:, 0:32], T.c1[:, 32:64], [("c1",) + f64], A.min)
        oo = 16 * t
        OW = ("own", oo, oo + 16)
        own = T.own[:, oo:oo + 16]
        tt(own, [OW], T.m1[:, 0:16], T.m1[:, 16:32], [("m1", 0, 32)], A.min)
        rs = 48 * t
        send(own, [T.rcv[:, rs + 16 * j:rs + 16 * j + 16] for j in range(3)], [OW], [("rcv", rs, rs + 48)], "a%d" % t, "l%d" % t)
        bias[0] = BIAS[3][2]
        ts(T.nb[:], [("nb",) + f64], T.cntT[:], [("cntT",) + f64, ("thr", 0, 1)], T.thr[:], BIG, A.is_lt, A.mult)
        tt(T.d1[:], [("d1",) + f64], T[vI][:, 16:80], T.bs[:], [(vI, 16, 80), ("bs",) + f64], A.add)
        tt(T.d1[:], [("d1",) + f64], T.d1[:], T.nb[:], [("d1",) + f64, ("nb",) + f64], A.add)
        tt(T.c1[:, 0:32], [("c1", 0, 32)], T.d1[:, 0:32], T.d1[:, 32:64], [("d1",) + f64], A.min)
        tt(T.dI[:], [("dI",) + f16], T.c1[:, 0:16], T.c1[:, 16:32], [("c1", 0, 32)], A.min)
        ts(T.WI[:], [("WI",) + f16], T.dI[:], [("dI",) + f16], 4095, None, A.bitwise_and)
        ts(T.bI[:], [("bI",) + f16], T.dI[:], [("dI",) + f16], 12, 7, A.arith_shift_right, A.bitwise_and)
        ts(T.kI[:], [("kI",) + f64], T.codeI[:], [("codeI",) + f64], 15, None, A.bitwise_and)
        cp(T.WU[:], [("WU",) + f16], T.WI[:], [("WI",) + f16])
        ts(T.bF[:], [("bF",) + f16], T.bI[:], [("bI",) + f16], 4.0, 480.0, A.min, A.mult)
        ts(T.kU[:], [("kU",) + f64], T.kI[:], [("kI",) + f64], -1.0, 15.0, A.mult, A.add)
        tt(T.bF[:], [("bF",) + f16], T.bF[:], T.ln[:], [("bF",) + f16, ("ln",) + f16], A.add)
        cp(T.bU[:], [("bU",) + f16], T.bF[:], [("bF",) + f16])
        ts(T.P1[:], [("P1",) + f64], T[vI][:, 0:64], [(vI, 0, 64)], 1.0, None, A.add)
        ts(T.Wp[:], [("Wp",) + f16], T.WI[:], [("WI",) + f16], 4097.0, None, A.add)
        tt(T.vD[:, 0:64], [("vD", 0, 64)], T[vI][:, 0:64], T.Dm[:], [(vI, 0, 64), ("Dm",) + f64], A.subtract)
        tt(T.vD[:, 64:80], [("vD", 64, 80)], T.WI[:], T.Dm[:, 0:16], [("WI",) + f16, ("Dm", 0, 16)], A.subtract)
        act(T.xW[:], [("xW", 0, 240)], T.xw[:, 0:V].indirect(T.WU[:, 0:15]), [XW, ("WU",) + f16])
        for s in range(S, 0, -1):
            act(T.Bs[:, 240 * s - 240:240 * s], [("Bs", 240 * s - 240, 240 * s)], T.Wk[:].indirect(T.kU[:, 16 * s - 16:16 * s - 1]), [("Wk",) + f16, ("kU",) + f64])
        for s in [x for x in range(S, 1, -1) if x not in ACT_EVENTS]:
            cp(T.vall[:, 240 * s - 240:240 * s], [("vall", 240 * s - 240, 240 * s)], T.iw[:].indirect(T[vU][:, 16 * s - 16:16 * s - 1]), [("iw", 0, 8192), (vU, 16 * s - 16, 16 * s)])
        tt(T.xs2[:], [("xs2", 0, 240)], T.zg[:].indirect(T.bU[:, 0:15]), T.xW[:], [("zg", 0, 2400), ("bU",) + f16, ("xW", 0, 240)], A.add)
        ts(T.xt2[:], [("xt2", 0, 240)], T.xs2[:], [("xs2", 0, 240)], 0.5, 1023.75, A.mult, A.add)
        ts(T.xn[:], [("xn", 0, 240)], T.xt2[:], [("xt2", 0, 240)], -1024.0, None, A.add)
        if t + 1 < RACES:
            v_start(t + 1)
            z_start(t + 1)

        bias[0] = BIAS[3][1]
        def rc(j, lo, hi):
            o = rs + 16 * (j - 1)
            return T.rcv[:, o + lo:o + hi]
        RC, WM = ("rcv", rs, rs + 48), ("Wm", 0, 16)
        tt(T.Wm[:, 0:10], [("Wm", 0, 10)], T.own[:, oo:oo + 10], rc(3, 5, 15), [OW, RC], A.min)
        tt(T.Wm[:, 10:15], [("Wm", 10, 15)], T.own[:, oo + 10:oo + 15], rc(2, 0, 5), [OW, RC], A.min)
        tt(T.Wm[:, 0:5], [("Wm", 0, 5)], T.Wm[:, 0:5], rc(2, 10, 15), [WM, RC], A.min)
        tt(T.Wm[:, 5:15], [("Wm", 5, 15)], T.Wm[:, 5:15], rc(1, 0, 10), [WM, RC], A.min)
        ts(T.x1[:], [("x1",) + f16], T.Wm[:], [WM], BIG, None, A.is_lt)
        tt(T.x2[:], [("x2",) + f16], T.Wm[:], own, [WM, OW], A.not_equal)
        cp(T.WmI[:], [("WmI",) + f16], T.Wm[:], [WM])
        tt(T.lost[:], [("lost",) + f16], T.x1[:], T.x2[:], [("x1",) + f16, ("x2",) + f16], A.mult)
        ts(T.bw[:], [("bw",) + f16], T.WmI[:], [("WmI",) + f16], 14, 7, A.arith_shift_right, A.bitwise_and)
        ts(T.uwI[:], [("uwI",) + f16], T.WmI[:], [("WmI",) + f16], 4095, None, A.bitwise_and)
        tt(T.lc[:], [("lc",) + f16], T.bw[:], T.lost[:], [("bw",) + f16, ("lost",) + f16], A.mult)
        tt(T.won[:], [("won",) + f16], T.x1[:], T.lost[:], [("x1",) + f16, ("lost",) + f16], A.subtract)
        cp(T.uwU[:], [("uwU",) + f16], T.uwI[:], [("uwI",) + f16])
        for s in range(1, S + 1):
            ts(T.on[:, 16 * s - 16:16 * s], [("on", 16 * s - 16, 16 * s)], T.lc[:], [("lc",) + f16], float(s), None, A.is_ge)
        tt(T.kt1[:], [("kt1",) + f16], T.won[:], T.Wp[:], [("won",) + f16, ("Wp",) + f16], A.mult)
        tt(T.kk[:], [("kk",) + f64], T.P1[:], T.on[:], [("P1",) + f64, ("on",) + f64], A.mult)
        tt(T.kk[:, 0:16], [("kk", 0, 16)], T.kk[:, 0:16], T.kt1[:], [("kk", 0, 16), ("kt1",) + f16], A.add)
        ts(T.key[:, 16:64], [("key", 16, 64)], T.kk[:, 16:64], [("kk", 16, 64)], -1.0, None, A.add)
        ts(T.key[:, 0:16], [("key", 0, 16)], T.kk[:, 0:16], [("kk", 0, 16)], -1.0, None, A.add)
        ts(T.nkey[:], [("nkey",) + f64], T.kk[:], [("kk",) + f64], -1.0, 1.0, A.mult, A.add)
        cp(T.keyU[:], [("keyU",) + f16], T.key[:, 0:16], [("key", 0, 16)])
        tt(T.fo[:, 0:64], [("fo", 0, 64)], T.on[:], T.vD[:, 0:64], [("on",) + f64, ("vD", 0, 64)], A.mult)
        tt(T.fo[:, 64:80], [("fo", 64, 80)], T.won[:], T.vD[:, 64:80], [("won",) + f16, ("vD", 64, 80)], A.mult)
        cp(T.wonb[:], [("wonb",) + f16], T.won[:], [("won",) + f16])
        if 1 not in ACT_EVENTS:
            cp(T.vall[:, 0:240], [("vall", 0, 240)], T.iw[:].indirect(T.keyU[:, 0:15]), [("iw", 0, 8192), ("keyU",) + f16])
        mm(T.pc[:, 480:495], [("pc", 0, 512)], T.ones[:], T.wonb[:, 0:15], [("ones", 0, 128), ("wonb",) + f16], True, True)
        if t + 1 < RACES:
            op("V", lambda e: e.tensor_reduce(T.tot[:], T.pc[:, 480:495], AxisListType.X, A.add), [("pc", 0, 512)], [("tot", 0, 1)], 64 * CYC)
            cp(T.totI[:], [("totI", 0, 1)], T.tot[:], [("tot", 0, 1)])
            ts(T.totI[:], [("totI", 0, 1)], T.totI[:], [("totI", 0, 1)], 1, None, A.bitwise_and)
            ts(T.thr[:], [("thr", 0, 1)], T.totI[:], [("totI", 0, 1)], 12.0, None, A.add)
        bank = {4: "ps", 3: "pa1", 2: "pa0", 1: "pz"}

        def flat(b, lo, hi):
            return T[b][:, 0, lo:hi] if b[:2] == "pa" else T[b][:, lo:hi]

        def event(s):
            o, r, k0 = 1920 * (s - 1), 240 * s - 240, 16 * s - 16
            on_act = s in ACT_EVENTS
            if on_act:
                lst, src = (T.keyU[:, 0:15], ("keyU",) + f16) if s == 1 else (T[vU][:, k0:k0 + 15], (vU, k0, k0 + 16))
                act(T.valf[:], [("valf", 0, 240)], T.iw[:].indirect(lst), [("iw", 0, 8192), src])
            for a in range(15):
                n = 240 - 16 * a
                if on_act:
                    act(T.eqm[:, o:o + n], [("eqm", o, o + n)], T.valf[:, 240 - n:240], [("valf", 0, 240), ("nkey", k0, k0 + 16)], ABS, bias=T.nkey[:, k0 + a:k0 + a + 1])
                    if a in (7, 14):
                        e0 = 1920 * (s - 1) + (0 if a == 7 else 1472)
                        act(T.eqm[:, e0:o + n], [("eqm", e0, o + n)], T.eqm[:, e0:o + n], [("eqm", e0, o + n)], RELU, bias=1.0, scale=-1.0)
                else:
                    ts(T.eqm[:, o:o + n], [("eqm", o, o + n)], T.vall[:, r + 240 - n:r + 240], [("vall", r + 240 - n, r + 240), ("key", k0, k0 + 16)],
                       T.key[:, k0 + a:k0 + a + 1], None, A.is_equal)
                o += n
            o = 1920 * (s - 1)
            for a in range(15):
                n = 240 - 16 * a
                mm(flat(bank[s], 16 * a, 240), [(bank[s], 0, 512)], T.Wt[:, 128 * a:128 * a + 128], T.eqm[:, o:o + n], [("Wt", 0, 1920), ("eqm", o, o + n)], a == 0, a == 14)
                o += n
            tt(T.fl[:, r:r + 240], [("fl", r, r + 240)], flat(bank[s], 0, 240), T.W2d[:], [(bank[s], 0, 512), ("W2d", 0, 240)], A.is_lt)
            scan(T.Fs[:, r:r + 240], [("Fs", r, r + 240)], T.rmb[:, 0:240], T.fl[:, r:r + 240], [("rmb", 0, 240), ("fl", r, r + 240)], A.mult, A.add)

            def place(k):
                of = T.of[:, k:k + 15]
                tt(of, [("of", k, k + 15)], T.Fs[:, r + 15:r + 240:16], T.fo[:, k:k + 15], [("Fs", r, r + 240), ("fo", k, k + 15)], A.mult)
                tt(of, [("of", k, k + 15)], of, T.Dm[:, 0:15], [("of", k, k + 15), ("Dm", 0, 15)], A.add)
                cp(T.offU[:, k:k + 15], [("offU", k, k + 15)], of, [("of", k, k + 15)])
            place(k0)
            if s == 1:
                place(64)

        cp(T.urep[:], [("urep", 0, 240)], T.iw[:].indirect(T.uwU[:, 0:15]), [("iw", 0, 8192), ("uwU",) + f16])
        for s in range(S, 0, -1):
            r = 240 * s - 240
            tt(T.xs[:, r:r + 240], [("xs", r, r + 240)], T.Wk[:].indirect(T.kU[:, 16 * s - 16:16 * s - 1]), T.urep[:], [("Wk",) + f16, ("kU",) + f64, ("urep", 0, 240)], A.mult)
            bias[0] = BIAS[3][3] if s == S else BIAS[3][4]
            event(s)
        bias[0] = 0.0
        cp(T.xw[:].indirect(T.offU[:, 64:79]), [("xw", 0, WIN)], T.xn[:], [("xn", 0, 240), ("offU", 64, 80)])
        for s in range(S, 0, -1):
            r = 240 * s - 240
            lst = T.kw[:, 0:V].indirect(T[vU][:, 16 * s - 16:16 * s - 1])
            RD = [KW, (vU, 16 * s - 16, 16 * s)]
            mm(T.pc[:, 0:240], [("pc", 0, 512)], T.idS[:, 128 * s - 128:128 * s], T.Bs[:, r:r + 240], [("idS", 0, 512), ("Bs", r, r + 240)], True, False)
            act(T.kt[:], [("kt", 0, 240)], lst, RD, ID, bias=-131072.0)
            mm(T.pc[:, 0:240], [("pc", 0, 512)], T.idf[:], T.kt[:], [("idf", 0, 128), ("kt", 0, 240)], False, True)
            tt(T.kp[:], [("kp", 0, 240)], lst, T.xs[:, r:r + 240], RD + [("xs", r, r + 240)], A.mult)
            tt(T.kz[:], [("kz", 0, 240)], T.kp[:], T.pc[:, 0:240], [("kp", 0, 240), ("pc", 0, 512)], A.add)
            ts(T.kn[:], [("kn", 0, 240)], T.kz[:], [("kz", 0, 240)], 131040, None, A.bitwise_and)
            cp(T.kw[:].indirect(T.offU[:, 16 * s - 16:16 * s - 1]), [("kw", 0, WIN)], T.kn[:], [("kn", 0, 240), ("offU", 16 * s - 16, 16 * s - 1)])

    for t in range(RACES):
        race(t)
    for a in range(8):
        act(T.idx[:, 128 * a:128 * a + 128], [("idx", 128 * a, 128 * a + 128)], T.idb[:], [("idb", 0, 128)], ID, scale=float(a + 1))
    for a in range(4):
        act(T.idk[:, 128 * a:128 * a + 128], [("idk", 128 * a, 128 * a + 128)], T.idb[:], [("idb", 0, 128)], ID, scale=(a + 1) / 32.0)
    for a in range(8):
        mm(T.ps[:], [("ps", 0, 512)], T.idx[:, 128 * a:128 * a + 128], T.xw[:, 512 * a:512 * a + 512], [("idx", 0, 1024), ("xw", 512 * a, 512 * a + 512)], a == 0, a == 7)
    act(T.ox[:], [("ox", 0, 512)], T.ps[:], [("ps", 0, 512)])
    dma("Y", "oy", T.yx[:], T.ox[:], [("ox", 0, 512)], [], 2000.0)
    for a in range(4):
        mm(T.pz[:], [("pz", 0, 512)], T.idk[:, 128 * a:128 * a + 128], T.kw[:, 512 * a:512 * a + 512], [("idk", 0, 512), ("kw", 512 * a, 512 * a + 512)], a == 0, a == 3)
    for a in range(4, 8):
        b = "pb%d" % (a - 4) if a < 7 else "pc"
        act(T[b][:, :, :] if a < 7 else T[b][:], [(b, 0, 512)], T.kw[:, 512 * a:512 * a + 512], [("kw", 512 * a, 512 * a + 512)], ID, scale=(a + 1) / 32.0)
    OK = ("ok", 0, 512)
    cp(T.ok[:], [OK], T.pb0[:, :, :], [("pb0", 0, 512)])
    for b in ("pb1", "pb2", "pc", "pz"):
        tt(T.ok[:], [OK], T.ok[:], T[b][:, :, :] if b[1] == "b" else T[b][:], [OK, (b, 0, 512)], A.add)
    dma("Y", "ok", T.yk[:], T.ok[:], [OK], [], 2000.0)
    cnt = emit()
    g.sync.wait_ge(T.sem.oy, 16)
    g.sync.wait_ge(T.sem.ok, 16)
    for q in "VSTG":
        g.wait_ge(T.sem["q" + q], cnt[q])
    for l in ("lz", "lv", "l0", "l1", "l2"):
        g.wait_ge(T.sem[l], ne)
